import numpy as np, ml_dtypes
CORES = [1,5,17,21,33,37,49,53]
N = 8
import mx_ref
BF = ml_dtypes.bfloat16
def cols(t, e):
    v = np.concatenate([t.reshape(128, -1, 4), np.zeros((128, 1, 4), BF)], axis=1)
    return np.ascontiguousarray(v[:, e]).reshape(128, -1)
def cut(t, i, w=512):
    return t[:, w * i:w * i + w]
def f(rng, *shape):
    return mx_ref.flush((rng.standard_normal(shape, dtype=np.float32) * np.exp2(rng.integers(-2, 3, shape[:-1] + (1,)))).astype(BF))
def wide(rng, *shape, cols=0):
    v = rng.standard_normal(shape, dtype=np.float32) * np.exp2(rng.integers(-12, 13, shape)).astype(np.float32)
    if cols: v *= np.repeat(np.exp2(rng.integers(-cols, cols + 1, shape[:-2] + (1, shape[-1] // 4))) * (rng.random(shape[:-2] + (1, shape[-1] // 4)) > 0.0625), 4, axis=-1).astype(np.float32)
    return mx_ref.flush(v.astype(BF))
P, K, R, O = 256, 48, 6, 2
PART = [1, 2, 4, 1, 2, 4]
def scores(c, qt):
    k = mx_ref.quantize(np.concatenate([qt[r][:, :4 * R] for r in range(N)], axis=1))
    s = [mx_ref.matmul(mx_ref.quantize(cut(c[q], i)), k) for q in range(N) for i in range(P // 128)]
    return np.concatenate(s).reshape(N * P, N, R)
def play(s):
    held, use, out = np.arange(N * P).reshape(N, P), np.zeros((N, P), np.float32), []
    for t in range(R):
        left = []
        for r in range(N):
            v = s[held[r], r, t]
            use[r] = use[r] + v * v
            left.append(np.argsort(use[r], kind="stable")[:K])
        new = held.copy()
        for r in range(N):
            p = r ^ PART[t]
            new[r, left[r]] = held[p, left[p]]
            use[r, left[r]] = 0
        held = new
        out.append(held)
    return np.stack(out)
def fit(s):
    a = np.abs(s)
    return bool(np.isfinite(a).all() and ((a == 0) | (a >= 2.0 ** -60) & (a <= 2.0 ** 60)).all())
def times(t, v):
    return mx_ref.flush((t.astype(np.float32) * np.asarray(v, np.float32)).astype(BF))
def plain(rng):
    q = np.array(f(rng, N, 128, 512))
    q[:, :, 4 * R:] = 0
    return {"c": f(rng, N, 128, 4 * P), "qt": q, "w": f(rng, N, 128, 512 * O)}
def first(make, good=None):
    for i in range(50):
        d = make()
        s = scores(d["c"], d["qt"])
        if fit(s) and (good is None or good(s)): return d
    raise RuntimeError("no draw of 50 is fit")
def athome(s):
    h, a = play(s), np.ones((N, R + 1, P), bool)
    for r in range(N):
        for t in range(R): a[r, t + 1] = np.isin(np.arange(P * r, P * r + P), h[t, r])
    return a
def setup_inputs(rng):
    return first(lambda: plain(rng))
def setup_inputs_sides(rng):
    top = np.arange(128) < 64
    def make():
        d = plain(rng)
        half = np.stack([rng.permutation(P) < P // 2 for r in range(N)])
        d["c"] = times(d["c"], np.repeat(half[:, None, :] == top[None, :, None], 4, axis=2))
        for t in range(R):
            g = np.where(top == (PART[t] == 1), 1.0, 2.0 ** -6) * 4.0 ** t
            d["qt"][:, :, 4 * t:4 * t + 4] = times(d["qt"][:, :, 4 * t:4 * t + 4], g[None, :, None])
        return d
    def good(s):
        a = athome(s)
        return bool((~a[:, :-1] & a[:, 1:]).any(axis=(1, 2)).all())
    return first(make, good)
def setup_inputs_ties(rng):
    def make():
        d = plain(rng)
        d["c"] = np.stack([times(cols(d["c"][r], rng.integers(0, 6, P)), np.repeat(1 - 2 * rng.integers(0, 2, P), 4)) for r in range(N)])
        return d
    def good(s):
        for r in range(N):
            v = s[P * r:P * r + P, r, 0]
            u = np.sort(v * v)
            if u[K - 1] != u[K]: return False
        return True
    return first(make, good)
def setup_inputs_shrink(rng):
    low = np.arange(N) >= N - N // 4
    def make():
        d = plain(rng)
        size = np.exp2(np.where(low, -30.0, 23.0)[:, None] + 2 * rng.random((N, P))) * (1 - 2 * rng.integers(0, 2, (N, P)))
        d["c"] = ((1 + rng.random((N, 128, 4 * P))) * np.repeat(size, 4, axis=1)[:, None, :]).astype(np.float32).astype(BF)
        on = ~low[:, None] | np.stack([rng.permutation(128) < 2 for r in range(N)])
        for t in range(R):
            g = np.exp2(np.where(low, 8.0 * (R - 1 - t) - 30.0, 21.0 - 8.0 * t))
            d["qt"][:, :, 4 * t:4 * t + 4] = ((1 + rng.random((N, 128, 4))) * (g[:, None] * on)[:, :, None]).astype(np.float32).astype(BF)
        return d
    def good(s):
        h, a, b = play(s), np.zeros(N, bool), np.zeros(N, bool)
        for r in range(N):
            at, use, since = np.arange(P * r, P * r + P), np.zeros(P, np.float32), np.zeros(P, int)
            if low[r] and np.abs(s[at, r, R - 1]).max() > 2.0 ** -50 or not low[r] and np.abs(s[at, r, 0]).min() < 2.0 ** 50: return False
            for t in range(R):
                v = s[at, r]
                use = use + v[:, t] * v[:, t]
                sums = np.concatenate([np.zeros((P, 1), np.float32), np.cumsum(v * v, axis=1)], axis=1)
                diff = sums[:, t + 1] - sums[np.arange(P), since]
                a[r] |= (np.argsort(use, kind="stable")[:K] != np.argsort(diff, kind="stable")[:K]).any()
                b[r] |= np.sort(use)[K - 1] > 1e30
                moved = h[t, r] != at
                at = h[t, r]
                use[moved] = 0
                since[moved] = t + 1
        return bool(2 * a.sum() > N and 2 * b.sum() > N)
    return first(make, good)
def setup_inputs_turn(rng):
    on = (np.arange(128) // (128 // N))[None, :] == np.arange(N)[:, None]
    def make():
        d = plain(rng)
        d["c"] = times(d["c"], np.where(on, 2.0 ** -8, 1.0)[:, :, None])
        d["qt"] = times(d["qt"], on[:, :, None])
        return d
    return first(make, lambda s: bool((~athome(s)).any(axis=1).all()))
def setup_inputs_spread(rng):
    return first(lambda: {**plain(rng), "c": wide(rng, N, 128, 4 * P, cols=6)})
def check_inputs(d):
    b = []
    for k in ("c", "qt", "w"):
        v = np.abs(d[k].astype(np.float32))
        if not (np.isfinite(v).all() and ((v == 0) | (v >= 2.0 ** -30) & (v <= 2.0 ** 30)).all()): b.append("a value of " + k)
    if (d["qt"][:, :, 4 * R:].astype(np.float32) != 0).any(): b.append("qt has numbers behind its first R columns")
    if not b and not fit(scores(d["c"], d["qt"])): b.append("a score")
    return b
def reference(c, qt, w):
    held = play(scores(c, qt))
    every = np.concatenate([c[q] for q in range(N)], axis=1)
    y = np.zeros((N, 128, R * O * P), np.float32)
    for r in range(N):
        u, at = np.unique(held[:, r].reshape(-1), return_inverse=True)
        at = at.reshape(R, P)
        q = mx_ref.quantize(cols(every, np.concatenate([u, np.full(-len(u) % 4, -1)])))
        for o in range(O):
            z = mx_ref.matmul(mx_ref.quantize(cut(w[r], o)), q)
            for t in range(R):
                i = (t * O + o) * P
                y[r, :, i:i + P] = z[:, at[t]]
    return {"y": y}

@@ -1,0 +1,378 @@
+from concourse.bass import DstId, RemoteDMATransfer
+from concourse.mybir import dt, AluOpType, AxisListType, ActivationFunctionType
+
+N, P, K, R, O = 8, 256, 48, 6, 2
+PART = [1, 2, 4, 1, 2, 4]
+NE = 8
+W = [P + K * t for t in range(R)]
+PRED = 1.0 - 2.0 ** -24
+TINY = 2.0 ** -122
+PAD = 3 * K
+RADIX = 512
+
+F32, CODE, U8, U16, BF = "float32", "float8_e4m3fn_x4", "uint8", "uint16", "bfloat16"
+SCRATCH = {n: ("sbuf", [128, w], d) for n, w, d in (
+    ("cb", 4 * P, BF), ("qb", 512, BF), ("wb", 512 * O, BF),
+    ("qc", 128, CODE), ("qs", 128, U8), ("rc", 128 * R, CODE), ("rs", 128 * R, U8), ("wc", 128 * O, CODE), ("ws", 128 * O, U8),
+    ("VZ", 2 * P, F32), ("U", P, F32), ("F", P, F32), ("A", K, F32), ("A2", K, F32), ("FX", 2 * K, F32), ("ZA", 2 * K, F32),
+    ("EK", 2 * K, F32), ("EP", 2 * K + 2, F32), ("vc", 2, F32), ("pl", 2, F32), ("OG", 64, F32), ("TC", 64, F32), ("big", K, F32),
+    ("C", 2 * (P + K + 1), F32), ("S", 4, F32), ("J", P, F32), ("JS", P, F32), ("zz", 32, F32), ("bc", 64, F32), ("RC", 64, F32),
+    ("E", 195, F32), ("JE", 130, F32), ("Pm", 4, F32), ("T1", 4, F32), ("T2", 4, F32), ("lo", 4, F32), ("hi", 4, F32),
+    ("pi", 4, "int32"), ("gi", 4, "int32"), ("pf", 4, F32), ("GL", 4, U16), ("du", 6, U16), ("qo", 8 * R, U16),
+    ("PT", P + K * R, F32), ("G6", 96, F32), ("T6", 96, F32), ("D", 8, F32),
+    ("Y", O * P, F32), ("YA", O * K, F32), ("p6c", 128, CODE), ("p6s", 128 + PAD, U8))}
+for _t in range(R):
+    for _n, _w, _d in (("p%dc", W[_t], CODE), ("p%ds", W[_t] + PAD, U8), ("o%dc", K, CODE), ("o%ds", K + PAD, U8),
+                       ("L%d", 4, U16), ("LP%d", 4, U16), ("Q%d", P, F32), ("AQ%d", K, F32)):
+        if _t or _d != F32:
+            SCRATCH[_n % _t] = ("sbuf", [128, _w], _d)
+for _b in range(8):
+    SCRATCH["b%d" % _b] = ("psum", [128, 512], F32)
+NDMA = 28
+SEMAPHORES = ["sv", "sa", "st", "sp", "sent"] + ["arr%d" % t for t in range(R)] + ["d%d" % i for i in range(NDMA)]
+
+
+def rank_program(g, core, T, topo):
+    rank = T.rank_of(core)
+    if rank is None:
+        return
+    op_ = AluOpType
+    act = ActivationFunctionType
+    X = AxisListType.X
+    queues = {"v": g.vector, "a": g.scalar, "t": g.tensor, "p": g, "s": g.sync}
+    count = {"v": 0, "a": 0, "t": 0, "p": 0, "d": 0}
+    seen = {}
+    log = {}
+    psum = {"b%d" % b for b in range(8)}
+
+    def V(n, c0=0, c1=None, p0=0, p1=128, s=1):
+        return (n, p0, p1, c0, SCRATCH[n][1][1] if c1 is None else c1, s)
+
+    def ap(v):
+        n, p0, p1, c0, c1, s = v
+        return T[n][p0:p1, c0:c1] if s == 1 else T[n][p0:p1, c0:c1:s]
+
+    def u8(v):
+        return ap(v).bitcast(dt.uint8)
+
+    def wait(q, sem, val):
+        if seen.get((q, sem), 0) < val:
+            seen[(q, sem)] = val
+            queues[q].wait_ge(T.sem[sem], val)
+
+    def order(q, sem, val, writes, reads):
+        need = {}
+        for views, wr in ((reads, False), (writes, True)):
+            for n, p0, p1, c0, c1, s in views:
+                whole = n in psum
+                for a0, a1, b0, b1, w2, q2, sem2, val2 in log.get(n, ()):
+                    if not whole and (a1 <= p0 or p1 <= a0 or b1 <= c0 or c1 <= b0):
+                        continue
+                    if whole and q2 == q and not (w2 and not wr):
+                        continue
+                    if not whole and not (w2 or wr):
+                        continue
+                    if q2 == q and q != "s" and not w2:
+                        continue
+                    need[sem2] = max(need.get(sem2, 0), val2)
+        for s2 in sorted(need):
+            wait(q, s2, need[s2])
+        for views, wr in ((reads, False), (writes, True)):
+            for n, p0, p1, c0, c1, s in views:
+                old = log.setdefault(n, [])
+                if wr and s == 1:
+                    old[:] = [e for e in old if not (p0 <= e[0] and e[1] <= p1 and c0 <= e[2] and e[3] <= c1)]
+                old.append((p0, p1, c0, c1, wr, q, sem, val))
+
+    def op(q, writes, reads, fn):
+        count[q] += 1
+        sem = "s" + q
+        order(q, sem, count[q], writes, reads)
+        fn().then_inc(T.sem[sem], 1)
+
+    def dma(q, out, in_, writes, reads):
+        sem = "d%d" % count["d"]
+        count["d"] += 1
+        order(q, sem, 16, writes, reads)
+        queues[q].dma_start(out, in_).then_inc(T.sem[sem], 16)
+
+    def ts(out, in0, s1, s2, o0, o1=None):
+        r = [in0] + [s for s in (s1, s2) if isinstance(s, tuple)]
+        a1 = ap(s1) if isinstance(s1, tuple) else s1
+        a2 = ap(s2) if isinstance(s2, tuple) else s2
+        if o1 is None:
+            op("v", [out], r, lambda: g.vector.tensor_scalar(ap(out), ap(in0), a1, None, o0))
+        else:
+            op("v", [out], r, lambda: g.vector.tensor_scalar(ap(out), ap(in0), a1, a2, o0, o1))
+
+    def tt(out, a, b, o):
+        op("v", [out], [a, b], lambda: g.vector.tensor_tensor(ap(out), ap(a), ap(b), o))
+
+    def copy(out, a):
+        op("v", [out], [a], lambda: g.vector.tensor_copy(ap(out), ap(a)))
+
+    def gather(out, win, off):
+        op("v", [out], [win, off], lambda: g.vector.tensor_copy(ap(out), ap(win).indirect(ap(off))))
+
+    def scatter(win, off, a):
+        op("v", [win], [a, off], lambda: g.vector.tensor_copy(ap(win).indirect(ap(off)), ap(a)))
+
+    def turn(out, a):
+        op("v", [out], [a], lambda: g.vector.transpose(ap(out), ap(a)))
+
+    def fill(v, x):
+        op("v", [v], [], lambda: g.vector.memset(ap(v), x))
+
+    def sact(out, a, f):
+        op("a", [out], [a], lambda: g.scalar.activation(ap(out), ap(a), f))
+
+    def asum(out, junk, a):
+        op("a", [out, junk], [a], lambda: g.scalar.activation(ap(junk), ap(a), act.Copy, accum_out=ap(out)))
+
+    def vsum(out, a, o=op_.add):
+        op("v", [out], [a], lambda: g.vector.tensor_reduce(ap(out), ap(a), X, o))
+
+    def quant(c, s, a):
+        op("v", [c, s], [a], lambda: g.vector.quantize_mx(ap(c), ap(s), ap(a)))
+
+    def mm(bank, n, lc, ls, rc, rs):
+        out = V(bank, 0, n)
+        op("t", [out], [lc, ls, rc, rs], lambda: g.tensor.matmul_mx(ap(out), ap(lc), ap(ls), ap(rc), ap(rs), True, True))
+
+    def pick(oc, os, c, s, off):
+        op("v", [oc], [c, off], lambda: g.vector.tensor_copy(ap(oc).bitcast(dt.uint32), ap(c).bitcast(dt.uint32).indirect(ap(off))))
+        op("a", [os], [s, off], lambda: g.scalar.activation(ap(os), ap(s).indirect(ap(off)), act.Copy))
+
+    def qrep(a, b):
+        pick(V("rc", 128 * a, 128 * b), V("rs", 128 * a, 128 * b), V("qc"), V("qs"), V("qo", 8 * a, 8 * b))
+
+    def rep(t):
+        return V("rc", 128 * t, 128 * t + 128), V("rs", 128 * t, 128 * t + 128)
+
+    def tile(o):
+        return V("wc", 128 * o, 128 * o + 128), V("ws", 128 * o, 128 * o + 128)
+
+    def whole(v, out, **k):
+        op("p", [v], [], lambda: g.iota(ap(v), *out, **k))
+
+    dma("s", ap(V("cb")), T.c[:], [V("cb")], [])
+    dma("a", ap(V("qb")), T.qt[:], [V("qb")], [])
+    dma("s", ap(V("wb")), T.w[:], [V("wb")], [])
+    c0lo, c0hi, c0ar = V("C", 0, 128), V("C", 128, 256), V("C", 256, 304)
+    sl = V("C", 304, 306)
+    c1ar, c1lo, c1hi = V("C", 306, 354), V("C", 354, 482), V("C", 482, 610)
+    fl = {"allow_small_or_imprecise_dtypes": True}
+    whole(V("pi", 0, 1), ([[0, 1]], 0, 1))
+    whole(V("gi"), ([[128, 2], [16, 2]], 0, 0))
+    whole(sl, ([[128, 2]], 0, 1), **fl)
+    whole(V("pl"), ([[128, 2]], 0, 1), **fl)
+    whole(V("PT", 0, P), ([[1, P]], 0, 0), **fl)
+    fill(V("F"), PRED)
+    op("p", [V("F")], [V("F")], lambda: g.affine_select(ap(V("F")), ap(V("F")), [[0, 2], [-1, 128]], op_.is_gt, 1.0, 0, 1))
+    for t in range(R):
+        fill(V("qo", 8 * t, 8 * t + 8), t)
+    fill(V("zz"), 0.0)
+    fill(V("E"), 0.0)
+    fill(c0ar, 0.0)
+    fill(c1ar, 0.0)
+    fill(V("big"), 1e29)
+    ts(V("pi", 1, 2), V("pi", 0, 1), 0x6F, None, op_.bitwise_and)
+    ts(V("pi", 2, 3), V("pi", 0, 1), 0x0F, None, op_.bitwise_and)
+    copy(V("pf", 1, 3), V("pi", 1, 3))
+    ts(V("GL"), V("gi"), V("pf", 1, 2), None, op_.add)
+    ts(V("big"), V("big"), 1e9, None, op_.mult)
+    span = P * RADIX - (RADIX - 1)
+    for m in range(3):
+        ts(V("lo", m, m + 1), V("pf", 2, 3), float(RADIX), float(16 * RADIX * m), op_.mult, op_.add)
+        ts(V("E", 65 * m + 64, 65 * m + 65, 0, 32), V("pf", 2, 3, 0, 32), float(-span), float(-(span * 16 * m + (RADIX - 1) * (P - 1))), op_.mult, op_.add)
+        for j in (2 * m, 2 * m + 1):
+            ts(V("du", j, j + 1), V("pf", 2, 3), float(16 * m), None, op_.add)
+    ts(V("hi", 0, 3), V("lo", 0, 3), float(RADIX - 1), None, op_.add)
+    quant(V("qc"), V("qs"), V("qb"))
+    qrep(0, 1)
+    qrep(1, 2)
+    own = V("p0c"), V("p0s", 0, P)
+    quant(*own, V("cb"))
+
+    mm("b0", P, *rep(0), *own)
+    for x in range(2):
+        mm("b%d" % (6 + x), 128, V("p0c", 128 * x, 128 * x + 128), V("p0s", 128 * x, 128 * x + 128), V("qc"), V("qs"))
+    for x in (1, 0):
+        sact(V("U", 128 * x, 128 * x + 128), V("b0", 128 * x, 128 * x + 128), act.Square)
+    for x in range(2):
+        s0 = V("b%d" % (6 + x), 0, 1)
+        ts(V("vc", x, x + 1), s0, s0, TINY, op_.mult, op_.max)
+    for x in (1, 0):
+        ts(V("VZ", 128 * x, 128 * x + 128), V("U", 128 * x, 128 * x + 128), TINY, None, op_.max)
+
+    def gap(k=1):
+        for _ in range(min(k, len(fill_in))):
+            fill_in.pop(0)()
+
+    def store(t):
+        dma("s", T.y[:, t * O * P:(t + 1) * O * P], ap(V("Y")), [], [V("Y")])
+
+    for t in range(R + 1):
+        more = t + 1 < R
+        fill_in, at_end = [], []
+        D0, D1, D2, D3 = V("D", 0, 2), V("D", 2, 4), V("D", 4, 6), V("D", 6, 8)
+        if t:
+            n = W[t] if t < R else 128
+            log.setdefault("p%dc" % t, []).append((0, 128, n - K, n, True, "net", "arr%d" % (t - 1), NE))
+            log.setdefault("p%ds" % t, []).append((0, 128, n - K, n + PAD, True, "net", "arr%d" % (t - 1), NE))
+            wnd = V("p%dc" % t, n - 128, n), V("p%ds" % t, n - 128, n)
+            lp = V("LP%d" % (t - 1), 0, 3)
+            if t < R:
+                mm("b0", 128, *rep(t), *wnd)
+                sact(V("A"), V("b0", 80, 128), act.Square)
+        else:
+            for t2 in range(R):
+                v = V("o%ds" % t2, K, K + PAD)
+                dma("s", ap(v), ap(V("p0s", 0, PAD)), [v], [V("p0s", 0, PAD)])
+        if t < R:
+            n2 = W[t] if more else 80
+            for x in "cs":
+                a, b = V("p%d%s" % (t, x), 0, n2), V("p%d%s" % (t + 1, x), 0, n2)
+                dma("s", u8(b) if x == "c" else ap(b), u8(a) if x == "c" else ap(a), [b], [a])
+            if 1 < t < R - 1:
+                store(t - 2)
+        if t:
+            def later(t2, b):
+                mm(b, 128, *rep(t2), *wnd)
+                sact(V("AQ%d" % t2), V(b, 80, 128), act.Square)
+                fill_in.append(lambda: scatter(V("Q%d" % t2), lp, V("AQ%d" % t2)))
+
+            def result(o):
+                mm("b%d" % (6 + o), 128, *tile(o), *wnd)
+                sact(V("YA", K * o, K * o + K), V("b%d" % (6 + o), 80, 128), act.Copy)
+
+                def put():
+                    scatter(V("Y", P * o, P * o + P), lp, V("YA", K * o, K * o + K))
+                    i = (t - 1) * O * P
+                    if t == R:
+                        dma("sa"[o], T.y[:, i + P * o:i + P * o + P], ap(V("Y", P * o, P * o + P)), [], [V("Y", P * o, P * o + P)])
+                    elif o == O - 1 and t >= R - 2:
+                        store(t - 1)
+                (at_end if t == R - 2 else fill_in).append(put)
+
+            if more:
+                fill_in.append(lambda: scatter(V("U"), lp, V("A")))
+                later(t + 1, "b1")
+            for o in range(O):
+                result(o)
+            for t2 in range(t + 2, R):
+                later(t2, "b%d" % (t2 - t))
+            if t < R:
+                tt(V("EP", 0, K), V("EK", 0, K), V("A"), op_.mult)
+                tt(V("EP", K + 1, 2 * K + 1), V("EK", K, 2 * K), V("A"), op_.mult)
+                ts(V("A2"), V("A"), TINY, None, op_.max)
+                vsum(V("vc", 0, 1), V("EP", 0, K + 1), op_.max)
+                vsum(V("vc", 1, 2), V("EP", K + 1, 2 * K + 2), op_.max)
+                for x in range(2):
+                    tt(V("ZA", K * x, K * x + K), V("A2"), V("FX", K * x, K * x + K), op_.mult)
+        else:
+            fill_in += [lambda: quant(V("wc"), V("ws"), V("wb")), lambda: qrep(2, 4), lambda: qrep(4, 6)]
+        if t < R:
+            v0, v1 = V("vc", 0, 1), V("vc", 1, 2)
+            f = float(RADIX)
+            if not t:
+                ts(c0hi, V("VZ", 128, 256), v0, f, op_.is_lt, op_.mult)
+                ts(c1lo, V("VZ", 0, 128), v1, f, op_.is_le, op_.mult)
+                tt(V("VZ", P, 2 * P), V("VZ", 0, P), V("F"), op_.mult)
+            ts(c0lo, V("VZ", 256, 384), v0, f, op_.is_lt, op_.mult)
+            if t:
+                ts(c0hi, V("VZ", 128, 256), v0, f, op_.is_lt, op_.mult)
+            asum(V("S", 0, 1), V("J"), V("C", 0, 256))
+            if t:
+                ts(c1lo, V("VZ", 0, 128), v1, f, op_.is_le, op_.mult)
+            ts(c1hi, V("VZ", 384, 512), v1, f, op_.is_lt, op_.mult)
+            asum(V("S", 1, 2), V("JS"), V("C", 354, 610))
+            if t:
+                ts(c0ar, V("ZA", 0, K), v0, f, op_.is_lt, op_.mult)
+                ts(c1ar, V("ZA", K, 2 * K), v1, f, op_.is_lt, op_.mult)
+                gap(more)
+            vsum(V("S", 3, 4), V("C", 256, 305))
+            vsum(V("S", 2, 3), V("C", 305, 354))
+            gap(not t)
+            ts(V("bc", 0, 32), V("zz"), V("S", 0, 1), V("S", 3, 4), op_.add, op_.add)
+            ts(V("bc", 32, 64), V("zz"), V("S", 1, 2), V("S", 2, 3), op_.add, op_.add)
+            turn(V("RC"), V("bc"))
+            for m in range(3):
+                ts(V("E", 65 * m, 65 * m + 64), V("RC"), V("lo", m, m + 1), V("hi", m, m + 1), op_.max, op_.min)
+                if m < 2:
+                    asum(V("Pm", m, m + 1), V("JE", 65 * m, 65 * m + 65), V("E", 65 * m, 65 * m + 65))
+            if more:
+                tt(D0, V("bc", 0, 64, s=32), sl, op_.subtract)
+            vsum(V("Pm", 2, 3), V("E", 130, 195))
+            for a in (0, 64):
+                tt(V("T1", 0, 3, a, a + 64), V("Pm", 0, 3, a, a + 64), V("Pm", 0, 3, 64 - a, 128 - a), op_.add)
+            if more:
+                ts(D1, D0, 1.0 / RADIX, float(W[t]), op_.mult, op_.add)
+                ts(D2, D0, float(RADIX * K), None, op_.is_ge)
+            for a in (0, 32, 64, 96):
+                b = a ^ 32
+                tt(V("T2", 0, 3, a, a + 32), V("T1", 0, 3, a, a + 32), V("T1", 0, 3, b, b + 32), op_.add)
+            if more:
+                tt(D3, sl, D1, op_.subtract)
+            lst = V("L%d" % t, 0, 3)
+            copy(lst, V("T2", 0, 3))
+            pick(V("o%dc" % t), V("o%ds" % t, 0, K), V("p%dc" % t), V("p%ds" % t, 0, W[t]), lst)
+            dst = T.cores[rank ^ PART[t]]
+            rid, pid, _e = topo.addr(dst)
+            engs = topo.engines(core, dst)[:NE]
+            n1 = W[t + 1] if more else 128
+            order("p", "sent", 0, [], [V("o%dc" % t), V("o%ds" % t)])
+            g.remote_dma_fused([
+                RemoteDMATransfer(dst_ids=[DstId(rid=rid, pnc=pid)], dma_engine_mask=sum(1 << e for e in es), remote_sem=T.sem["arr%d" % t], src=src, dst=out)
+                for es, src, out in (
+                    (engs[0::2], u8(V("o%dc" % t)), u8(V("p%dc" % (t + 1), n1 - K, n1))),
+                    (engs[1::2], ap(V("o%ds" % t)), ap(V("p%ds" % (t + 1), n1 - K, n1 + PAD))))], local_sem=T.sem["sent"])
+            new = V("PT", W[t], W[t] + K)
+            gather(new, V("PT", 0, W[t]), lst)
+            if t == 0:
+                mm("b1", P, *rep(1), *own)
+                sact(V("Q1"), V("b1", 0, P), act.Square)
+            gap(bool(t))
+            gather(V("G6"), new, V("du"))
+            if more:
+                tt(D3, D3, D2, op_.mult)
+            gap()
+            turn(V("T6"), V("G6"))
+            if more:
+                tt(V("U"), V("U"), V("Q%d" % (t + 1)), op_.add)
+                tt(sl, D1, D3, op_.add)
+            copy(V("LP%d" % t, 0, 3), V("T6", 0, 96, s=32))
+        if more:
+            gap()
+            scatter(V("U"), V("LP%d" % t, 0, 3), V("big"))
+            gap()
+            ts(V("VZ", 0, P), V("U"), TINY, None, op_.max)
+            for x in range(2):
+                ts(V("EK", K * x, K * x + K), new, V("pl", x, x + 1), None, op_.is_equal)
+                ts(V("FX", K * x, K * x + K), new, V("pl", x, x + 1), PRED, op_.is_ge, op_.max)
+            gather(V("OG"), V("VZ", 0, P), V("GL"))
+            tt(V("VZ", P, 2 * P), V("VZ", 0, P), V("F"), op_.mult)
+            turn(V("TC"), V("OG"))
+        gap(len(fill_in))
+        for put in at_end:
+            put()
+        if t == 0:
+            for t2 in range(2, R):
+                b = "b%d" % t2
+                mm(b, P, *rep(t2), *own)
+                sact(V("Q%d" % t2), V(b, 0, P), act.Square)
+            for o in range(O):
+                b = "b%d" % (6 + o)
+                mm(b, P, *tile(o), *own)
+                sact(V("Y", P * o, P * o + P), V(b, 0, P), act.Copy)
+        if more:
+            for x in range(2):
+                ts(V("EP", 49 * x + K, 49 * x + K + 1), V("TC", 32 * x, 32 * x + 1), V("D", 4 + x, 5 + x), TINY, op_.mult, op_.max)
+
+    for q in "vatp":
+        wait("p", "s" + q, count[q])
+    for i in range(count["d"]):
+        wait("p", "d%d" % i, 16)
+    for t in range(R):
+        wait("p", "arr%d" % t, NE)
+    wait("p", "sent", NE * R)

@@ -4,31 +4,39 @@ from concourse.mybir import dt, AluOpType, AxisListType, ActivationFunctionType
 N, P, K, R, O = 8, 256, 48, 6, 2
 PART = [1, 2, 4, 1, 2, 4]
 NE = 8
-W = [P + K * t for t in range(R)]
-PRED = 1.0 - 2.0 ** -24
+W = [P + K * t for t in range(R + 1)]
+STEP = 2.0 ** -24
+PRED = 1.0 - STEP
 TINY = 2.0 ** -122
+NIL = 2.0 ** -86
+UNIT = 2.0 ** -17
 PAD = 3 * K
-RADIX = 512
+ITEMS = 3 * 128
+XW = K + 64
+BW = 3 * XW // 2
+EW = 97
 
-F32, CODE, U8, U16, BF = "float32", "float8_e4m3fn_x4", "uint8", "uint16", "bfloat16"
+F32, CODE, U8, U16, BF, I32 = "float32", "float8_e4m3fn_x4", "uint8", "uint16", "bfloat16", "int32"
 SCRATCH = {n: ("sbuf", [128, w], d) for n, w, d in (
     ("cb", 4 * P, BF), ("qb", 512, BF), ("wb", 512 * O, BF),
     ("qc", 128, CODE), ("qs", 128, U8), ("rc", 128 * R, CODE), ("rs", 128 * R, U8), ("wc", 128 * O, CODE), ("ws", 128 * O, U8),
-    ("VZ", 2 * P, F32), ("U", P, F32), ("F", P, F32), ("A", K, F32), ("A2", K, F32), ("FX", 2 * K, F32), ("ZA", 2 * K, F32),
-    ("EK", 2 * K, F32), ("EP", 2 * K + 2, F32), ("vc", 2, F32), ("pl", 2, F32), ("OG", 64, F32), ("TC", 64, F32), ("big", K, F32),
-    ("C", 2 * (P + K + 1), F32), ("S", 4, F32), ("J", P, F32), ("JS", P, F32), ("zz", 32, F32), ("bc", 64, F32), ("RC", 64, F32),
-    ("E", 195, F32), ("JE", 130, F32), ("Pm", 4, F32), ("T1", 4, F32), ("T2", 4, F32), ("lo", 4, F32), ("hi", 4, F32),
-    ("pi", 4, "int32"), ("gi", 4, "int32"), ("pf", 4, F32), ("GL", 4, U16), ("du", 6, U16), ("qo", 8 * R, U16),
-    ("PT", P + K * R, F32), ("G6", 96, F32), ("T6", 96, F32), ("D", 8, F32),
-    ("Y", O * P, F32), ("YA", O * K, F32), ("p6c", 128, CODE), ("p6s", 128 + PAD, U8))}
+    ("IT", W[R], F32), ("SV", W[R], F32), ("PT", W[R] + 2, F32), ("F", P, F32), ("DM", 64, F32), ("DP", K + 2, F32),
+    ("pi", 4, I32), ("gi", 8, I32), ("pf", 4, F32), ("pn", 2, F32), ("pl", 2, F32), ("I17", 17, F32), ("M16", 32, F32),
+    ("li", 3, F32), ("lo", 3, F32), ("hi", 3, F32), ("bi", R, F32), ("bs", R, F32), ("big", K, F32),
+    ("GL", 8, U16), ("QL", 4, U16), ("qo", 8 * R, U16), ("LS", 16, U16),
+    ("U", P, F32), ("ZS", 2 * P, F32), ("ZF", P, F32), ("G2", P + K, F32), ("RZ", P, F32), ("SQ", W[R - 2], F32),
+    ("A", K, F32), ("A2", K, F32), ("Z2", K, F32), ("G", 2 * K, F32), ("CM", 2 * K, F32), ("v", 4, F32),
+    ("CS", 2 * P, F32), ("C2", P, F32), ("J", 3 * P, F32), ("JE", 2 * EW, F32), ("S", 4, F32), ("X", 3 * XW, F32), ("BC", BW, F32),
+    ("RC", 96, F32), ("E", 3 * EW, F32), ("Pm", 4, F32), ("T1", 4, F32), ("T2", 4, F32),
+    ("D1", K, F32), ("D2", K + 2, F32), ("DS", P, F32), ("OG", 128, F32), ("TC", 128, F32),
+    ("ZP", O * W[R], F32), ("Y", 2 * O * P, F32), ("YL", O * P, F32), ("YA", O * K, F32), ("p6c", 128, CODE), ("p6s", 128 + PAD, U8))}
 for _t in range(R):
     for _n, _w, _d in (("p%dc", W[_t], CODE), ("p%ds", W[_t] + PAD, U8), ("o%dc", K, CODE), ("o%ds", K + PAD, U8),
-                       ("L%d", 4, U16), ("LP%d", 4, U16), ("Q%d", P, F32), ("AQ%d", K, F32)):
-        if _t or _d != F32:
-            SCRATCH[_n % _t] = ("sbuf", [128, _w], _d)
+                       ("L%d", 4, U16), ("LP%d", 4, U16)):
+        SCRATCH[_n % _t] = ("sbuf", [128, _w], _d)
 for _b in range(8):
     SCRATCH["b%d" % _b] = ("psum", [128, 512], F32)
-NDMA = 28
+NDMA = 30
 SEMAPHORES = ["sv", "sa", "st", "sp", "sent"] + ["arr%d" % t for t in range(R)] + ["d%d" % i for i in range(NDMA)]
 
 
@@ -38,7 +46,6 @@ def rank_program(g, core, T, topo):
         return
     op_ = AluOpType
     act = ActivationFunctionType
-    X = AxisListType.X
     queues = {"v": g.vector, "a": g.scalar, "t": g.tensor, "p": g, "s": g.sync}
     count = {"v": 0, "a": 0, "t": 0, "p": 0, "d": 0}
     seen = {}
@@ -48,12 +55,20 @@ def rank_program(g, core, T, topo):
     def V(n, c0=0, c1=None, p0=0, p1=128, s=1):
         return (n, p0, p1, c0, SCRATCH[n][1][1] if c1 is None else c1, s)
 
+    def col(n, c):
+        return V(n, c, c + 1)
+
     def ap(v):
+        if not isinstance(v, tuple):
+            return v
         n, p0, p1, c0, c1, s = v
         return T[n][p0:p1, c0:c1] if s == 1 else T[n][p0:p1, c0:c1:s]
 
     def u8(v):
         return ap(v).bitcast(dt.uint8)
+
+    def views(*xs):
+        return [x for x in xs if isinstance(x, tuple)]
 
     def wait(q, sem, val):
         if seen.get((q, sem), 0) < val:
@@ -62,11 +77,11 @@ def rank_program(g, core, T, topo):
 
     def order(q, sem, val, writes, reads):
         need = {}
-        for views, wr in ((reads, False), (writes, True)):
-            for n, p0, p1, c0, c1, s in views:
+        for vs, wr in ((reads, False), (writes, True)):
+            for n, p0, p1, c0, c1, s in vs:
                 whole = n in psum
-                for a0, a1, b0, b1, w2, q2, sem2, val2 in log.get(n, ()):
-                    if not whole and (a1 <= p0 or p1 <= a0 or b1 <= c0 or c1 <= b0):
+                for a0, a1, b0, b1, s2, w2, q2, sem2, val2 in log.get(n, ()):
+                    if not whole and (a1 <= p0 or p1 <= a0 or b1 <= c0 or c1 <= b0 or (s == s2 and (c0 - b0) % s)):
                         continue
                     if whole and q2 == q and not (w2 and not wr):
                         continue
@@ -77,12 +92,12 @@ def rank_program(g, core, T, topo):
                     need[sem2] = max(need.get(sem2, 0), val2)
         for s2 in sorted(need):
             wait(q, s2, need[s2])
-        for views, wr in ((reads, False), (writes, True)):
-            for n, p0, p1, c0, c1, s in views:
+        for vs, wr in ((reads, False), (writes, True)):
+            for n, p0, p1, c0, c1, s in vs:
                 old = log.setdefault(n, [])
                 if wr and s == 1:
                     old[:] = [e for e in old if not (p0 <= e[0] and e[1] <= p1 and c0 <= e[2] and e[3] <= c1)]
-                old.append((p0, p1, c0, c1, wr, q, sem, val))
+                old.append((p0, p1, c0, c1, s, wr, q, sem, val))
 
     def op(q, writes, reads, fn):
         count[q] += 1
@@ -97,16 +112,24 @@ def rank_program(g, core, T, topo):
         queues[q].dma_start(out, in_).then_inc(T.sem[sem], 16)
 
     def ts(out, in0, s1, s2, o0, o1=None):
-        r = [in0] + [s for s in (s1, s2) if isinstance(s, tuple)]
-        a1 = ap(s1) if isinstance(s1, tuple) else s1
-        a2 = ap(s2) if isinstance(s2, tuple) else s2
+        r = views(in0, s1, s2)
         if o1 is None:
-            op("v", [out], r, lambda: g.vector.tensor_scalar(ap(out), ap(in0), a1, None, o0))
+            op("v", [out], r, lambda: g.vector.tensor_scalar(ap(out), ap(in0), ap(s1), None, o0))
         else:
-            op("v", [out], r, lambda: g.vector.tensor_scalar(ap(out), ap(in0), a1, a2, o0, o1))
+            op("v", [out], r, lambda: g.vector.tensor_scalar(ap(out), ap(in0), ap(s1), ap(s2), o0, o1))
 
-    def tt(out, a, b, o):
-        op("v", [out], [a, b], lambda: g.vector.tensor_tensor(ap(out), ap(a), ap(b), o))
+    def tt(out, a, b, o, off=None):
+        op("v", [out], views(a, b, off), lambda: g.vector.tensor_tensor(ap(out), ap(a).indirect(ap(off)) if off else ap(a), ap(b), o))
+
+    def scan(out, a, b, first, o0, o1):
+        op("v", [out], views(a, b, first), lambda: g.vector.tensor_tensor_scan(ap(out), ap(a), ap(b), ap(first), o0, o1))
+
+    def total(out, a, first):
+        n, p0, p1, c0, c1, s = a
+        scan(out, V(n, c0, c1, s=2), V(n, c0 + 1, c1, s=2), first, op_.add, op_.add)
+
+    def vsum(out, a):
+        op("v", [out], [a], lambda: g.vector.tensor_reduce(ap(out), ap(a), AxisListType.X, op_.add))
 
     def copy(out, a):
         op("v", [out], [a], lambda: g.vector.tensor_copy(ap(out), ap(a)))
@@ -123,251 +146,288 @@ def rank_program(g, core, T, topo):
     def fill(v, x):
         op("v", [v], [], lambda: g.vector.memset(ap(v), x))
 
-    def sact(out, a, f):
-        op("a", [out], [a], lambda: g.scalar.activation(ap(out), ap(a), f))
+    def sact(out, a, f, off=None, **k):
+        op("a", [out], views(a, off, *k.values()), lambda: g.scalar.activation(
+            ap(out), ap(a).indirect(ap(off)) if off else ap(a), f, **{n: ap(x) for n, x in k.items()}))
 
-    def asum(out, junk, a):
-        op("a", [out, junk], [a], lambda: g.scalar.activation(ap(junk), ap(a), act.Copy, accum_out=ap(out)))
-
-    def vsum(out, a, o=op_.add):
-        op("v", [out], [a], lambda: g.vector.tensor_reduce(ap(out), ap(a), X, o))
+    def asum(out, junk, a, bias=0.0):
+        op("a", [out, junk], views(a, bias), lambda: g.scalar.activation(ap(junk), ap(a), act.Identity, bias=ap(bias), accum_out=ap(out)))
 
     def quant(c, s, a):
         op("v", [c, s], [a], lambda: g.vector.quantize_mx(ap(c), ap(s), ap(a)))
 
-    def mm(bank, n, lc, ls, rc, rs):
-        out = V(bank, 0, n)
+    def mm(bank, lc, ls, rc, rs):
+        out = V(bank, 0, rc[4] - rc[3])
         op("t", [out], [lc, ls, rc, rs], lambda: g.tensor.matmul_mx(ap(out), ap(lc), ap(ls), ap(rc), ap(rs), True, True))
 
     def pick(oc, os, c, s, off):
         op("v", [oc], [c, off], lambda: g.vector.tensor_copy(ap(oc).bitcast(dt.uint32), ap(c).bitcast(dt.uint32).indirect(ap(off))))
-        op("a", [os], [s, off], lambda: g.scalar.activation(ap(os), ap(s).indirect(ap(off)), act.Copy))
+        sact(os, s, act.Copy, off)
 
-    def qrep(a, b):
-        pick(V("rc", 128 * a, 128 * b), V("rs", 128 * a, 128 * b), V("qc"), V("qs"), V("qo", 8 * a, 8 * b))
+    def pair(n, a, b):
+        return V(n + "c", a, b), V(n + "s", a, b)
+
+    def qrep(a):
+        pick(*rep(a), V("qc"), V("qs"), V("qo", 8 * a, 8 * a + 8))
 
     def rep(t):
-        return V("rc", 128 * t, 128 * t + 128), V("rs", 128 * t, 128 * t + 128)
+        return pair("r", 128 * t, 128 * t + 128)
 
     def tile(o):
-        return V("wc", 128 * o, 128 * o + 128), V("ws", 128 * o, 128 * o + 128)
+        return pair("w", 128 * o, 128 * o + 128)
 
-    def whole(v, out, **k):
-        op("p", [v], [], lambda: g.iota(ap(v), *out, **k))
+    def whole(v, *pat):
+        k = {} if SCRATCH[v[0]][2] == I32 else {"allow_small_or_imprecise_dtypes": True}
+        op("p", [v], [], lambda: g.iota(ap(v), *pat, **k))
 
-    dma("s", ap(V("cb")), T.c[:], [V("cb")], [])
-    dma("a", ap(V("qb")), T.qt[:], [V("qb")], [])
-    dma("s", ap(V("wb")), T.w[:], [V("wb")], [])
-    c0lo, c0hi, c0ar = V("C", 0, 128), V("C", 128, 256), V("C", 256, 304)
-    sl = V("C", 304, 306)
-    c1ar, c1lo, c1hi = V("C", 306, 354), V("C", 354, 482), V("C", 482, 610)
-    fl = {"allow_small_or_imprecise_dtypes": True}
-    whole(V("pi", 0, 1), ([[0, 1]], 0, 1))
-    whole(V("gi"), ([[128, 2], [16, 2]], 0, 0))
-    whole(sl, ([[128, 2]], 0, 1), **fl)
-    whole(V("pl"), ([[128, 2]], 0, 1), **fl)
-    whole(V("PT", 0, P), ([[1, P]], 0, 0), **fl)
-    fill(V("F"), PRED)
-    op("p", [V("F")], [V("F")], lambda: g.affine_select(ap(V("F")), ap(V("F")), [[0, 2], [-1, 128]], op_.is_gt, 1.0, 0, 1))
-    for t in range(R):
-        fill(V("qo", 8 * t, 8 * t + 8), t)
-    fill(V("zz"), 0.0)
-    fill(V("E"), 0.0)
-    fill(c0ar, 0.0)
-    fill(c1ar, 0.0)
-    fill(V("big"), 1e29)
-    ts(V("pi", 1, 2), V("pi", 0, 1), 0x6F, None, op_.bitwise_and)
-    ts(V("pi", 2, 3), V("pi", 0, 1), 0x0F, None, op_.bitwise_and)
-    copy(V("pf", 1, 3), V("pi", 1, 3))
-    ts(V("GL"), V("gi"), V("pf", 1, 2), None, op_.add)
-    ts(V("big"), V("big"), 1e9, None, op_.mult)
-    span = P * RADIX - (RADIX - 1)
-    for m in range(3):
-        ts(V("lo", m, m + 1), V("pf", 2, 3), float(RADIX), float(16 * RADIX * m), op_.mult, op_.add)
-        ts(V("E", 65 * m + 64, 65 * m + 65, 0, 32), V("pf", 2, 3, 0, 32), float(-span), float(-(span * 16 * m + (RADIX - 1) * (P - 1))), op_.mult, op_.add)
-        for j in (2 * m, 2 * m + 1):
-            ts(V("du", j, j + 1), V("pf", 2, 3), float(16 * m), None, op_.add)
-    ts(V("hi", 0, 3), V("lo", 0, 3), float(RADIX - 1), None, op_.add)
-    quant(V("qc"), V("qs"), V("qb"))
-    qrep(0, 1)
-    qrep(1, 2)
-    own = V("p0c"), V("p0s", 0, P)
-    quant(*own, V("cb"))
+    def select(v, pat, o, x, base, k):
+        op("p", [v], [v], lambda: g.affine_select(ap(v), ap(v), pat, o, x, base, k))
 
-    mm("b0", P, *rep(0), *own)
-    for x in range(2):
-        mm("b%d" % (6 + x), 128, V("p0c", 128 * x, 128 * x + 128), V("p0s", 128 * x, 128 * x + 128), V("qc"), V("qs"))
-    for x in (1, 0):
-        sact(V("U", 128 * x, 128 * x + 128), V("b0", 128 * x, 128 * x + 128), act.Square)
-    for x in range(2):
-        s0 = V("b%d" % (6 + x), 0, 1)
-        ts(V("vc", x, x + 1), s0, s0, TINY, op_.mult, op_.max)
-    for x in (1, 0):
-        ts(V("VZ", 128 * x, 128 * x + 128), V("U", 128 * x, 128 * x + 128), TINY, None, op_.max)
+    def half(n, x):
+        return V(n, 128 * x, 128 * x + 128)
 
     def gap(k=1):
         for _ in range(min(k, len(fill_in))):
             fill_in.pop(0)()
 
-    def store(t):
-        dma("s", T.y[:, t * O * P:(t + 1) * O * P], ap(V("Y")), [], [V("Y")])
+    Z, SR = V("ZS", 0, P), V("ZS", P, 2 * P)
+    q16 = col("pf", 2)
 
-    for t in range(R + 1):
+    dma("a", ap(V("qb", 0, 4 * R)), T.qt[:, 0:4 * R], [V("qb", 0, 4 * R)], [])
+    for x in range(2):
+        dma("sa"[x], ap(V("cb", 512 * x, 512 * x + 512)), T.c[:, 512 * x:512 * x + 512], [V("cb", 512 * x, 512 * x + 512)], [])
+    fill(V("qb", 4 * R), 0.0)
+    fill(V("F"), PRED)
+    whole(V("IT"), [[1, W[R]]], 0, 0)
+    whole(V("pi", 0, 1), [[0, 1]], 0, 1)
+    whole(V("pn"), [[128, 2]], 0, 1)
+    select(V("F"), [[0, 2], [-1, 128]], op_.is_gt, 1.0, 0, 1)
+    whole(V("li"), [[16, 3]], 0, 0)
+    whole(V("I17"), [[1, 17]], -1, 0)
+    whole(V("gi"), [[256, 2], [128, 2], [16, 2]], 0, 0)
+    whole(V("bi"), [[K, R]], 128, 1)
+    for t in range(R):
+        fill(V("qo", 8 * t, 8 * t + 8), t)
+    fill(V("BC", BW - 96), float(ITEMS))
+    fill(V("X"), 0.0)
+    fill(V("DP"), 0.0)
+    fill(V("big"), 1e29)
+    fill(col("DP", K + 1), -1.0)
+    quant(V("qc"), V("qs"), V("qb"))
+    ts(V("big"), V("big"), 1e9, None, op_.mult)
+    sact(V("SV"), V("IT"), act.Copy, scale=UNIT)
+    qrep(0)
+    ts(col("pi", 1), col("pi", 0), 0x6F, None, op_.bitwise_and)
+    ts(col("pi", 2), col("pi", 0), 0x0F, None, op_.bitwise_and)
+    ts(V("pl"), V("pn"), UNIT, None, op_.mult)
+    sact(V("PT", 0, P), V("IT", 0, P), act.Copy, scale=UNIT)
+    sact(V("PT", P), V("IT", 0, W[R] + 2 - P), act.Copy, scale=0.0)
+    own = pair("p0", 0, P)
+    for x in range(2):
+        quant(*pair("p0", 128 * x, 128 * x + 128), V("cb", 512 * x, 512 * x + 512))
+    dma("s", ap(V("wb")), T.w[:], [V("wb")], [V("cb")])
+    select(V("DP"), [[1, K + 2]], op_.not_equal, -4.0, 128 - K, -1)
+    select(V("DP"), [[1, K + 2]], op_.not_equal, 1.0, 127 - K, -1)
+
+    fill_in = [
+        lambda: copy(V("pf", 1, 3), V("pi", 1, 3)),
+        lambda: qrep(1),
+        lambda: qrep(2),
+        lambda: ts(V("lo"), V("li"), q16, None, op_.add),
+        lambda: qrep(3),
+        lambda: ts(V("hi"), V("lo"), 511.0 / 512, None, op_.add),
+        lambda: ts(V("E", EW - 1, 3 * EW, s=EW), V("lo"), -(ITEMS - 511.0 / 512) / 4, -(ITEMS - 1) * 511.0 / 2048, op_.mult, op_.add),
+        lambda: ts(V("M16", 0, 16), V("I17", 1, 17), q16, -4.0, op_.is_equal, op_.mult),
+        lambda: ts(V("M16", 16, 32), V("I17", 0, 16), q16, None, op_.is_equal),
+        lambda: ts(V("QL"), V("I17", 0, 4), 0.0, q16, op_.mult, op_.add),
+        lambda: tt(V("M16", 0, 16), V("M16", 0, 16), V("M16", 16, 32), op_.add),
+        lambda: ts(V("GL"), V("gi"), col("pf", 1), None, op_.add),
+        lambda: ts(col("pf", 0), col("pn", 0), float(128 - K), None, op_.is_lt),
+        lambda: ts(col("pf", 3), q16, 15.0, None, op_.is_lt),
+        lambda: ts(V("bs"), V("bi"), UNIT, col("pf", 0), op_.mult, op_.max),
+        lambda: quant(*tile(0), V("wb", 0, 512)),
+        lambda: quant(*tile(1), V("wb", 512, 1024))]
+
+    def cs(x, h):
+        return V("CS", P * x + 128 * h, P * x + 128 * h + 128)
+
+    def xs(m, n=K):
+        return V("X", XW * m, XW * m + n)
+
+    def store(t):
+        y = V("Y", t % 2 * O * P, (t % 2 + 1) * O * P)
+        dma("s", T.y[:, t * O * P:(t + 1) * O * P], ap(y), [], [y])
+
+    def ygather(t, o):
+        i = ((t - 1) % 2 * O + o) * P
+        sact(V("Y", i, i + P), V("ZP", W[R] * o, W[R] * o + W[t]), act.Copy, V("LS"))
+
+    def results(wnd, a, b, out):
+        for o in range(O):
+            mm("b%d" % (6 + o), *tile(o), *wnd)
+            sact(out(o), V("b%d" % (6 + o), a, b), act.Copy)
+
+    def compare(rows, v0, v1):
+        ts(cs(0, 1), half(rows, 1), v0, None, op_.is_lt)
+        ts(cs(0, 0), half("ZF", 0), v0, None, op_.is_lt)
+        ts(cs(1, 0), half(rows, 0), v1, None, op_.is_le)
+        ts(cs(1, 1), half("ZF", 1), v1, None, op_.is_lt)
+
+    def counts(*slots):
+        for x in range(2):
+            asum(col("S", x), V("J", P * x, P * x + P), V("CS", P * x, P * x + P), slots[x])
+
+    def diagonal(i):
+        scan(V("DS", 64 * i, 64 * i + 64), V("DM"), V("ZS", P + 64 * i, P + 64 * i + 64), 0.0, op_.add, op_.max)
+
+    for t in range(R):
         more = t + 1 < R
-        fill_in, at_end = [], []
-        D0, D1, D2, D3 = V("D", 0, 2), V("D", 2, 4), V("D", 4, 6), V("D", 6, 8)
-        if t:
-            n = W[t] if t < R else 128
-            log.setdefault("p%dc" % t, []).append((0, 128, n - K, n, True, "net", "arr%d" % (t - 1), NE))
-            log.setdefault("p%ds" % t, []).append((0, 128, n - K, n + PAD, True, "net", "arr%d" % (t - 1), NE))
-            wnd = V("p%dc" % t, n - 128, n), V("p%ds" % t, n - 128, n)
-            lp = V("LP%d" % (t - 1), 0, 3)
-            if t < R:
-                mm("b0", 128, *rep(t), *wnd)
-                sact(V("A"), V("b0", 80, 128), act.Square)
+        n = W[t]
+        if t == 0:
+            mm("b0", *rep(0), *own)
+            for x in range(2):
+                mm("b%d" % (3 + x), *pair("p0", 128 * x, 128 * x + 128), V("qc"), V("qs"))
+            for x in range(2):
+                sact(half("RZ", x), half("b0", x), act.Abs, bias=NIL)
+            gap(3)
+            for x in range(2):
+                s0 = col("b%d" % (3 + x), 0)
+                ts(col("v", 2 + x), s0, -1.0, s0, op_.mult, op_.max)
+            tt(half("ZF", 0), half("RZ", 0), half("F", 0), op_.mult)
+            ts(V("v", 0, 2), V("v", 2, 4), NIL, None, op_.max)
+            tt(half("ZF", 1), half("RZ", 1), half("F", 1), op_.mult)
+            compare("RZ", col("v", 0), col("v", 1))
+            counts(col("pl", 0), col("pl", 1))
+            gap(5)
+            for x in range(2):
+                ts(V("BC", BW - 96 + x, BW, s=3), V("X", K, K + 32), col("S", x), None, op_.add)
+            v = V("o0s", K, K + PAD)
+            dma("s", ap(v), ap(V("p0s", 0, PAD)), [v], [V("p0s", 0, PAD)])
+            sact(V("U"), V("b0", 0, P), act.Square)
         else:
-            for t2 in range(R):
+            log.setdefault("p%dc" % t, []).append((0, 128, n - K, n, 1, True, "net", "arr%d" % (t - 1), NE))
+            log.setdefault("p%ds" % t, []).append((0, 128, n - K, n + PAD, 1, True, "net", "arr%d" % (t - 1), NE))
+            wnd = pair("p%d" % t, n - 128, n)
+            mm("b0", *rep(t), *wnd)
+            mm("b1", *wnd, V("qc"), V("qs"))
+            sact(V("A"), V("b0", 128 - K, 128), act.Square)
+            counts(col("TC", 64), col("TC", 96))
+            s0, v0 = col("b1", t), col("v", 0)
+            ts(v0, s0, s0, TINY, op_.mult, op_.max)
+            ts(V("A2"), V("A"), TINY, None, op_.max)
+            ts(V("C2"), V("RZ"), v0, None, op_.is_lt)
+            asum(col("S", 2), V("J", 2 * P), V("C2"), col("bs", t))
+            results(wnd, 128 - K, 128, lambda o: V("ZP", W[R] * o + n - K, W[R] * o + n))
+            tt(V("Z2"), V("A2"), V("G2", P), op_.mult)
+            for x in range(2):
+                tt(xs(x), V("A2"), V("CM", K * x, K * x + K), op_.is_le)
+            ts(xs(2), V("Z2"), v0, None, op_.is_lt)
+            for m in range(3):
+                total(V("BC", m, BW, s=3), xs(m, XW), col("S", m))
+            if more:
+                fill_in.append(lambda: scatter(V("U"), V("LP%d" % (t - 1), 0, 3), V("A")))
+            fill_in += [lambda i=i: diagonal(i) for i in range(4)]
+            fill_in.append(lambda: ts(V("LS"), V("DS", 15, P, s=16), col("pf", 3), 1.0 / UNIT, op_.subtract, op_.mult))
+            if more:
+                mm("b2", *rep(t + 1), *pair("p%d" % t, 0, n))
+                sact(V("SQ", 0, n), V("b2", 0, n), act.Square)
+        n2 = n if more else 128 - K
+        for x in "cs":
+            a, b = V("p%d%s" % (t, x), 0, n2), V("p%d%s" % (t + 1, x), 0, n2)
+            dma("s", u8(b) if x == "c" else ap(b), u8(a) if x == "c" else ap(a), [b], [a])
+        if t == 0:
+            for t2 in range(1, R):
                 v = V("o%ds" % t2, K, K + PAD)
                 dma("s", ap(v), ap(V("p0s", 0, PAD)), [v], [V("p0s", 0, PAD)])
-        if t < R:
-            n2 = W[t] if more else 80
-            for x in "cs":
-                a, b = V("p%d%s" % (t, x), 0, n2), V("p%d%s" % (t + 1, x), 0, n2)
-                dma("s", u8(b) if x == "c" else ap(b), u8(a) if x == "c" else ap(a), [b], [a])
-            if 1 < t < R - 1:
-                store(t - 2)
-        if t:
-            def later(t2, b):
-                mm(b, 128, *rep(t2), *wnd)
-                sact(V("AQ%d" % t2), V(b, 80, 128), act.Square)
-                fill_in.append(lambda: scatter(V("Q%d" % t2), lp, V("AQ%d" % t2)))
-
-            def result(o):
-                mm("b%d" % (6 + o), 128, *tile(o), *wnd)
-                sact(V("YA", K * o, K * o + K), V("b%d" % (6 + o), 80, 128), act.Copy)
-
-                def put():
-                    scatter(V("Y", P * o, P * o + P), lp, V("YA", K * o, K * o + K))
-                    i = (t - 1) * O * P
-                    if t == R:
-                        dma("sa"[o], T.y[:, i + P * o:i + P * o + P], ap(V("Y", P * o, P * o + P)), [], [V("Y", P * o, P * o + P)])
-                    elif o == O - 1 and t >= R - 2:
-                        store(t - 1)
-                (at_end if t == R - 2 else fill_in).append(put)
-
-            if more:
-                fill_in.append(lambda: scatter(V("U"), lp, V("A")))
-                later(t + 1, "b1")
-            for o in range(O):
-                result(o)
-            for t2 in range(t + 2, R):
-                later(t2, "b%d" % (t2 - t))
-            if t < R:
-                tt(V("EP", 0, K), V("EK", 0, K), V("A"), op_.mult)
-                tt(V("EP", K + 1, 2 * K + 1), V("EK", K, 2 * K), V("A"), op_.mult)
-                ts(V("A2"), V("A"), TINY, None, op_.max)
-                vsum(V("vc", 0, 1), V("EP", 0, K + 1), op_.max)
-                vsum(V("vc", 1, 2), V("EP", K + 1, 2 * K + 2), op_.max)
-                for x in range(2):
-                    tt(V("ZA", K * x, K * x + K), V("A2"), V("FX", K * x, K * x + K), op_.mult)
-        else:
-            fill_in += [lambda: quant(V("wc"), V("ws"), V("wb")), lambda: qrep(2, 4), lambda: qrep(4, 6)]
-        if t < R:
-            v0, v1 = V("vc", 0, 1), V("vc", 1, 2)
-            f = float(RADIX)
-            if not t:
-                ts(c0hi, V("VZ", 128, 256), v0, f, op_.is_lt, op_.mult)
-                ts(c1lo, V("VZ", 0, 128), v1, f, op_.is_le, op_.mult)
-                tt(V("VZ", P, 2 * P), V("VZ", 0, P), V("F"), op_.mult)
-            ts(c0lo, V("VZ", 256, 384), v0, f, op_.is_lt, op_.mult)
-            if t:
-                ts(c0hi, V("VZ", 128, 256), v0, f, op_.is_lt, op_.mult)
-            asum(V("S", 0, 1), V("J"), V("C", 0, 256))
-            if t:
-                ts(c1lo, V("VZ", 0, 128), v1, f, op_.is_le, op_.mult)
-            ts(c1hi, V("VZ", 384, 512), v1, f, op_.is_lt, op_.mult)
-            asum(V("S", 1, 2), V("JS"), V("C", 354, 610))
-            if t:
-                ts(c0ar, V("ZA", 0, K), v0, f, op_.is_lt, op_.mult)
-                ts(c1ar, V("ZA", K, 2 * K), v1, f, op_.is_lt, op_.mult)
-                gap(more)
-            vsum(V("S", 3, 4), V("C", 256, 305))
-            vsum(V("S", 2, 3), V("C", 305, 354))
-            gap(not t)
-            ts(V("bc", 0, 32), V("zz"), V("S", 0, 1), V("S", 3, 4), op_.add, op_.add)
-            ts(V("bc", 32, 64), V("zz"), V("S", 1, 2), V("S", 2, 3), op_.add, op_.add)
-            turn(V("RC"), V("bc"))
-            for m in range(3):
-                ts(V("E", 65 * m, 65 * m + 64), V("RC"), V("lo", m, m + 1), V("hi", m, m + 1), op_.max, op_.min)
-                if m < 2:
-                    asum(V("Pm", m, m + 1), V("JE", 65 * m, 65 * m + 65), V("E", 65 * m, 65 * m + 65))
-            if more:
-                tt(D0, V("bc", 0, 64, s=32), sl, op_.subtract)
-            vsum(V("Pm", 2, 3), V("E", 130, 195))
-            for a in (0, 64):
-                tt(V("T1", 0, 3, a, a + 64), V("Pm", 0, 3, a, a + 64), V("Pm", 0, 3, 64 - a, 128 - a), op_.add)
-            if more:
-                ts(D1, D0, 1.0 / RADIX, float(W[t]), op_.mult, op_.add)
-                ts(D2, D0, float(RADIX * K), None, op_.is_ge)
-            for a in (0, 32, 64, 96):
-                b = a ^ 32
-                tt(V("T2", 0, 3, a, a + 32), V("T1", 0, 3, a, a + 32), V("T1", 0, 3, b, b + 32), op_.add)
-            if more:
-                tt(D3, sl, D1, op_.subtract)
-            lst = V("L%d" % t, 0, 3)
-            copy(lst, V("T2", 0, 3))
-            pick(V("o%dc" % t), V("o%ds" % t, 0, K), V("p%dc" % t), V("p%ds" % t, 0, W[t]), lst)
-            dst = T.cores[rank ^ PART[t]]
-            rid, pid, _e = topo.addr(dst)
-            engs = topo.engines(core, dst)[:NE]
-            n1 = W[t + 1] if more else 128
-            order("p", "sent", 0, [], [V("o%dc" % t), V("o%ds" % t)])
-            g.remote_dma_fused([
-                RemoteDMATransfer(dst_ids=[DstId(rid=rid, pnc=pid)], dma_engine_mask=sum(1 << e for e in es), remote_sem=T.sem["arr%d" % t], src=src, dst=out)
-                for es, src, out in (
-                    (engs[0::2], u8(V("o%dc" % t)), u8(V("p%dc" % (t + 1), n1 - K, n1))),
-                    (engs[1::2], ap(V("o%ds" % t)), ap(V("p%ds" % (t + 1), n1 - K, n1 + PAD))))], local_sem=T.sem["sent"])
-            new = V("PT", W[t], W[t] + K)
-            gather(new, V("PT", 0, W[t]), lst)
-            if t == 0:
-                mm("b1", P, *rep(1), *own)
-                sact(V("Q1"), V("b1", 0, P), act.Square)
-            gap(bool(t))
-            gather(V("G6"), new, V("du"))
-            if more:
-                tt(D3, D3, D2, op_.mult)
-            gap()
-            turn(V("T6"), V("G6"))
-            if more:
-                tt(V("U"), V("U"), V("Q%d" % (t + 1)), op_.add)
-                tt(sl, D1, D3, op_.add)
-            copy(V("LP%d" % t, 0, 3), V("T6", 0, 96, s=32))
-        if more:
-            gap()
-            scatter(V("U"), V("LP%d" % t, 0, 3), V("big"))
-            gap()
-            ts(V("VZ", 0, P), V("U"), TINY, None, op_.max)
-            for x in range(2):
-                ts(V("EK", K * x, K * x + K), new, V("pl", x, x + 1), None, op_.is_equal)
-                ts(V("FX", K * x, K * x + K), new, V("pl", x, x + 1), PRED, op_.is_ge, op_.max)
-            gather(V("OG"), V("VZ", 0, P), V("GL"))
-            tt(V("VZ", P, 2 * P), V("VZ", 0, P), V("F"), op_.mult)
-            turn(V("TC"), V("OG"))
-        gap(len(fill_in))
-        for put in at_end:
-            put()
+        k = 1 if t else 2
+        gap(k)
+        turn(V("RC"), V("BC", BW - 96))
+        gap(k)
+        for m in range(3):
+            ts(V("E", EW * m, EW * m + 96), V("RC"), col("lo", m), col("hi", m), op_.max, op_.min)
+            if m < 2:
+                asum(col("Pm", m), V("JE", EW * m, EW * m + EW), V("E", EW * m, EW * m + EW))
+        gap(k)
+        vsum(col("Pm", 2), V("E", 2 * EW))
+        gap()
         if t == 0:
-            for t2 in range(2, R):
-                b = "b%d" % t2
-                mm(b, P, *rep(t2), *own)
-                sact(V("Q%d" % t2), V(b, 0, P), act.Square)
+            mm("b2", *rep(1), *own)
+            sact(V("SQ", 0, P), V("b2", 0, P), act.Square)
+            sact(SR, V("SV", 0, P), act.Copy)
+            sact(V("DM"), V("M16", 0, 16), act.Copy, V("QL"))
+        for a in (0, 64):
+            tt(V("T1", 0, 3, a, a + 64), V("Pm", 0, 3, a, a + 64), V("Pm", 0, 3, 64 - a, 128 - a), op_.add)
+        for a in (0, 32, 64, 96):
+            b = a ^ 32
+            tt(V("T2", 0, 3, a, a + 32), V("T1", 0, 3, a, a + 32), V("T1", 0, 3, b, b + 32), op_.add)
+        gap()
+        lst = V("L%d" % t, 0, 3)
+        ts(lst, V("T2", 0, 3), 512.0, None, op_.mult)
+        gap()
+        pick(*pair("o%d" % t, 0, K), *pair("p%d" % t, 0, n), lst)
+        dst = T.cores[rank ^ PART[t]]
+        rid, pid, _e = topo.addr(dst)
+        engs = topo.engines(core, dst)[:NE]
+        n1 = W[t + 1] if more else 128
+        order("p", "sent", 0, [], [V("o%dc" % t), V("o%ds" % t)])
+        g.remote_dma_fused([
+            RemoteDMATransfer(dst_ids=[DstId(rid=rid, pnc=pid)], dma_engine_mask=sum(1 << e for e in es), remote_sem=T.sem["arr%d" % t], src=src, dst=out)
+            for es, src, out in (
+                (engs[0::2], u8(V("o%dc" % t)), u8(V("p%dc" % (t + 1), n1 - K, n1))),
+                (engs[1::2], ap(V("o%ds" % t)), ap(V("p%ds" % (t + 1), n1 - K, n1 + PAD))))], local_sem=T.sem["sent"])
+        new, lp = V("PT", n, n + K), V("LP%d" % t, 0, 3)
+        sact(new, V("PT", 0, n), act.Copy, lst)
+        gap(99)
+        if t:
+            ygather(t, 0)
+        if not more:
+            ygather(t, 1)
+            store(t - 1)
             for o in range(O):
-                b = "b%d" % (6 + o)
-                mm(b, P, *tile(o), *own)
-                sact(V("Y", P * o, P * o + P), V(b, 0, P), act.Copy)
+                gather(V("YL", P * o, P * o + P), V("ZP", W[R] * o, W[R] * o + n), V("LS"))
+        elif t:
+            tt(V("U"), V("SQ", 0, n), V("U"), op_.add, V("LS"))
+        else:
+            tt(V("U"), V("SQ", 0, n), V("U"), op_.add)
+        scan(V("D1"), V("DM", 0, K), new, 0.0, op_.add, op_.max)
         if more:
+            scan(V("D2"), V("DP"), V("PT", n, n + K + 2), 0.0, op_.add, op_.max)
+        ts(lp, V("D1", 15, K, s=16), col("pf", 3), 1.0 / UNIT, op_.subtract, op_.mult)
+        if more:
+            p2 = col("D2", K + 1)
+            sact(V("G2", 0, P), V("SV", 0, P), act.Sign, scale=-1.0, bias=p2)
+            sact(V("G2", P), new, act.Sign, scale=-1.0, bias=p2)
+            sact(V("G2"), V("G2"), act.Identity, scale=-STEP, bias=1.0)
+            ts(Z, V("U"), TINY, None, op_.max)
+            scatter(SR, lp, V("SV", n, n + K))
+            scatter(Z, lp, V("big"))
             for x in range(2):
-                ts(V("EP", 49 * x + K, 49 * x + K + 1), V("TC", 32 * x, 32 * x + 1), V("D", 4 + x, 5 + x), TINY, op_.mult, op_.max)
+                ts(V("G", K * x, K * x + K), new, col("pl", x), PRED, op_.is_lt, op_.max)
+            sact(V("OG"), V("ZS"), act.Copy, V("GL"))
+            if t:
+                ygather(t, 1)
+            tt(V("ZF"), Z, V("F"), op_.mult)
+            turn(V("TC"), V("OG"))
+            tt(V("RZ"), Z, V("G2", 0, P), op_.mult)
+            for x in range(2):
+                sact(V("CM", K * x, K * x + K), V("G", K * x, K * x + K), act.Copy, scale=col("TC", 32 * x))
+            compare("ZS", col("TC", 0), col("TC", 32))
+            if t == 0:
+                results(own, 0, P, lambda o: V("ZP", W[R] * o, W[R] * o + P))
+                qrep(4)
+                qrep(5)
+            else:
+                wait("s", "arr%d" % t, NE)
+                store(t - 1)
+
+    log["p6c"].append((0, 128, 128 - K, 128, 1, True, "net", "arr%d" % (R - 1), NE))
+    log["p6s"].append((0, 128, 128 - K, 128 + PAD, 1, True, "net", "arr%d" % (R - 1), NE))
+    results(pair("p6", 0, 128), 128 - K, 128, lambda o: V("YA", K * o, K * o + K))
+    for o in range(O):
+        y = V("YL", P * o, P * o + P)
+        scatter(y, V("LP%d" % (R - 1), 0, 3), V("YA", K * o, K * o + K))
+        i = (R - 1) * O * P + P * o
+        dma("sa"[o], T.y[:, i:i + P], ap(y), [], [y])
 
     for q in "vatp":
         wait("p", "s" + q, count[q])

@@ -9,34 +9,35 @@ STEP = 2.0 ** -24
 PRED = 1.0 - STEP
 TINY = 2.0 ** -122
 NIL = 2.0 ** -86
-UNIT = 2.0 ** -17
+UNIT = 1.0 / 512
 PAD = 3 * K
 ITEMS = 3 * 128
 XW = K + 64
-BW = 3 * XW // 2
+AW = K + 33
+BW = 3 * AW
 EW = 97
 
 F32, CODE, U8, U16, BF, I32 = "float32", "float8_e4m3fn_x4", "uint8", "uint16", "bfloat16", "int32"
 SCRATCH = {n: ("sbuf", [128, w], d) for n, w, d in (
     ("cb", 4 * P, BF), ("qb", 512, BF), ("wb", 512 * O, BF),
     ("qc", 128, CODE), ("qs", 128, U8), ("rc", 128 * R, CODE), ("rs", 128 * R, U8), ("wc", 128 * O, CODE), ("ws", 128 * O, U8),
-    ("IT", W[R], F32), ("SV", W[R], F32), ("PT", W[R] + 2, F32), ("F", P, F32), ("DM", 64, F32), ("DP", K + 2, F32),
-    ("pi", 4, I32), ("gi", 8, I32), ("pf", 4, F32), ("pn", 2, F32), ("pl", 2, F32), ("I17", 17, F32), ("M16", 32, F32),
-    ("li", 3, F32), ("lo", 3, F32), ("hi", 3, F32), ("bi", R, F32), ("bs", R, F32), ("big", K, F32),
-    ("GL", 8, U16), ("QL", 4, U16), ("qo", 8 * R, U16), ("LS", 16, U16),
-    ("U", P, F32), ("ZS", 2 * P, F32), ("ZF", P, F32), ("G2", P + K, F32), ("RZ", P, F32), ("SQ", W[R - 2], F32),
-    ("A", K, F32), ("A2", K, F32), ("Z2", K, F32), ("G", 2 * K, F32), ("CM", 2 * K, F32), ("v", 4, F32),
-    ("CS", 2 * P, F32), ("C2", P, F32), ("J", 3 * P, F32), ("JE", 2 * EW, F32), ("S", 4, F32), ("X", 3 * XW, F32), ("BC", BW, F32),
-    ("RC", 96, F32), ("E", 3 * EW, F32), ("Pm", 4, F32), ("T1", 4, F32), ("T2", 4, F32),
-    ("D1", K, F32), ("D2", K + 2, F32), ("DS", P, F32), ("OG", 128, F32), ("TC", 128, F32),
-    ("ZP", O * W[R], F32), ("Y", 2 * O * P, F32), ("YL", O * P, F32), ("YA", O * K, F32), ("p6c", 128, CODE), ("p6s", 128 + PAD, U8))}
+    ("IT", W[R], F32), ("SV", W[R], F32), ("PT", W[R], F32), ("F", P, F32), ("DM", K, F32), ("SH", 128, F32),
+    ("pi", 6, I32), ("qi", 8 * R, I32), ("gi", 12, I32), ("pf", 5, F32), ("pg", 3, F32), ("pn", 2, F32), ("pl", 2, F32),
+    ("I17", 17, F32), ("M16", 32, F32), ("li", 3, F32), ("lo", 3, F32), ("hi", 3, F32), ("bi", R, F32), ("bs", R, F32), ("big", 2 * K, F32),
+    ("GL", 12, U16), ("QL", 4, U16), ("PL", 2, U16), ("qo", 8 * R, U16),
+    ("Q", R * P, F32), ("AQ", 4 * K, F32), ("CU", 8 * K, F32), ("SR", P, F32), ("Z", 2 * P, F32), ("B", 2 * P, F32), ("OG", P, F32), ("TC", 128, F32),
+    ("G", 128 + 3 * K, F32), ("RZ", 128, F32), ("A", K, F32), ("A2", K, F32), ("Z2", K, F32), ("CM", 2 * K, F32), ("v", 2, F32),
+    ("p2", 16, F32), ("fl", 2, F32), ("zb", 4, F32), ("CS", 2 * P, F32), ("C2", 128, F32), ("X", 2 * XW, F32), ("X2", AW, F32),
+    ("J", 5 * 128, F32), ("JE", 2 * EW, F32), ("S", 2, F32), ("BC", BW, F32), ("RC", 96, F32), ("E", 3 * EW, F32),
+    ("Pm", 4, F32), ("T1", 4, F32), ("T2", 4, F32), ("D1", K, F32),
+    ("Y", O * P, F32), ("YL", O * P, F32), ("YA", O * K, F32), ("p6c", 128, CODE), ("p6s", 128 + PAD, U8))}
 for _t in range(R):
     for _n, _w, _d in (("p%dc", W[_t], CODE), ("p%ds", W[_t] + PAD, U8), ("o%dc", K, CODE), ("o%ds", K + PAD, U8),
-                       ("L%d", 4, U16), ("LP%d", 4, U16)):
+                       ("L%d", 4, U16), ("LP%d", 6, U16)):
         SCRATCH[_n % _t] = ("sbuf", [128, _w], _d)
 for _b in range(8):
     SCRATCH["b%d" % _b] = ("psum", [128, 512], F32)
-NDMA = 30
+NDMA = 38
 SEMAPHORES = ["sv", "sa", "st", "sp", "sent"] + ["arr%d" % t for t in range(R)] + ["d%d" % i for i in range(NDMA)]
 
 
@@ -57,6 +58,9 @@ def rank_program(g, core, T, topo):
 
     def col(n, c):
         return V(n, c, c + 1)
+
+    def run(n, c, w):
+        return V(n, c, c + w)
 
     def ap(v):
         if not isinstance(v, tuple):
@@ -87,8 +91,6 @@ def rank_program(g, core, T, topo):
                         continue
                     if not whole and not (w2 or wr):
                         continue
-                    if q2 == q and q != "s" and not w2:
-                        continue
                     need[sem2] = max(need.get(sem2, 0), val2)
         for s2 in sorted(need):
             wait(q, s2, need[s2])
@@ -105,11 +107,11 @@ def rank_program(g, core, T, topo):
         order(q, sem, count[q], writes, reads)
         fn().then_inc(T.sem[sem], 1)
 
-    def dma(q, out, in_, writes, reads):
+    def dma(q, out, in_, writes, reads, **k):
         sem = "d%d" % count["d"]
         count["d"] += 1
         order(q, sem, 16, writes, reads)
-        queues[q].dma_start(out, in_).then_inc(T.sem[sem], 16)
+        queues[q].dma_start(out, in_, **k).then_inc(T.sem[sem], 16)
 
     def ts(out, in0, s1, s2, o0, o1=None):
         r = views(in0, s1, s2)
@@ -118,15 +120,11 @@ def rank_program(g, core, T, topo):
         else:
             op("v", [out], r, lambda: g.vector.tensor_scalar(ap(out), ap(in0), ap(s1), ap(s2), o0, o1))
 
-    def tt(out, a, b, o, off=None):
-        op("v", [out], views(a, b, off), lambda: g.vector.tensor_tensor(ap(out), ap(a).indirect(ap(off)) if off else ap(a), ap(b), o))
+    def tt(out, a, b, o):
+        op("v", [out], [a, b], lambda: g.vector.tensor_tensor(ap(out), ap(a), ap(b), o))
 
-    def scan(out, a, b, first, o0, o1):
-        op("v", [out], views(a, b, first), lambda: g.vector.tensor_tensor_scan(ap(out), ap(a), ap(b), ap(first), o0, o1))
-
-    def total(out, a, first):
-        n, p0, p1, c0, c1, s = a
-        scan(out, V(n, c0, c1, s=2), V(n, c0 + 1, c1, s=2), first, op_.add, op_.add)
+    def scan(out, a, b, first, o):
+        op("v", [out], views(a, b, first), lambda: g.vector.tensor_tensor_scan(ap(out), ap(a), ap(b), ap(first), op_.add, o))
 
     def vsum(out, a):
         op("v", [out], [a], lambda: g.vector.tensor_reduce(ap(out), ap(a), AxisListType.X, op_.add))
@@ -150,8 +148,11 @@ def rank_program(g, core, T, topo):
         op("a", [out], views(a, off, *k.values()), lambda: g.scalar.activation(
             ap(out), ap(a).indirect(ap(off)) if off else ap(a), f, **{n: ap(x) for n, x in k.items()}))
 
-    def asum(out, junk, a, bias=0.0):
-        op("a", [out, junk], views(a, bias), lambda: g.scalar.activation(ap(junk), ap(a), act.Identity, bias=ap(bias), accum_out=ap(out)))
+    def affine(out, a, scale, bias):
+        sact(out, a, act.Identity, scale=scale, bias=bias)
+
+    def asum(out, junk, a):
+        op("a", [out, junk], [a], lambda: g.scalar.activation(ap(junk), ap(a), act.Copy, accum_out=ap(out)))
 
     def quant(c, s, a):
         op("v", [c, s], [a], lambda: g.vector.quantize_mx(ap(c), ap(s), ap(a)))
@@ -167,8 +168,8 @@ def rank_program(g, core, T, topo):
     def pair(n, a, b):
         return V(n + "c", a, b), V(n + "s", a, b)
 
-    def qrep(a):
-        pick(*rep(a), V("qc"), V("qs"), V("qo", 8 * a, 8 * a + 8))
+    def qrep(a, b):
+        pick(*pair("r", 128 * a, 128 * b), V("qc"), V("qs"), V("qo", 8 * a, 8 * b))
 
     def rep(t):
         return pair("r", 128 * t, 128 * t + 128)
@@ -180,105 +181,97 @@ def rank_program(g, core, T, topo):
         k = {} if SCRATCH[v[0]][2] == I32 else {"allow_small_or_imprecise_dtypes": True}
         op("p", [v], [], lambda: g.iota(ap(v), *pat, **k))
 
-    def select(v, pat, o, x, base, k):
-        op("p", [v], [v], lambda: g.affine_select(ap(v), ap(v), pat, o, x, base, k))
-
     def half(n, x):
         return V(n, 128 * x, 128 * x + 128)
 
-    def gap(k=1):
-        for _ in range(min(k, len(fill_in))):
-            fill_in.pop(0)()
-
-    Z, SR = V("ZS", 0, P), V("ZS", P, 2 * P)
-    q16 = col("pf", 2)
-
-    dma("a", ap(V("qb", 0, 4 * R)), T.qt[:, 0:4 * R], [V("qb", 0, 4 * R)], [])
-    for x in range(2):
-        dma("sa"[x], ap(V("cb", 512 * x, 512 * x + 512)), T.c[:, 512 * x:512 * x + 512], [V("cb", 512 * x, 512 * x + 512)], [])
-    fill(V("qb", 4 * R), 0.0)
-    fill(V("F"), PRED)
-    whole(V("IT"), [[1, W[R]]], 0, 0)
-    whole(V("pi", 0, 1), [[0, 1]], 0, 1)
-    whole(V("pn"), [[128, 2]], 0, 1)
-    select(V("F"), [[0, 2], [-1, 128]], op_.is_gt, 1.0, 0, 1)
-    whole(V("li"), [[16, 3]], 0, 0)
-    whole(V("I17"), [[1, 17]], -1, 0)
-    whole(V("gi"), [[256, 2], [128, 2], [16, 2]], 0, 0)
-    whole(V("bi"), [[K, R]], 128, 1)
-    for t in range(R):
-        fill(V("qo", 8 * t, 8 * t + 8), t)
-    fill(V("BC", BW - 96), float(ITEMS))
-    fill(V("X"), 0.0)
-    fill(V("DP"), 0.0)
-    fill(V("big"), 1e29)
-    fill(col("DP", K + 1), -1.0)
-    quant(V("qc"), V("qs"), V("qb"))
-    ts(V("big"), V("big"), 1e9, None, op_.mult)
-    sact(V("SV"), V("IT"), act.Copy, scale=UNIT)
-    qrep(0)
-    ts(col("pi", 1), col("pi", 0), 0x6F, None, op_.bitwise_and)
-    ts(col("pi", 2), col("pi", 0), 0x0F, None, op_.bitwise_and)
-    ts(V("pl"), V("pn"), UNIT, None, op_.mult)
-    sact(V("PT", 0, P), V("IT", 0, P), act.Copy, scale=UNIT)
-    sact(V("PT", P), V("IT", 0, W[R] + 2 - P), act.Copy, scale=0.0)
-    own = pair("p0", 0, P)
-    for x in range(2):
-        quant(*pair("p0", 128 * x, 128 * x + 128), V("cb", 512 * x, 512 * x + 512))
-    dma("s", ap(V("wb")), T.w[:], [V("wb")], [V("cb")])
-    select(V("DP"), [[1, K + 2]], op_.not_equal, -4.0, 128 - K, -1)
-    select(V("DP"), [[1, K + 2]], op_.not_equal, 1.0, 127 - K, -1)
-
-    fill_in = [
-        lambda: copy(V("pf", 1, 3), V("pi", 1, 3)),
-        lambda: qrep(1),
-        lambda: qrep(2),
-        lambda: ts(V("lo"), V("li"), q16, None, op_.add),
-        lambda: qrep(3),
-        lambda: ts(V("hi"), V("lo"), 511.0 / 512, None, op_.add),
-        lambda: ts(V("E", EW - 1, 3 * EW, s=EW), V("lo"), -(ITEMS - 511.0 / 512) / 4, -(ITEMS - 1) * 511.0 / 2048, op_.mult, op_.add),
-        lambda: ts(V("M16", 0, 16), V("I17", 1, 17), q16, -4.0, op_.is_equal, op_.mult),
-        lambda: ts(V("M16", 16, 32), V("I17", 0, 16), q16, None, op_.is_equal),
-        lambda: ts(V("QL"), V("I17", 0, 4), 0.0, q16, op_.mult, op_.add),
-        lambda: tt(V("M16", 0, 16), V("M16", 0, 16), V("M16", 16, 32), op_.add),
-        lambda: ts(V("GL"), V("gi"), col("pf", 1), None, op_.add),
-        lambda: ts(col("pf", 0), col("pn", 0), float(128 - K), None, op_.is_lt),
-        lambda: ts(col("pf", 3), q16, 15.0, None, op_.is_lt),
-        lambda: ts(V("bs"), V("bi"), UNIT, col("pf", 0), op_.mult, op_.max),
-        lambda: quant(*tile(0), V("wb", 0, 512)),
-        lambda: quant(*tile(1), V("wb", 512, 1024))]
-
-    def cs(x, h):
-        return V("CS", P * x + 128 * h, P * x + 128 * h + 128)
-
-    def xs(m, n=K):
-        return V("X", XW * m, XW * m + n)
-
     def store(t):
-        y = V("Y", t % 2 * O * P, (t % 2 + 1) * O * P)
-        dma("s", T.y[:, t * O * P:(t + 1) * O * P], ap(y), [], [y])
-
-    def ygather(t, o):
-        i = ((t - 1) % 2 * O + o) * P
-        sact(V("Y", i, i + P), V("ZP", W[R] * o, W[R] * o + W[t]), act.Copy, V("LS"))
+        dma("s", T.y[:, t * O * P:(t + 1) * O * P], ap(V("Y")), [], [V("Y")])
 
     def results(wnd, a, b, out):
         for o in range(O):
             mm("b%d" % (6 + o), *tile(o), *wnd)
             sact(out(o), V("b%d" % (6 + o), a, b), act.Copy)
 
-    def compare(rows, v0, v1):
-        ts(cs(0, 1), half(rows, 1), v0, None, op_.is_lt)
-        ts(cs(0, 0), half("ZF", 0), v0, None, op_.is_lt)
-        ts(cs(1, 0), half(rows, 0), v1, None, op_.is_le)
-        ts(cs(1, 1), half("ZF", 1), v1, None, op_.is_lt)
+    def use(t):
+        return run("Q", P * t, P)
 
-    def counts(*slots):
+    def came(t, a, k=1):
+        return run("CU", t % 2 * 4 * K + K * a, K * k)
+
+    def squares(t, w=P):
+        mm("b5", *rep(t), *pair("p0", 0, w))
+        sact(run("Q", P * t, w), V("b5", 0, w), act.Square)
+
+    def counts():
         for x in range(2):
-            asum(col("S", x), V("J", P * x, P * x + P), V("CS", P * x, P * x + P), slots[x])
+            asum(col("S", x), run("J", P * x, P), run("CS", P * x, P))
 
-    def diagonal(i):
-        scan(V("DS", 64 * i, 64 * i + 64), V("DM"), V("ZS", P + 64 * i, P + 64 * i + 64), 0.0, op_.add, op_.max)
+    def gap():
+        if fill_in:
+            fill_in.pop(0)()
+
+    def ahead(t):
+        def plain():
+            ts(run("Z", 0, P), use(t), TINY, None, op_.max)
+            sact(run("OG", 128, 64), run("Z", 0, P), act.Copy, V("GL", 8, 12))
+        return [plain] + [lambda x=x: tt(half("Z", 2 + x), half("Z", x), half("F", x), op_.mult) for x in range(2)] + [
+            lambda: turn(run("TC", 0, 64), run("OG", 128, 64))]
+
+    def nothing():
+        pass
+
+    q16, b32 = col("pf", 0), col("pf", 1)
+
+    dma("a", ap(V("qb", 0, 4 * R)), T.qt[:, 0:4 * R], [V("qb", 0, 4 * R)], [])
+    for x in range(2):
+        dma("sa"[x], ap(run("cb", 512 * x, 512)), T.c[:, 512 * x:512 * x + 512], [run("cb", 512 * x, 512)], [])
+    whole(col("pi", 0), [[0, 1]], 0, 1)
+    whole(V("qi"), [[1, R], [0, 8]], 0, 0)
+    whole(V("I17"), [[1, 17]], -1, 0)
+    whole(V("pn"), [[128, 2]], 0, 1)
+    whole(V("li"), [[16, 3]], 0, 0)
+    whole(V("gi", 0, 8), [[16, 8]], 0, 0)
+    whole(V("gi", 8, 12), [[128, 2], [16, 2]], 0, 0)
+    whole(V("bi"), [[K, R]], 128, 1)
+    fill(V("qb", 4 * R), 0.0)
+    fill(V("F"), PRED)
+    whole(V("IT"), [[1, W[R]]], 0, 0)
+    op("p", [V("F")], [V("F")], lambda: g.affine_select(ap(V("F")), ap(V("F")), [[0, 2], [-1, 128]], op_.is_gt, 1.0, 0, 1))
+    for i, bits in enumerate((0x0F, 0x60, 0x30, 0x4F, 0x40)):
+        ts(col("pi", 1 + i), col("pi", 0), bits, None, op_.bitwise_and)
+    copy(V("qo"), V("qi"))
+    fill(V("X"), 0.0)
+    copy(V("pf"), V("pi", 1, 6))
+    fill(V("BC", BW - 96), float(ITEMS))
+    fill(V("X2"), 0.0)
+    fill(V("big"), 1e29)
+    ts(V("M16", 0, 16), V("I17", 1, 17), q16, -4.0, op_.is_equal, op_.mult)
+    ts(V("M16", 16, 32), V("I17", 0, 16), q16, None, op_.is_equal)
+    ts(V("QL"), V("X", 0, 4), q16, None, op_.add)
+    ts(col("PL", 0), col("pf", 2), 1.0, 15.0, op_.subtract, op_.max)
+    ts(V("GL", 0, 8), V("gi", 0, 8), col("pf", 3), col("pf", 4), op_.add, op_.add)
+    ts(V("GL", 8, 12), V("gi", 8, 12), q16, b32, op_.add, op_.add)
+    tt(V("M16", 0, 16), V("M16", 0, 16), V("M16", 16, 32), op_.add)
+    affine(V("pl"), V("pn"), UNIT, 0.0)
+    affine(V("lo"), V("li"), 1.0, q16)
+    sact(col("pg", 2), col("pn", 0), act.Relu, scale=-float(ITEMS), bias=float(ITEMS * (128 - K)))
+    sact(col("pg", 0), q16, act.Sign, bias=-15.0)
+    affine(V("hi"), V("lo"), 1.0, 1.0 - UNIT)
+    affine(V("E", EW - 1, 3 * EW, s=EW), V("lo"), -(ITEMS - 1.0 + UNIT) / 4, -(ITEMS - 1) * (1.0 - UNIT) / 4)
+    affine(V("bs"), V("bi"), UNIT, col("pg", 2))
+    affine(col("pg", 1), col("pg", 0), 1.0, P * UNIT)
+    sact(V("big"), V("big"), act.Copy, scale=1e9)
+    quant(V("qc"), V("qs"), V("qb"))
+    qrep(0, 1)
+    sact(V("DM"), V("M16", 0, 16), act.Copy, V("QL", 0, 3))
+    sact(V("SV"), V("IT"), act.Copy, scale=UNIT)
+    own = pair("p0", 0, P)
+    for x in range(2):
+        quant(*pair("p0", 128 * x, 128 * x + 128), run("cb", 512 * x, 512))
+    dma("s", ap(V("wb")), T.w[:], [V("wb")], [V("cb")])
+    for q, a, b in [("s", V("o0s", K), V("p0s", 0, PAD)), ("p", V("PT", 0, P), V("SV", 0, P)), ("s", V("SR"), V("SV", 0, P))] + [
+            ("s", V("SH", p0=64 * x, p1=64 * x + 64), V("SV", 128 * x, 128 * x + 128, 64 * x, 64 * x + 64)) for x in range(2)]:
+        dma(q, ap(a), ap(b), [a], [b])
 
     for t in range(R):
         more = t + 1 < R
@@ -288,49 +281,81 @@ def rank_program(g, core, T, topo):
             for x in range(2):
                 mm("b%d" % (3 + x), *pair("p0", 128 * x, 128 * x + 128), V("qc"), V("qs"))
             for x in range(2):
-                sact(half("RZ", x), half("b0", x), act.Abs, bias=NIL)
-            gap(3)
+                sact(half("B", x), half("b0", x), act.Abs, bias=NIL)
+            qrep(1, 3)
             for x in range(2):
                 s0 = col("b%d" % (3 + x), 0)
-                ts(col("v", 2 + x), s0, -1.0, s0, op_.mult, op_.max)
-            tt(half("ZF", 0), half("RZ", 0), half("F", 0), op_.mult)
-            ts(V("v", 0, 2), V("v", 2, 4), NIL, None, op_.max)
-            tt(half("ZF", 1), half("RZ", 1), half("F", 1), op_.mult)
-            compare("RZ", col("v", 0), col("v", 1))
-            counts(col("pl", 0), col("pl", 1))
-            gap(5)
+                ts(col("v", x), s0, -1.0, s0, op_.mult, op_.max)
             for x in range(2):
-                ts(V("BC", BW - 96 + x, BW, s=3), V("X", K, K + 32), col("S", x), None, op_.add)
-            v = V("o0s", K, K + PAD)
-            dma("s", ap(v), ap(V("p0s", 0, PAD)), [v], [V("p0s", 0, PAD)])
-            sact(V("U"), V("b0", 0, P), act.Square)
+                tt(half("B", 2 + x), half("B", x), half("F", x), op_.mult)
+            ts(run("CS", 0, P), run("B", 128, P), NIL, col("v", 0), op_.subtract, op_.is_lt)
+            ts(half("CS", 2), half("B", 0), NIL, col("v", 1), op_.subtract, op_.is_le)
+            ts(half("CS", 3), half("B", 3), NIL, col("v", 1), op_.subtract, op_.is_lt)
+            sact(use(0), V("b0", 0, P), act.Square)
+            counts()
+            squares(1)
+            qrep(3, 5)
+            for x in range(2):
+                ts(V("BC", BW - 96 + x, BW, s=3), V("X", 64, 96), col("S", x), col("pl", x), op_.add, op_.add)
+            a = ahead(1)
+            fill_in = [lambda x=x: tt(half("Q", 2 + x), half("Q", 2 + x), half("Q", x), op_.add) for x in range(2)]
+            fill_in += [lambda: quant(V("wc"), V("ws"), V("wb")), a[0], nothing] + a[1:]
         else:
             log.setdefault("p%dc" % t, []).append((0, 128, n - K, n, 1, True, "net", "arr%d" % (t - 1), NE))
             log.setdefault("p%ds" % t, []).append((0, 128, n - K, n + PAD, 1, True, "net", "arr%d" % (t - 1), NE))
             wnd = pair("p%d" % t, n - 128, n)
-            mm("b0", *rep(t), *wnd)
+            lq = V("LP%d" % (t - 1), 0, 3)
             mm("b1", *wnd, V("qc"), V("qs"))
+            mm("b0", *rep(t), *wnd)
             sact(V("A"), V("b0", 128 - K, 128), act.Square)
-            counts(col("TC", 64), col("TC", 96))
-            s0, v0 = col("b1", t), col("v", 0)
-            ts(v0, s0, s0, TINY, op_.mult, op_.max)
-            ts(V("A2"), V("A"), TINY, None, op_.max)
-            ts(V("C2"), V("RZ"), v0, None, op_.is_lt)
-            asum(col("S", 2), V("J", 2 * P), V("C2"), col("bs", t))
-            results(wnd, 128 - K, 128, lambda o: V("ZP", W[R] * o + n - K, W[R] * o + n))
-            tt(V("Z2"), V("A2"), V("G2", P), op_.mult)
+            sact(V("A2"), V("b0", 128 - K, 128), act.Abs, bias=NIL)
+            if more:
+                mm("b2", *rep(t + 1), *wnd)
+                sact(run("AQ", 0, K), V("b2", 128 - K, 128), act.Square)
+            s0 = V("b1", t, t + 1, 64)
+            for a in (0, 64):
+                ts(V("v", 0, 1, a, a + 64), s0, s0, TINY, op_.mult, op_.max)
+            ts(V("fl"), V("TC", 64, s=32), W[t - 1] * UNIT, float(ITEMS), op_.is_ge, op_.mult)
+            carry[2]()
+            ts(V("v", 1, 2, 64), s0, -1.0, s0, op_.mult, op_.max)
+            ts(V("C2"), V("RZ"), col("v", 0), None, op_.is_lt)
+            results(wnd, 128 - K, 128, lambda o: run("YA", K * o, K))
+            asum(col("X2", K), half("J", 4), V("C2"))
+            tt(V("X", K, s=XW), V("TC", 64, s=32), V("fl"), op_.add)
+            tt(run("X", 0, K), V("A"), run("CM", 0, K), op_.is_le)
+            tt(V("Z2", p0=64), V("A2", p0=64), V("G", 128, 128 + K, 64), op_.mult)
+            tt(run("X", XW, K), V("A"), run("CM", K, K), op_.is_le)
+            ts(V("X2", 0, K, 64), V("Z2", p0=64), NIL, V("v", 1, 2, 64), op_.subtract, op_.is_lt)
+            if more:
+                tt(came(t + 1, t - 1), V("A"), run("AQ", 0, K), op_.add)
             for x in range(2):
-                tt(xs(x), V("A2"), V("CM", K * x, K * x + K), op_.is_le)
-            ts(xs(2), V("Z2"), v0, None, op_.is_lt)
-            for m in range(3):
-                total(V("BC", m, BW, s=3), xs(m, XW), col("S", m))
+                scan(V("BC", BW - 3 * XW // 2 + x, BW, s=3), V("X", XW * x, XW * x + XW, s=2), V("X", XW * x + 1, XW * x + XW, s=2), col("S", x), op_.add)
+                if x == 0:
+                    scan(V("BC", 2, BW, 64, s=3), V("X2", p0=64), V("X2", p1=64), V("bs", t, t + 1, 64), op_.add)
             if more:
-                fill_in.append(lambda: scatter(V("U"), V("LP%d" % (t - 1), 0, 3), V("A")))
-            fill_in += [lambda i=i: diagonal(i) for i in range(4)]
-            fill_in.append(lambda: ts(V("LS"), V("DS", 15, P, s=16), col("pf", 3), 1.0 / UNIT, op_.subtract, op_.mult))
+                scatter(use(t + 1), lq, came(t + 1, t - 1))
+            further = nothing
+            if t + 2 < R:
+                w = max(128, K * t)
+                mm("b3", *rep(t + 2), *pair("p%d" % t, n - w, n))
+                sact(run("AQ", K, K * t), V("b3", w - K * t, w), act.Square)
+                if t == 1:
+                    sact(run("Q", 3 * P + n - w, w - K), V("b3", 0, w - K), act.Square)
+                    squares(3, n - w)
+                dma("p", ap(use(t + 2)), ap(use(t + 1)), [use(t + 2)], [use(t + 1)], accum_op=op_.add)
+
+                def further():
+                    tt(came(t + 2, 0, t), came(t + 1, 0, t), run("AQ", K, K * t), op_.add)
+
+            def first():
+                scatter(run("Y", 0, P), lq, run("YA", 0, K))
+                if not more:
+                    dma("s", T.y[:, (t - 1) * O * P:(t - 1) * O * P + P], ap(run("Y", 0, P)), [], [run("Y", 0, P)])
             if more:
-                mm("b2", *rep(t + 1), *pair("p%d" % t, 0, n))
-                sact(V("SQ", 0, n), V("b2", 0, n), act.Square)
+                a = ahead(t + 1)
+                fill_in = [further, a[0], first, nothing, a[3], a[1], a[2]]
+            else:
+                fill_in = [nothing, nothing, first]
         n2 = n if more else 128 - K
         for x in "cs":
             a, b = V("p%d%s" % (t, x), 0, n2), V("p%d%s" % (t + 1, x), 0, n2)
@@ -339,30 +364,26 @@ def rank_program(g, core, T, topo):
             for t2 in range(1, R):
                 v = V("o%ds" % t2, K, K + PAD)
                 dma("s", ap(v), ap(V("p0s", 0, PAD)), [v], [V("p0s", 0, PAD)])
-        k = 1 if t else 2
-        gap(k)
         turn(V("RC"), V("BC", BW - 96))
-        gap(k)
+        gap()
         for m in range(3):
-            ts(V("E", EW * m, EW * m + 96), V("RC"), col("lo", m), col("hi", m), op_.max, op_.min)
+            ts(run("E", EW * m, 96), V("RC"), col("lo", m), col("hi", m), op_.max, op_.min)
             if m < 2:
-                asum(col("Pm", m), V("JE", EW * m, EW * m + EW), V("E", EW * m, EW * m + EW))
-        gap(k)
+                asum(col("Pm", m), run("JE", EW * m, EW), run("E", EW * m, EW))
+        gap()
         vsum(col("Pm", 2), V("E", 2 * EW))
         gap()
-        if t == 0:
-            mm("b2", *rep(1), *own)
-            sact(V("SQ", 0, P), V("b2", 0, P), act.Square)
-            sact(SR, V("SV", 0, P), act.Copy)
-            sact(V("DM"), V("M16", 0, 16), act.Copy, V("QL"))
+        if t in (1, 2):
+            squares(t + 3)
         for a in (0, 64):
             tt(V("T1", 0, 3, a, a + 64), V("Pm", 0, 3, a, a + 64), V("Pm", 0, 3, 64 - a, 128 - a), op_.add)
+        gap()
         for a in (0, 32, 64, 96):
             b = a ^ 32
             tt(V("T2", 0, 3, a, a + 32), V("T1", 0, 3, a, a + 32), V("T1", 0, 3, b, b + 32), op_.add)
         gap()
         lst = V("L%d" % t, 0, 3)
-        ts(lst, V("T2", 0, 3), 512.0, None, op_.mult)
+        ts(lst, V("T2", 0, 3), 1.0 / UNIT, None, op_.mult)
         gap()
         pick(*pair("o%d" % t, 0, K), *pair("p%d" % t, 0, n), lst)
         dst = T.cores[rank ^ PART[t]]
@@ -375,57 +396,64 @@ def rank_program(g, core, T, topo):
             for es, src, out in (
                 (engs[0::2], u8(V("o%dc" % t)), u8(V("p%dc" % (t + 1), n1 - K, n1))),
                 (engs[1::2], ap(V("o%ds" % t)), ap(V("p%ds" % (t + 1), n1 - K, n1 + PAD))))], local_sem=T.sem["sent"])
-        new, lp = V("PT", n, n + K), V("LP%d" % t, 0, 3)
-        sact(new, V("PT", 0, n), act.Copy, lst)
-        gap(99)
+        new, lp = run("PT", n, K), V("LP%d" % t, 0, 3)
+        gather(new, V("PT", 0, n), lst)
+        if t == 0:
+            squares(2)
+        gap()
+        scan(V("D1"), V("DM"), new, 0.0, op_.max)
         if t:
-            ygather(t, 0)
+            scatter(run("Y", P, P), lq, run("YA", K, K))
+        gap()
+        if more:
+            ts(V("zb", 0, 2), V("TC", 0, 64, s=32), TINY, -1.0 / STEP, op_.is_le, op_.mult)
+        for x in range(2 if more else 1):
+            ts(V("LP%d" % t, 3 * x, 3 * x + 3), V("D1", 15, s=16), col("pg", x), 1.0 / UNIT, op_.add, op_.mult)
         if not more:
-            ygather(t, 1)
-            store(t - 1)
-            for o in range(O):
-                gather(V("YL", P * o, P * o + P), V("ZP", W[R] * o, W[R] * o + n), V("LS"))
-        elif t:
-            tt(V("U"), V("SQ", 0, n), V("U"), op_.add, V("LS"))
+            copy(V("YL"), V("Y"))
+            wait("s", "sent", NE * R)
+            dma("s", T.y[:, t * O * P - P:t * O * P], ap(run("Y", P, P)), [], [run("Y", P, P)])
         else:
-            tt(V("U"), V("SQ", 0, n), V("U"), op_.add)
-        scan(V("D1"), V("DM", 0, K), new, 0.0, op_.add, op_.max)
-        if more:
-            scan(V("D2"), V("DP"), V("PT", n, n + K + 2), 0.0, op_.add, op_.max)
-        ts(lp, V("D1", 15, K, s=16), col("pf", 3), 1.0 / UNIT, op_.subtract, op_.mult)
-        if more:
-            p2 = col("D2", K + 1)
-            sact(V("G2", 0, P), V("SV", 0, P), act.Sign, scale=-1.0, bias=p2)
-            sact(V("G2", P), new, act.Sign, scale=-1.0, bias=p2)
-            sact(V("G2"), V("G2"), act.Identity, scale=-STEP, bias=1.0)
-            ts(Z, V("U"), TINY, None, op_.max)
-            scatter(SR, lp, V("SV", n, n + K))
-            scatter(Z, lp, V("big"))
-            for x in range(2):
-                ts(V("G", K * x, K * x + K), new, col("pl", x), PRED, op_.is_lt, op_.max)
-            sact(V("OG"), V("ZS"), act.Copy, V("GL"))
-            if t:
-                ygather(t, 1)
-            tt(V("ZF"), Z, V("F"), op_.mult)
-            turn(V("TC"), V("OG"))
-            tt(V("RZ"), Z, V("G2", 0, P), op_.mult)
-            for x in range(2):
-                sact(V("CM", K * x, K * x + K), V("G", K * x, K * x + K), act.Copy, scale=col("TC", 32 * x))
-            compare("ZS", col("TC", 0), col("TC", 32))
             if t == 0:
-                results(own, 0, P, lambda o: V("ZP", W[R] * o, W[R] * o + P))
-                qrep(4)
-                qrep(5)
-            else:
+                dma("p", ap(use(2)), ap(use(1)), [use(2)], [use(1)], accum_op=op_.add)
+            sact(V("p2"), V("D1"), act.Identity, V("PL", 0, 1), bias=col("pg", 0))
+            p2 = col("p2", 0)
+            for x in range(2):
+                ts(run("G", 128 + K + K * x, K), new, col("pl", x), PRED, op_.is_lt, op_.max)
+            tt(V("zb", 2, 4), V("TC", 0, 64, s=32), V("zb", 0, 2), op_.subtract)
+            if t == 1:
+                qrep(5, 6)
+            sact(half("G", 0), V("SH"), act.Sign, scale=-1.0, bias=p2)
+            scatter(V("Z"), V("LP%d" % t), V("big"))
+            scatter(V("SR"), lp, run("SV", n, K))
+            for x in range(2):
+                affine(run("CM", K * x, K), run("G", 128 + K + K * x, K), col("zb", 2 + x), col("zb", x))
+            affine(half("G", 0), half("G", 0), -STEP, 1.0)
+            sact(half("OG", 0), run("Z", 0, P), act.Copy, V("GL", 0, 8))
+            sact(run("OG", 192, 64), V("SR"), act.Copy, V("GL", 8, 12))
+            ts(run("CS", 0, P), run("Z", 128, P), col("TC", 0), None, op_.is_lt)
+            ts(half("CS", 2), half("Z", 0), col("TC", 32), None, op_.is_le)
+            ts(half("CS", 3), half("Z", 3), col("TC", 32), None, op_.is_lt)
+            counts()
+            ts(run("G", 128, K), new, p2, PRED, op_.is_ge, op_.max)
+            carry = [lambda a=a, t=t: scatter(use(t + 2), V("LP%d" % a, 0, 3), came(t + 2, a)) for a in range(t if t + 2 < R else 0)]
+            carry = [nothing] * (2 - len(carry)) + carry + [nothing]
+            carry[0]()
+            tt(V("RZ"), half("OG", 0), half("G", 0), op_.mult)
+            turn(run("TC", 64, 64), run("OG", 192, 64))
+            if t == 0:
+                results(own, 0, P, lambda o: run("Y", P * o, P))
+            carry[1]()
+            if t:
                 wait("s", "arr%d" % t, NE)
                 store(t - 1)
 
     log["p6c"].append((0, 128, 128 - K, 128, 1, True, "net", "arr%d" % (R - 1), NE))
     log["p6s"].append((0, 128, 128 - K, 128 + PAD, 1, True, "net", "arr%d" % (R - 1), NE))
-    results(pair("p6", 0, 128), 128 - K, 128, lambda o: V("YA", K * o, K * o + K))
+    results(pair("p6", 0, 128), 128 - K, 128, lambda o: run("YA", K * o, K))
     for o in range(O):
-        y = V("YL", P * o, P * o + P)
-        scatter(y, V("LP%d" % (R - 1), 0, 3), V("YA", K * o, K * o + K))
+        y = run("YL", P * o, P)
+        scatter(y, V("LP%d" % (R - 1), 0, 3), run("YA", K * o, K))
         i = (R - 1) * O * P + P * o
         dma("sa"[o], T.y[:, i:i + P], ap(y), [], [y])
 

@@ -14,7 +14,7 @@ PAD = 3 * K
 ITEMS = 3 * 128
 XW = K + 64
 AW = K + 33
-BW = 3 * AW
+BW = 3 * 160
 EW = 97
 
 F32, CODE, U8, U16, BF, I32 = "float32", "float8_e4m3fn_x4", "uint8", "uint16", "bfloat16", "int32"
@@ -27,9 +27,9 @@ SCRATCH = {n: ("sbuf", [128, w], d) for n, w, d in (
     ("GL", 12, U16), ("QL", 4, U16), ("PL", 2, U16), ("qo", 8 * R, U16),
     ("Q", R * P, F32), ("AQ", 4 * K, F32), ("CU", 8 * K, F32), ("SR", P, F32), ("Z", 2 * P, F32), ("B", 2 * P, F32), ("OG", P, F32), ("TC", 128, F32),
     ("G", 128 + 3 * K, F32), ("RZ", 128, F32), ("A", K, F32), ("A2", K, F32), ("Z2", K, F32), ("CM", 2 * K, F32), ("v", 2, F32),
-    ("p2", 16, F32), ("fl", 2, F32), ("zb", 4, F32), ("CS", 2 * P, F32), ("C2", 128, F32), ("X", 2 * XW, F32), ("X2", AW, F32),
+    ("p2", 16, F32), ("fl", 2, F32), ("zb", 4, F32), ("CS", 2 * P + 64, F32), ("C2", 128, F32), ("X", 2 * XW, F32), ("X2", AW, F32),
     ("J", 5 * 128, F32), ("JE", 2 * EW, F32), ("S", 2, F32), ("BC", BW, F32), ("RC", 96, F32), ("E", 3 * EW, F32),
-    ("Pm", 4, F32), ("T1", 4, F32), ("T2", 4, F32), ("D1", K, F32),
+    ("Pm", 4, F32), ("T1", 4, F32), ("D1", K, F32),
     ("Y", O * P, F32), ("YL", O * P, F32), ("YA", O * K, F32), ("p6c", 128, CODE), ("p6s", 128 + PAD, U8))}
 for _t in range(R):
     for _n, _w, _d in (("p%dc", W[_t], CODE), ("p%ds", W[_t] + PAD, U8), ("o%dc", K, CODE), ("o%ds", K + PAD, U8),
@@ -161,15 +161,17 @@ def rank_program(g, core, T, topo):
         out = V(bank, 0, rc[4] - rc[3])
         op("t", [out], [lc, ls, rc, rs], lambda: g.tensor.matmul_mx(ap(out), ap(lc), ap(ls), ap(rc), ap(rs), True, True))
 
-    def pick(oc, os, c, s, off):
-        op("v", [oc], [c, off], lambda: g.vector.tensor_copy(ap(oc).bitcast(dt.uint32), ap(c).bitcast(dt.uint32).indirect(ap(off))))
-        sact(os, s, act.Copy, off)
+    def pick(oc, os, c, s, off, on="va"):
+        if "v" in on:
+            op("v", [oc], [c, off], lambda: g.vector.tensor_copy(ap(oc).bitcast(dt.uint32), ap(c).bitcast(dt.uint32).indirect(ap(off))))
+        if "a" in on:
+            sact(os, s, act.Copy, off)
 
     def pair(n, a, b):
         return V(n + "c", a, b), V(n + "s", a, b)
 
-    def qrep(a, b):
-        pick(*pair("r", 128 * a, 128 * b), V("qc"), V("qs"), V("qo", 8 * a, 8 * b))
+    def qrep(a, b, on="va"):
+        pick(*pair("r", 128 * a, 128 * b), V("qc"), V("qs"), V("qo", 8 * a, 8 * b), on)
 
     def rep(t):
         return pair("r", 128 * t, 128 * t + 128)
@@ -202,9 +204,8 @@ def rank_program(g, core, T, topo):
         mm("b5", *rep(t), *pair("p0", 0, w))
         sact(run("Q", P * t, w), V("b5", 0, w), act.Square)
 
-    def counts():
-        for x in range(2):
-            asum(col("S", x), run("J", P * x, P), run("CS", P * x, P))
+    def counts(x):
+        asum(col("S", x), run("J", P * x, P), run("CS", P * x, P))
 
     def gap():
         if fill_in:
@@ -244,6 +245,7 @@ def rank_program(g, core, T, topo):
     copy(V("pf"), V("pi", 1, 6))
     fill(V("BC", BW - 96), float(ITEMS))
     fill(V("X2"), 0.0)
+    fill(V("CS", 2 * P), 0.0)
     fill(V("big"), 1e29)
     ts(V("M16", 0, 16), V("I17", 1, 17), q16, -4.0, op_.is_equal, op_.mult)
     ts(V("M16", 16, 32), V("I17", 0, 16), q16, None, op_.is_equal)
@@ -263,43 +265,42 @@ def rank_program(g, core, T, topo):
     sact(V("big"), V("big"), act.Copy, scale=1e9)
     quant(V("qc"), V("qs"), V("qb"))
     qrep(0, 1)
-    sact(V("DM"), V("M16", 0, 16), act.Copy, V("QL", 0, 3))
     sact(V("SV"), V("IT"), act.Copy, scale=UNIT)
     own = pair("p0", 0, P)
-    for x in range(2):
-        quant(*pair("p0", 128 * x, 128 * x + 128), run("cb", 512 * x, 512))
     dma("s", ap(V("wb")), T.w[:], [V("wb")], [V("cb")])
-    for q, a, b in [("s", V("o0s", K), V("p0s", 0, PAD)), ("p", V("PT", 0, P), V("SV", 0, P)), ("s", V("SR"), V("SV", 0, P))] + [
-            ("s", V("SH", p0=64 * x, p1=64 * x + 64), V("SV", 128 * x, 128 * x + 128, 64 * x, 64 * x + 64)) for x in range(2)]:
-        dma(q, ap(a), ap(b), [a], [b])
 
     for t in range(R):
         more = t + 1 < R
         n = W[t]
         if t == 0:
-            mm("b0", *rep(0), *own)
             for x in range(2):
-                mm("b%d" % (3 + x), *pair("p0", 128 * x, 128 * x + 128), V("qc"), V("qs"))
-            for x in range(2):
-                sact(half("B", x), half("b0", x), act.Abs, bias=NIL)
-            qrep(1, 3)
+                part = pair("p0", 128 * x, 128 * x + 128)
+                quant(*part, run("cb", 512 * x, 512))
+                mm("b%d" % x, *rep(0), *part)
+                mm("b%d" % (3 + x), *part, V("qc"), V("qs"))
+                sact(half("B", x), V("b%d" % x, 0, 128), act.Abs, bias=NIL)
+                if x == 0:
+                    qrep(1, 3, "v")
             for x in range(2):
                 s0 = col("b%d" % (3 + x), 0)
                 ts(col("v", x), s0, -1.0, s0, op_.mult, op_.max)
-            for x in range(2):
                 tt(half("B", 2 + x), half("B", x), half("F", x), op_.mult)
             ts(run("CS", 0, P), run("B", 128, P), NIL, col("v", 0), op_.subtract, op_.is_lt)
             ts(half("CS", 2), half("B", 0), NIL, col("v", 1), op_.subtract, op_.is_le)
             ts(half("CS", 3), half("B", 3), NIL, col("v", 1), op_.subtract, op_.is_lt)
-            sact(use(0), V("b0", 0, P), act.Square)
-            counts()
-            squares(1)
-            qrep(3, 5)
+            for q, a, b in [("s", V("o0s", K), V("p0s", 0, PAD)), ("p", V("PT", 0, P), V("SV", 0, P)), ("s", V("SR"), V("SV", 0, P))] + [
+                    ("s", V("SH", p0=64 * x, p1=64 * x + 64), V("SV", 128 * x, 128 * x + 128, 64 * x, 64 * x + 64)) for x in range(2)]:
+                dma(q, ap(a), ap(b), [a], [b])
             for x in range(2):
-                ts(V("BC", BW - 96 + x, BW, s=3), V("X", 64, 96), col("S", x), col("pl", x), op_.add, op_.add)
-            a = ahead(1)
+                sact(half("Q", x), V("b%d" % x, 0, 128), act.Square)
+            qrep(1, 3, "a")
+            counts(0)
+            squares(1)
+            sact(V("DM"), V("M16", 0, 16), act.Copy, V("QL", 0, 3))
+            scan(V("BC", 1, BW, s=3), V("CS", P, s=2), V("CS", P + 1, s=2), col("pl", 1), op_.add)
+            ts(V("BC", BW - 96, BW, s=3), V("X", 64, 96), col("S", 0), col("pl", 0), op_.add, op_.add)
             fill_in = [lambda x=x: tt(half("Q", 2 + x), half("Q", 2 + x), half("Q", x), op_.add) for x in range(2)]
-            fill_in += [lambda: quant(V("wc"), V("ws"), V("wb")), a[0], nothing] + a[1:]
+            fill_in += [lambda: quant(V("wc"), V("ws"), V("wb"))] + ahead(1)
         else:
             log.setdefault("p%dc" % t, []).append((0, 128, n - K, n, 1, True, "net", "arr%d" % (t - 1), NE))
             log.setdefault("p%ds" % t, []).append((0, 128, n - K, n + PAD, 1, True, "net", "arr%d" % (t - 1), NE))
@@ -307,33 +308,33 @@ def rank_program(g, core, T, topo):
             lq = V("LP%d" % (t - 1), 0, 3)
             mm("b1", *wnd, V("qc"), V("qs"))
             mm("b0", *rep(t), *wnd)
-            sact(V("A"), V("b0", 128 - K, 128), act.Square)
             sact(V("A2"), V("b0", 128 - K, 128), act.Abs, bias=NIL)
+            sact(V("A"), V("b0", 128 - K, 128), act.Square)
+            sact(V("fl"), V("TC", 64, s=32), act.Relu, scale=ITEMS * 2 / UNIT, bias=ITEMS * (1.0 - 2 * W[t - 1]))
+            counts(1)
             if more:
                 mm("b2", *rep(t + 1), *wnd)
                 sact(run("AQ", 0, K), V("b2", 128 - K, 128), act.Square)
             s0 = V("b1", t, t + 1, 64)
             for a in (0, 64):
                 ts(V("v", 0, 1, a, a + 64), s0, s0, TINY, op_.mult, op_.max)
-            ts(V("fl"), V("TC", 64, s=32), W[t - 1] * UNIT, float(ITEMS), op_.is_ge, op_.mult)
-            carry[2]()
             ts(V("v", 1, 2, 64), s0, -1.0, s0, op_.mult, op_.max)
+            carry[1]()
             ts(V("C2"), V("RZ"), col("v", 0), None, op_.is_lt)
-            results(wnd, 128 - K, 128, lambda o: run("YA", K * o, K))
+            for x in range(2):
+                affine(col("X", XW * x + K), col("TC", 64 + 32 * x), 1.0, col("fl", x))
             asum(col("X2", K), half("J", 4), V("C2"))
-            tt(V("X", K, s=XW), V("TC", 64, s=32), V("fl"), op_.add)
-            tt(run("X", 0, K), V("A"), run("CM", 0, K), op_.is_le)
+            results(wnd, 128 - K, 128, lambda o: run("YA", K * o, K))
             tt(V("Z2", p0=64), V("A2", p0=64), V("G", 128, 128 + K, 64), op_.mult)
-            tt(run("X", XW, K), V("A"), run("CM", K, K), op_.is_le)
+            for x in range(2):
+                tt(run("X", XW * x, K), V("A"), run("CM", K * x, K), op_.is_le)
             ts(V("X2", 0, K, 64), V("Z2", p0=64), NIL, V("v", 1, 2, 64), op_.subtract, op_.is_lt)
-            if more:
-                tt(came(t + 1, t - 1), V("A"), run("AQ", 0, K), op_.add)
             for x in range(2):
                 scan(V("BC", BW - 3 * XW // 2 + x, BW, s=3), V("X", XW * x, XW * x + XW, s=2), V("X", XW * x + 1, XW * x + XW, s=2), col("S", x), op_.add)
-                if x == 0:
-                    scan(V("BC", 2, BW, 64, s=3), V("X2", p0=64), V("X2", p1=64), V("bs", t, t + 1, 64), op_.add)
+            scan(V("BC", BW - 3 * AW + 2, BW, 64, s=3), V("X2", p0=64), V("X2", p1=64), V("bs", t, t + 1, 64), op_.add)
             if more:
-                scatter(use(t + 1), lq, came(t + 1, t - 1))
+                tt(came(t + 1, t - 1), V("A"), run("AQ", 0, K), op_.add)
+            carry[2]()
             further = nothing
             if t + 2 < R:
                 w = max(128, K * t)
@@ -342,10 +343,14 @@ def rank_program(g, core, T, topo):
                 if t == 1:
                     sact(run("Q", 3 * P + n - w, w - K), V("b3", 0, w - K), act.Square)
                     squares(3, n - w)
-                dma("p", ap(use(t + 2)), ap(use(t + 1)), [use(t + 2)], [use(t + 1)], accum_op=op_.add)
 
                 def further():
                     tt(came(t + 2, 0, t), came(t + 1, 0, t), run("AQ", K, K * t), op_.add)
+
+            def renew():
+                scatter(use(t + 1), lq, came(t + 1, t - 1))
+                if t + 2 < R:
+                    dma("p", ap(use(t + 2)), ap(use(t + 1)), [use(t + 2)], [use(t + 1)], accum_op=op_.add)
 
             def first():
                 scatter(run("Y", 0, P), lq, run("YA", 0, K))
@@ -353,9 +358,9 @@ def rank_program(g, core, T, topo):
                     dma("s", T.y[:, (t - 1) * O * P:(t - 1) * O * P + P], ap(run("Y", 0, P)), [], [run("Y", 0, P)])
             if more:
                 a = ahead(t + 1)
-                fill_in = [further, a[0], first, nothing, a[3], a[1], a[2]]
+                fill_in = [renew, a[0], further, a[1], a[2], lambda a=a: (a[3](), first())]
             else:
-                fill_in = [nothing, nothing, first]
+                fill_in = [nothing] * 5 + [first]
         n2 = n if more else 128 - K
         for x in "cs":
             a, b = V("p%d%s" % (t, x), 0, n2), V("p%d%s" % (t + 1, x), 0, n2)
@@ -375,15 +380,14 @@ def rank_program(g, core, T, topo):
         gap()
         if t in (1, 2):
             squares(t + 3)
-        for a in (0, 64):
-            tt(V("T1", 0, 3, a, a + 64), V("Pm", 0, 3, a, a + 64), V("Pm", 0, 3, 64 - a, 128 - a), op_.add)
-        gap()
         for a in (0, 32, 64, 96):
             b = a ^ 32
-            tt(V("T2", 0, 3, a, a + 32), V("T1", 0, 3, a, a + 32), V("T1", 0, 3, b, b + 32), op_.add)
+            tt(V("T1", 0, 3, a, a + 32), V("Pm", 0, 3, a, a + 32), V("Pm", 0, 3, b, b + 32), op_.add)
         gap()
         lst = V("L%d" % t, 0, 3)
-        ts(lst, V("T2", 0, 3), 1.0 / UNIT, None, op_.mult)
+        for a in (0, 64):
+            for m in range(3):
+                ts(V("L%d" % t, m, m + 1, a, a + 64), V("T1", m, m + 1, a, a + 64), V("T1", m, m + 1, 64 - a, 128 - a), 1.0 / UNIT, op_.add, op_.mult)
         gap()
         pick(*pair("o%d" % t, 0, K), *pair("p%d" % t, 0, n), lst)
         dst = T.cores[rank ^ PART[t]]
@@ -400,6 +404,7 @@ def rank_program(g, core, T, topo):
         gather(new, V("PT", 0, n), lst)
         if t == 0:
             squares(2)
+            qrep(3, 5)
         gap()
         scan(V("D1"), V("DM"), new, 0.0, op_.max)
         if t:
@@ -418,6 +423,8 @@ def rank_program(g, core, T, topo):
                 dma("p", ap(use(2)), ap(use(1)), [use(2)], [use(1)], accum_op=op_.add)
             sact(V("p2"), V("D1"), act.Identity, V("PL", 0, 1), bias=col("pg", 0))
             p2 = col("p2", 0)
+            if t == 0:
+                results(own, 0, P, lambda o: run("Y", P * o, P))
             for x in range(2):
                 ts(run("G", 128 + K + K * x, K), new, col("pl", x), PRED, op_.is_lt, op_.max)
             tt(V("zb", 2, 4), V("TC", 0, 64, s=32), V("zb", 0, 2), op_.subtract)
@@ -426,24 +433,21 @@ def rank_program(g, core, T, topo):
             sact(half("G", 0), V("SH"), act.Sign, scale=-1.0, bias=p2)
             scatter(V("Z"), V("LP%d" % t), V("big"))
             scatter(V("SR"), lp, run("SV", n, K))
-            for x in range(2):
-                affine(run("CM", K * x, K), run("G", 128 + K + K * x, K), col("zb", 2 + x), col("zb", x))
             affine(half("G", 0), half("G", 0), -STEP, 1.0)
             sact(half("OG", 0), run("Z", 0, P), act.Copy, V("GL", 0, 8))
             sact(run("OG", 192, 64), V("SR"), act.Copy, V("GL", 8, 12))
+            for x in range(2):
+                affine(run("CM", K * x, K), run("G", 128 + K + K * x, K), col("zb", 2 + x), col("zb", x))
             ts(run("CS", 0, P), run("Z", 128, P), col("TC", 0), None, op_.is_lt)
             ts(half("CS", 2), half("Z", 0), col("TC", 32), None, op_.is_le)
             ts(half("CS", 3), half("Z", 3), col("TC", 32), None, op_.is_lt)
-            counts()
+            counts(0)
             ts(run("G", 128, K), new, p2, PRED, op_.is_ge, op_.max)
             carry = [lambda a=a, t=t: scatter(use(t + 2), V("LP%d" % a, 0, 3), came(t + 2, a)) for a in range(t if t + 2 < R else 0)]
             carry = [nothing] * (2 - len(carry)) + carry + [nothing]
             carry[0]()
             tt(V("RZ"), half("OG", 0), half("G", 0), op_.mult)
             turn(run("TC", 64, 64), run("OG", 192, 64))
-            if t == 0:
-                results(own, 0, P, lambda o: run("Y", P * o, P))
-            carry[1]()
             if t:
                 wait("s", "arr%d" % t, NE)
                 store(t - 1)

@@ -10,34 +10,39 @@ PRED = 1.0 - STEP
 TINY = 2.0 ** -122
 NIL = 2.0 ** -86
 UNIT = 1.0 / 512
-PAD = 3 * K
+PAD = 0 * K
 ITEMS = 3 * 128
-XW = K + 64
-AW = K + 33
-BW = 3 * 160
+XW = K + 32
+OUT = 8.0
+AW = 128 + K + 31
+BW = 3 * 208
+QW = W[R - 2]
 EW = 97
+LIST = 1
+ROUND = 100
 
 F32, CODE, U8, U16, BF, I32 = "float32", "float8_e4m3fn_x4", "uint8", "uint16", "bfloat16", "int32"
 SCRATCH = {n: ("sbuf", [128, w], d) for n, w, d in (
     ("cb", 4 * P, BF), ("qb", 512, BF), ("wb", 512 * O, BF),
     ("qc", 128, CODE), ("qs", 128, U8), ("rc", 128 * R, CODE), ("rs", 128 * R, U8), ("wc", 128 * O, CODE), ("ws", 128 * O, U8),
-    ("IT", W[R], F32), ("SV", W[R], F32), ("PT", W[R], F32), ("F", P, F32), ("DM", K, F32), ("SH", 128, F32),
-    ("pi", 6, I32), ("qi", 8 * R, I32), ("gi", 12, I32), ("pf", 5, F32), ("pg", 3, F32), ("pn", 2, F32), ("pl", 2, F32),
-    ("I17", 17, F32), ("M16", 32, F32), ("li", 3, F32), ("lo", 3, F32), ("hi", 3, F32), ("bi", R, F32), ("bs", R, F32), ("big", 2 * K, F32),
+    ("IT", P, F32), ("SV", 4 * K, F32), ("ok", 2, F32), ("PT", W[R], F32), ("F", P, F32), ("TH", P, F32), ("DM", K, F32), ("SH", 128, F32),
+    ("pi", 6, I32), ("qi", 8 * R, I32), ("gi", 16, I32), ("pf", 5, F32), ("pg", 3, F32), ("pn", 2, F32), ("pl", 2, F32), ("pm", 2, F32),
+    ("I17", 17, F32), ("M16", 32, F32), ("li", 3, F32), ("lo", 3, F32), ("hi", 3, F32), ("bi", R, F32), ("bs", R, F32), ("ZL", 3 * K, F32),
     ("GL", 12, U16), ("QL", 4, U16), ("PL", 2, U16), ("qo", 8 * R, U16),
-    ("Q", R * P, F32), ("AQ", 4 * K, F32), ("CU", 8 * K, F32), ("SR", P, F32), ("Z", 2 * P, F32), ("B", 2 * P, F32), ("OG", P, F32), ("TC", 128, F32),
+    ("Q", R * QW, F32), ("AQ", K, F32), ("SR", P, F32), ("PU", W[R - 1], F32), ("SF", 16, F32), ("SO", 16, U16), ("GS", 4, U16),
+    ("B", P, F32), ("B0", 2 * P, F32), ("OG", P, F32), ("TC", 128, F32),
     ("G", 128 + 3 * K, F32), ("RZ", 128, F32), ("A", K, F32), ("A2", K, F32), ("Z2", K, F32), ("CM", 2 * K, F32), ("v", 2, F32),
-    ("p2", 16, F32), ("fl", 2, F32), ("zb", 4, F32), ("CS", 2 * P + 64, F32), ("C2", 128, F32), ("X", 2 * XW, F32), ("X2", AW, F32),
-    ("J", 5 * 128, F32), ("JE", 2 * EW, F32), ("S", 2, F32), ("BC", BW, F32), ("RC", 96, F32), ("E", 3 * EW, F32),
-    ("Pm", 4, F32), ("T1", 4, F32), ("D1", K, F32),
-    ("Y", O * P, F32), ("YL", O * P, F32), ("YA", O * K, F32), ("p6c", 128, CODE), ("p6s", 128 + PAD, U8))}
+    ("p2", 16, F32), ("zb", 4, F32), ("CS", 2 * P, F32), ("C0", 4 * 160, F32), ("SG", 2 * K, F32), ("X", 4 * XW, F32), ("X2", AW, F32),
+    ("J", 5 * 128, F32), ("JE", 3 * EW, F32), ("S", 2, F32), ("BC", BW, F32), ("RC", 96, F32), ("E", 3 * EW, F32),
+    ("T1", 4, F32), ("D1", 2 * K, F32),
+    ("Y0", O * P, F32), ("Y1", O * P, F32), ("YA", O * K, F32), ("p6c", 128, CODE), ("p6s", 128 + PAD, U8))}
 for _t in range(R):
     for _n, _w, _d in (("p%dc", W[_t], CODE), ("p%ds", W[_t] + PAD, U8), ("o%dc", K, CODE), ("o%ds", K + PAD, U8),
-                       ("L%d", 4, U16), ("LP%d", 6, U16)):
+                       ("L%d", 4, U16), ("LP%d", 8, U16)):
         SCRATCH[_n % _t] = ("sbuf", [128, _w], _d)
 for _b in range(8):
     SCRATCH["b%d" % _b] = ("psum", [128, 512], F32)
-NDMA = 38
+NDMA = 52
 SEMAPHORES = ["sv", "sa", "st", "sp", "sent"] + ["arr%d" % t for t in range(R)] + ["d%d" % i for i in range(NDMA)]
 
 
@@ -48,10 +53,13 @@ def rank_program(g, core, T, topo):
     op_ = AluOpType
     act = ActivationFunctionType
     queues = {"v": g.vector, "a": g.scalar, "t": g.tensor, "p": g, "s": g.sync}
-    count = {"v": 0, "a": 0, "t": 0, "p": 0, "d": 0}
-    seen = {}
+    calls = []
     log = {}
     psum = {"b%d" % b for b in range(8)}
+    now, lanes = [0, 0], []
+
+    def at(step, later=0):
+        now[1] = ROUND * (now[0] + later) + step
 
     def V(n, c0=0, c1=None, p0=0, p1=128, s=1):
         return (n, p0, p1, c0, SCRATCH[n][1][1] if c1 is None else c1, s)
@@ -74,397 +82,463 @@ def rank_program(g, core, T, topo):
     def views(*xs):
         return [x for x in xs if isinstance(x, tuple)]
 
-    def wait(q, sem, val):
-        if seen.get((q, sem), 0) < val:
-            seen[(q, sem)] = val
-            queues[q].wait_ge(T.sem[sem], val)
-
-    def order(q, sem, val, writes, reads):
-        need = {}
+    def call(q, writes, reads, fn, after=(), kind="op"):
+        need = set(after)
         for vs, wr in ((reads, False), (writes, True)):
             for n, p0, p1, c0, c1, s in vs:
                 whole = n in psum
-                for a0, a1, b0, b1, s2, w2, q2, sem2, val2 in log.get(n, ()):
+                for a0, a1, b0, b1, s2, w2, q2, j in log.get(n, ()):
                     if not whole and (a1 <= p0 or p1 <= a0 or b1 <= c0 or c1 <= b0 or (s == s2 and (c0 - b0) % s)):
                         continue
-                    if whole and q2 == q and not (w2 and not wr):
-                        continue
-                    if not whole and not (w2 or wr):
-                        continue
-                    need[sem2] = max(need.get(sem2, 0), val2)
-        for s2 in sorted(need):
-            wait(q, s2, need[s2])
+                    if w2 or wr or whole and q2 != q:
+                        need.add(j)
         for vs, wr in ((reads, False), (writes, True)):
             for n, p0, p1, c0, c1, s in vs:
                 old = log.setdefault(n, [])
                 if wr and s == 1:
                     old[:] = [e for e in old if not (p0 <= e[0] and e[1] <= p1 and c0 <= e[2] and e[3] <= c1)]
-                old.append((p0, p1, c0, c1, s, wr, q, sem, val))
+                old.append((p0, p1, c0, c1, s, wr, q, len(calls)))
+        calls.append((now[1], q, fn, sorted(need), kind))
+        return len(calls) - 1
 
-    def op(q, writes, reads, fn):
-        count[q] += 1
-        sem = "s" + q
-        order(q, sem, count[q], writes, reads)
-        fn().then_inc(T.sem[sem], 1)
-
-    def dma(q, out, in_, writes, reads, **k):
-        sem = "d%d" % count["d"]
-        count["d"] += 1
-        order(q, sem, 16, writes, reads)
-        queues[q].dma_start(out, in_, **k).then_inc(T.sem[sem], 16)
+    def dma(q, out, in_, writes, reads, after=(), **k):
+        return call(q, writes, reads, lambda: queues[q].dma_start(out, in_, **k), after, "dma")
 
     def ts(out, in0, s1, s2, o0, o1=None):
-        r = views(in0, s1, s2)
-        if o1 is None:
-            op("v", [out], r, lambda: g.vector.tensor_scalar(ap(out), ap(in0), ap(s1), None, o0))
-        else:
-            op("v", [out], r, lambda: g.vector.tensor_scalar(ap(out), ap(in0), ap(s1), ap(s2), o0, o1))
+        more = () if o1 is None else (o1,)
+        call("v", [out], views(in0, s1, s2), lambda: g.vector.tensor_scalar(ap(out), ap(in0), ap(s1), ap(s2), o0, *more))
 
     def tt(out, a, b, o):
-        op("v", [out], [a, b], lambda: g.vector.tensor_tensor(ap(out), ap(a), ap(b), o))
+        call("v", [out], [a, b], lambda: g.vector.tensor_tensor(ap(out), ap(a), ap(b), o))
 
     def scan(out, a, b, first, o):
-        op("v", [out], views(a, b, first), lambda: g.vector.tensor_tensor_scan(ap(out), ap(a), ap(b), ap(first), op_.add, o))
+        call("v", [out], views(a, b, first), lambda: g.vector.tensor_tensor_scan(ap(out), ap(a), ap(b), ap(first), op_.add, o))
 
     def vsum(out, a):
-        op("v", [out], [a], lambda: g.vector.tensor_reduce(ap(out), ap(a), AxisListType.X, op_.add))
+        call("v", [out], [a], lambda: g.vector.tensor_reduce(ap(out), ap(a), AxisListType.X, op_.add))
 
     def copy(out, a):
-        op("v", [out], [a], lambda: g.vector.tensor_copy(ap(out), ap(a)))
+        call("v", [out], [a], lambda: g.vector.tensor_copy(ap(out), ap(a)))
 
     def gather(out, win, off):
-        op("v", [out], [win, off], lambda: g.vector.tensor_copy(ap(out), ap(win).indirect(ap(off))))
+        call("v", [out], [win, off], lambda: g.vector.tensor_copy(ap(out), ap(win).indirect(ap(off))))
 
     def scatter(win, off, a):
-        op("v", [win], [a, off], lambda: g.vector.tensor_copy(ap(win).indirect(ap(off)), ap(a)))
+        call("v", [win], [a, off], lambda: g.vector.tensor_copy(ap(win).indirect(ap(off)), ap(a)))
 
     def turn(out, a):
-        op("v", [out], [a], lambda: g.vector.transpose(ap(out), ap(a)))
+        call("v", [out], [a], lambda: g.vector.transpose(ap(out), ap(a)))
 
     def fill(v, x):
-        op("v", [v], [], lambda: g.vector.memset(ap(v), x))
+        call("v", [v], [], lambda: g.vector.memset(ap(v), x))
 
     def sact(out, a, f, off=None, **k):
-        op("a", [out], views(a, off, *k.values()), lambda: g.scalar.activation(
+        call("a", [out], views(a, off, *k.values()), lambda: g.scalar.activation(
             ap(out), ap(a).indirect(ap(off)) if off else ap(a), f, **{n: ap(x) for n, x in k.items()}))
 
     def affine(out, a, scale, bias):
         sact(out, a, act.Identity, scale=scale, bias=bias)
 
-    def asum(out, junk, a):
-        op("a", [out, junk], [a], lambda: g.scalar.activation(ap(junk), ap(a), act.Copy, accum_out=ap(out)))
+    def asum(out, junk, a, f=act.Copy, **k):
+        call("a", [out, junk], [a], lambda: g.scalar.activation(ap(junk), ap(a), f, accum_out=ap(out), **k))
 
     def quant(c, s, a):
-        op("v", [c, s], [a], lambda: g.vector.quantize_mx(ap(c), ap(s), ap(a)))
+        call("v", [c, s], [a], lambda: g.vector.quantize_mx(ap(c), ap(s), ap(a)))
 
     def mm(bank, lc, ls, rc, rs):
         out = V(bank, 0, rc[4] - rc[3])
-        op("t", [out], [lc, ls, rc, rs], lambda: g.tensor.matmul_mx(ap(out), ap(lc), ap(ls), ap(rc), ap(rs), True, True))
+        call("t", [out], [lc, ls, rc, rs], lambda: g.tensor.matmul_mx(ap(out), ap(lc), ap(ls), ap(rc), ap(rs), True, True))
 
-    def pick(oc, os, c, s, off, on="va"):
-        if "v" in on:
-            op("v", [oc], [c, off], lambda: g.vector.tensor_copy(ap(oc).bitcast(dt.uint32), ap(c).bitcast(dt.uint32).indirect(ap(off))))
-        if "a" in on:
-            sact(os, s, act.Copy, off)
+    def pick(oc, os, c, s, off, then=None):
+        call("v", [oc], [c, off], lambda: g.vector.tensor_copy(ap(oc).bitcast(dt.uint32), ap(c).bitcast(dt.uint32).indirect(ap(off))))
+        if then is not None:
+            at(then)
+        sact(os, s, act.Copy, off)
 
     def pair(n, a, b):
         return V(n + "c", a, b), V(n + "s", a, b)
 
-    def qrep(a, b, on="va"):
-        pick(*pair("r", 128 * a, 128 * b), V("qc"), V("qs"), V("qo", 8 * a, 8 * b), on)
-
     def rep(t):
         return pair("r", 128 * t, 128 * t + 128)
+
+    def qrep(t, then=None):
+        pick(*rep(t), V("qc"), V("qs"), V("qo", 8 * t, 8 * t + 8), then)
 
     def tile(o):
         return pair("w", 128 * o, 128 * o + 128)
 
     def whole(v, *pat):
         k = {} if SCRATCH[v[0]][2] == I32 else {"allow_small_or_imprecise_dtypes": True}
-        op("p", [v], [], lambda: g.iota(ap(v), *pat, **k))
+        call("p", [v], [], lambda: g.iota(ap(v), *pat, **k))
+
+    def slope(x, o, s):
+        call("p", [half("F", x)], [half("F", x)], lambda: g.affine_select(ap(half("F", x)), ap(half("F", x)), [[-s, 128]], o, 1.0, 0, s))
 
     def half(n, x):
         return V(n, 128 * x, 128 * x + 128)
-
-    def store(t):
-        dma("s", T.y[:, t * O * P:(t + 1) * O * P], ap(V("Y")), [], [V("Y")])
 
     def results(wnd, a, b, out):
         for o in range(O):
             mm("b%d" % (6 + o), *tile(o), *wnd)
             sact(out(o), V("b%d" % (6 + o), a, b), act.Copy)
 
-    def use(t):
-        return run("Q", P * t, P)
+    def use(t, w=P):
+        return run("Q", QW * t, w)
 
     def came(t, a, k=1):
-        return run("CU", t % 2 * 4 * K + K * a, K * k)
+        return run("Q", QW * t + P + K * a, K * k)
+
+    def add_to(out, a, after=()):
+        dma("p", ap(out), ap(a), [out], [a], after, accum_op=op_.add)
 
     def squares(t, w=P):
         mm("b5", *rep(t), *pair("p0", 0, w))
-        sact(run("Q", P * t, w), V("b5", 0, w), act.Square)
+        sact(use(t, w), V("b5", 0, w), act.Square)
 
-    def counts(x):
-        asum(col("S", x), run("J", P * x, P), run("CS", P * x, P))
+    def block(t, o):
+        return run("Y%d" % (t == R - 2), P * o, P)
 
-    def gap():
-        if fill_in:
-            fill_in.pop(0)()
+    def store(t, o, q, after=()):
+        i = (t * O + o) * P
+        dma(q, T.y[:, i:i + P], ap(block(t, o)), [], [block(t, o)], after)
 
-    def ahead(t):
-        def plain():
-            ts(run("Z", 0, P), use(t), TINY, None, op_.max)
-            sact(run("OG", 128, 64), run("Z", 0, P), act.Copy, V("GL", 8, 12))
-        return [plain] + [lambda x=x: tt(half("Z", 2 + x), half("Z", x), half("F", x), op_.mult) for x in range(2)] + [
-            lambda: turn(run("TC", 0, 64), run("OG", 128, 64))]
+    q16, b32, p2 = col("pf", 0), col("pf", 1), col("p2", 0)
 
-    def nothing():
-        pass
-
-    q16, b32 = col("pf", 0), col("pf", 1)
-
+    at(-90)
     dma("a", ap(V("qb", 0, 4 * R)), T.qt[:, 0:4 * R], [V("qb", 0, 4 * R)], [])
     for x in range(2):
         dma("sa"[x], ap(run("cb", 512 * x, 512)), T.c[:, 512 * x:512 * x + 512], [run("cb", 512 * x, 512)], [])
-    whole(col("pi", 0), [[0, 1]], 0, 1)
+    dma("s", ap(V("wb")), T.w[:], [V("wb")], [V("cb")])
+    fill(V("F"), PRED)
+    fill(V("qb", 4 * R), 0.0)
     whole(V("qi"), [[1, R], [0, 8]], 0, 0)
-    whole(V("I17"), [[1, 17]], -1, 0)
+    whole(col("pi", 0), [[0, 1]], 0, 1)
     whole(V("pn"), [[128, 2]], 0, 1)
     whole(V("li"), [[16, 3]], 0, 0)
-    whole(V("gi", 0, 8), [[16, 8]], 0, 0)
+    whole(V("I17"), [[1, 17]], -1, 0)
     whole(V("gi", 8, 12), [[128, 2], [16, 2]], 0, 0)
-    whole(V("bi"), [[K, R]], 128, 1)
-    fill(V("qb", 4 * R), 0.0)
-    fill(V("F"), PRED)
-    whole(V("IT"), [[1, W[R]]], 0, 0)
-    op("p", [V("F")], [V("F")], lambda: g.affine_select(ap(V("F")), ap(V("F")), [[0, 2], [-1, 128]], op_.is_gt, 1.0, 0, 1))
+    slope(0, op_.is_gt, 1)
+    whole(V("gi", 0, 8), [[16, 8]], 0, 0)
+    whole(V("gi", 12, 16), [[8, 2], [1, 2]], 0, 0)
+    whole(V("bi"), [[K, R]], 128 - K * 512, 1)
+    whole(V("IT"), [[1, P]], 0, 0)
+    whole(V("PU", 0, P), [[1, 16], [16, 16]], 0, 0)
+    slope(1, op_.is_ge, -1)
+    copy(V("qo"), V("qi"))
     for i, bits in enumerate((0x0F, 0x60, 0x30, 0x4F, 0x40)):
         ts(col("pi", 1 + i), col("pi", 0), bits, None, op_.bitwise_and)
-    copy(V("qo"), V("qi"))
-    fill(V("X"), 0.0)
+    for c in range(4):
+        fill(run("C0", 160 * c + 128, 32), 0.0)
     copy(V("pf"), V("pi", 1, 6))
+    fill(V("X"), 0.0)
+    quant(V("qc"), V("qs"), V("qb"))
     fill(V("BC", BW - 96), float(ITEMS))
-    fill(V("X2"), 0.0)
-    fill(V("CS", 2 * P), 0.0)
-    fill(V("big"), 1e29)
-    ts(V("M16", 0, 16), V("I17", 1, 17), q16, -4.0, op_.is_equal, op_.mult)
-    ts(V("M16", 16, 32), V("I17", 0, 16), q16, None, op_.is_equal)
-    ts(V("QL"), V("X", 0, 4), q16, None, op_.add)
-    ts(col("PL", 0), col("pf", 2), 1.0, 15.0, op_.subtract, op_.max)
-    ts(V("GL", 0, 8), V("gi", 0, 8), col("pf", 3), col("pf", 4), op_.add, op_.add)
-    ts(V("GL", 8, 12), V("gi", 8, 12), q16, b32, op_.add, op_.add)
-    tt(V("M16", 0, 16), V("M16", 0, 16), V("M16", 16, 32), op_.add)
+    fill(V("X2", 128 + K), 0.0)
+    ts(col("pg", 0), q16, 15.0, -float(P), op_.is_lt, op_.mult)
+    qrep(0)
     affine(V("pl"), V("pn"), UNIT, 0.0)
     affine(V("lo"), V("li"), 1.0, q16)
+    affine(V("pm"), V("pn"), -1.0, 0.0)
+    affine(col("pg", 1), b32, 1.0 / 16, 0.0)
     sact(col("pg", 2), col("pn", 0), act.Relu, scale=-float(ITEMS), bias=float(ITEMS * (128 - K)))
-    sact(col("pg", 0), q16, act.Sign, bias=-15.0)
+    at(-76)
     affine(V("hi"), V("lo"), 1.0, 1.0 - UNIT)
     affine(V("E", EW - 1, 3 * EW, s=EW), V("lo"), -(ITEMS - 1.0 + UNIT) / 4, -(ITEMS - 1) * (1.0 - UNIT) / 4)
+    affine(col("pg", 1), q16, 16.0, col("pg", 1))
+    at(-79)
+    qrep(1)
+    at(-69)
+    ts(V("M16", 0, 16), V("I17", 1, 17), q16, -4.0 * P, op_.is_equal, op_.mult)
+    ts(V("M16", 16, 32), V("I17", 0, 16), q16, float(P), op_.is_equal, op_.mult)
+    ts(V("QL"), run("C0", 128, 4), q16, None, op_.add)
+    ts(V("GL", 8, 12), V("gi", 8, 12), q16, b32, op_.add, op_.add)
+    at(25.5)
+    tt(V("M16", 0, 16), V("M16", 0, 16), V("M16", 16, 32), op_.add)
+    ts(col("PL", 0), col("pf", 2), 1.0, 15.0, op_.subtract, op_.max)
+    at(30)
+    sact(V("DM"), V("M16", 0, 16), act.Copy, V("QL", 0, 3))
+    at(-59)
+    ts(V("GL", 0, 8), V("gi", 0, 8), col("pf", 3), col("pf", 4), op_.add, op_.add)
+    at(-40)
     affine(V("bs"), V("bi"), UNIT, col("pg", 2))
-    affine(col("pg", 1), col("pg", 0), 1.0, P * UNIT)
-    sact(V("big"), V("big"), act.Copy, scale=1e9)
-    quant(V("qc"), V("qs"), V("qb"))
-    qrep(0, 1)
-    sact(V("SV"), V("IT"), act.Copy, scale=UNIT)
+    affine(V("ok"), V("pn"), 0.0, OUT * OUT * K)
+    affine(V("SV"), run("IT", 0, 4 * K), UNIT, P * UNIT)
+    sact(V("SR"), V("PU", 0, P), act.Copy, scale=UNIT)
+    for q, a, b in [("p", V("PT", 0, P), V("IT", 0, P))] + [
+            ("s", V("SH", p0=64 * x, p1=64 * x + 64), V("IT", 128 * x, 128 * x + 128, 64 * x, 64 * x + 64)) for x in range(2)]:
+        dma(q, ap(a), ap(b), [a], [b])
     own = pair("p0", 0, P)
-    dma("s", ap(V("wb")), T.w[:], [V("wb")], [V("cb")])
+    arrival = None
 
     for t in range(R):
+        now[0] = t
         more = t + 1 < R
         n = W[t]
         if t == 0:
             for x in range(2):
                 part = pair("p0", 128 * x, 128 * x + 128)
+                at(-80 + 10 * x)
                 quant(*part, run("cb", 512 * x, 512))
                 mm("b%d" % x, *rep(0), *part)
                 mm("b%d" % (3 + x), *part, V("qc"), V("qs"))
-                sact(half("B", x), V("b%d" % x, 0, 128), act.Abs, bias=NIL)
-                if x == 0:
-                    qrep(1, 3, "v")
-            for x in range(2):
+                at(-75 + 10 * x)
+                sact(half("B0", x), V("b%d" % x, 0, 128), act.Abs, bias=NIL)
+                at(-60 + 10 * x)
                 s0 = col("b%d" % (3 + x), 0)
                 ts(col("v", x), s0, -1.0, s0, op_.mult, op_.max)
-                tt(half("B", 2 + x), half("B", x), half("F", x), op_.mult)
-            ts(run("CS", 0, P), run("B", 128, P), NIL, col("v", 0), op_.subtract, op_.is_lt)
-            ts(half("CS", 2), half("B", 0), NIL, col("v", 1), op_.subtract, op_.is_le)
-            ts(half("CS", 3), half("B", 3), NIL, col("v", 1), op_.subtract, op_.is_lt)
-            for q, a, b in [("s", V("o0s", K), V("p0s", 0, PAD)), ("p", V("PT", 0, P), V("SV", 0, P)), ("s", V("SR"), V("SV", 0, P))] + [
-                    ("s", V("SH", p0=64 * x, p1=64 * x + 64), V("SV", 128 * x, 128 * x + 128, 64 * x, 64 * x + 64)) for x in range(2)]:
-                dma(q, ap(a), ap(b), [a], [b])
-            for x in range(2):
+                tt(half("B0", 2 + x), half("B0", x), half("F", 0), op_.mult)
                 sact(half("Q", x), V("b%d" % x, 0, 128), act.Square)
-            qrep(1, 3, "a")
-            counts(0)
+            for c, b, x, o, step in ((0, 2, 0, op_.is_lt, -45), (1, 1, 0, op_.is_lt, -45), (2, 0, 1, op_.is_le, -44), (3, 3, 1, op_.is_lt, -44)):
+                at(step)
+                ts(run("C0", 160 * c, 128), half("B0", b), NIL, col("v", x), op_.subtract, o)
+            at(14)
+            for x in range(2):
+                scan(V("BC", BW - 480 + x, BW, s=3), run("C0", 320 * x, 160), run("C0", 320 * x + 160, 160), col("pl", x), op_.add)
+            at(-48)
+            for t2 in range(R if PAD else 0):
+                v = V("o%ds" % t2, K, K + PAD)
+                dma("s", ap(v), ap(V("p0s", 0, PAD)), [v], [V("p0s", 0, PAD)])
             squares(1)
-            sact(V("DM"), V("M16", 0, 16), act.Copy, V("QL", 0, 3))
-            scan(V("BC", 1, BW, s=3), V("CS", P, s=2), V("CS", P + 1, s=2), col("pl", 1), op_.add)
-            ts(V("BC", BW - 96, BW, s=3), V("X", 64, 96), col("S", 0), col("pl", 0), op_.add, op_.add)
-            fill_in = [lambda x=x: tt(half("Q", 2 + x), half("Q", 2 + x), half("Q", x), op_.add) for x in range(2)]
-            fill_in += [lambda: quant(V("wc"), V("ws"), V("wb"))] + ahead(1)
+            for x in range(2):
+                at(15 + 3 * x)
+                tt(run("Q", QW + 128 * x, 128), run("Q", QW + 128 * x, 128), half("Q", x), op_.add)
+            at(40)
+            ts(V("GS"), V("gi", 12, 16), col("pg", 1), None, op_.add)
+            at(37.2)
+            qrep(2, 18)
+            at(44.5)
+            squares(2)
+            at(53)
+            qrep(3)
+            at(46.5)
+            quant(V("wc"), V("ws"), V("wb"))
         else:
-            log.setdefault("p%dc" % t, []).append((0, 128, n - K, n, 1, True, "net", "arr%d" % (t - 1), NE))
-            log.setdefault("p%ds" % t, []).append((0, 128, n - K, n + PAD, 1, True, "net", "arr%d" % (t - 1), NE))
             wnd = pair("p%d" % t, n - 128, n)
-            lq = V("LP%d" % (t - 1), 0, 3)
-            mm("b1", *wnd, V("qc"), V("qs"))
+            at(0)
             mm("b0", *rep(t), *wnd)
+            mm("b1", *wnd, V("qc"), V("qs"))
+            at(3)
             sact(V("A2"), V("b0", 128 - K, 128), act.Abs, bias=NIL)
             sact(V("A"), V("b0", 128 - K, 128), act.Square)
-            sact(V("fl"), V("TC", 64, s=32), act.Relu, scale=ITEMS * 2 / UNIT, bias=ITEMS * (1.0 - 2 * W[t - 1]))
-            counts(1)
-            if more:
-                mm("b2", *rep(t + 1), *wnd)
-                sact(run("AQ", 0, K), V("b2", 128 - K, 128), act.Square)
             s0 = V("b1", t, t + 1, 64)
             for a in (0, 64):
                 ts(V("v", 0, 1, a, a + 64), s0, s0, TINY, op_.mult, op_.max)
             ts(V("v", 1, 2, 64), s0, -1.0, s0, op_.mult, op_.max)
-            carry[1]()
-            ts(V("C2"), V("RZ"), col("v", 0), None, op_.is_lt)
-            for x in range(2):
-                affine(col("X", XW * x + K), col("TC", 64 + 32 * x), 1.0, col("fl", x))
-            asum(col("X2", K), half("J", 4), V("C2"))
-            results(wnd, 128 - K, 128, lambda o: run("YA", K * o, K))
+            at(6)
             tt(V("Z2", p0=64), V("A2", p0=64), V("G", 128, 128 + K, 64), op_.mult)
             for x in range(2):
-                tt(run("X", XW * x, K), V("A"), run("CM", K * x, K), op_.is_le)
-            ts(V("X2", 0, K, 64), V("Z2", p0=64), NIL, V("v", 1, 2, 64), op_.subtract, op_.is_lt)
+                tt(run("X", XW * 2 * x, K), V("A"), run("CM", K * x, K), op_.is_le)
+            ts(V("X2", 0, 128), V("RZ"), col("v", 0), None, op_.is_lt)
+            ts(V("X2", 128, 128 + K, 0, 64), V("ZL", 2 * K, p1=64), V("v", 0, 1, 0, 64), None, op_.is_ge)
+            ts(V("X2", 128, 128 + K, 64), V("Z2", p0=64), NIL, V("v", 1, 2, 64), op_.subtract, op_.is_lt)
+            at(12)
             for x in range(2):
-                scan(V("BC", BW - 3 * XW // 2 + x, BW, s=3), V("X", XW * x, XW * x + XW, s=2), V("X", XW * x + 1, XW * x + XW, s=2), col("S", x), op_.add)
+                scan(V("BC", BW - 3 * XW + x, BW, s=3), run("X", XW * 2 * x, XW), run("X", XW * (2 * x + 1), XW), col("S", x), op_.subtract)
             scan(V("BC", BW - 3 * AW + 2, BW, 64, s=3), V("X2", p0=64), V("X2", p1=64), V("bs", t, t + 1, 64), op_.add)
             if more:
-                tt(came(t + 1, t - 1), V("A"), run("AQ", 0, K), op_.add)
-            carry[2]()
-            further = nothing
+                at(1)
+                mm("b2", *rep(t + 1), *wnd)
+                at(4)
+                sact(V("AQ"), V("b2", 128 - K, 128), act.Square)
+                at(13)
+                tt(came(t + 1, t - 1), V("A"), V("AQ"), op_.add)
             if t + 2 < R:
                 w = max(128, K * t)
+                at(7)
                 mm("b3", *rep(t + 2), *pair("p%d" % t, n - w, n))
-                sact(run("AQ", K, K * t), V("b3", w - K * t, w), act.Square)
                 if t == 1:
-                    sact(run("Q", 3 * P + n - w, w - K), V("b3", 0, w - K), act.Square)
+                    sact(run("Q", QW * 3 + n - w, w), V("b3", 0, w), act.Square)
                     squares(3, n - w)
-
-                def further():
-                    tt(came(t + 2, 0, t), came(t + 1, 0, t), run("AQ", K, K * t), op_.add)
-
-            def renew():
-                scatter(use(t + 1), lq, came(t + 1, t - 1))
-                if t + 2 < R:
-                    dma("p", ap(use(t + 2)), ap(use(t + 1)), [use(t + 2)], [use(t + 1)], accum_op=op_.add)
-
-            def first():
-                scatter(run("Y", 0, P), lq, run("YA", 0, K))
+                else:
+                    sact(came(t + 2, 0, t), V("b3", w - K * t, w), act.Square)
+                    squares(t + 2)
+                at(14)
+                add_to(use(t + 2, n), use(t + 1, n))
+            if t + 3 < R:
+                at(16)
+                qrep(t + 3, 23)
+            at(8)
+            results(wnd, 128 - K, 128, lambda o: run("YA", K * o, K))
+            if t == 1:
+                at(24)
+                results(own, 0, P, lambda o: block(0, o))
+            for o in range(O):
+                if t > 1:
+                    at(1)
+                    store(t - 2, o, "s", [arrival])
                 if not more:
-                    dma("s", T.y[:, (t - 1) * O * P:(t - 1) * O * P + P], ap(run("Y", 0, P)), [], [run("Y", 0, P)])
-            if more:
-                a = ahead(t + 1)
-                fill_in = [renew, a[0], further, a[1], a[2], lambda a=a: (a[3](), first())]
+                    at(6)
+                    sact(block(t - 1, o), block(t - 2, o), act.Copy)
+                at((53 if t == 1 else (32.5, 47)[o]) if more else 18)
+                scatter(block(t - 1, o), V("LP%d" % (t - 1), 0, 3), run("YA", K * o, K))
+        if more:
+            if t == 0:
+                at(24)
+                tt(V("X", K, s=2 * XW), V("pl"), V("ok"), op_.add)
             else:
-                fill_in = [nothing] * 5 + [first]
+                at(6.5)
+                sact(V("B"), use(t + 1, n - K), act.Copy, V("SO") if t > 1 else None)
+                at(18)
+                scatter(V("B"), V("LP%d" % (t - 1), 0, 3), came(t + 1, t - 1))
+                if t + 2 < R:
+                    at(43)
+                    ts(V("SO"), V("SF"), 1.0 / UNIT, None, op_.mult)
+                at(6)
+                sact(run("OG", 192, 64), V("SR"), act.Copy, V("GS"))
+                at(15)
+                turn(run("TC", 64, 64), run("OG", 192, 64))
+                at(24)
+                tt(V("X", K, s=2 * XW), V("TC", 64, s=32), V("ok"), op_.add)
+            at(22)
+            row = V("B") if t else use(1)
+            z = [run(row[0], row[3] + 128 * x, 128) for x in range(2)]
+            sact(run("OG", 128, 64), row, act.Copy, V("GL", 8, 12))
+            sact(half("OG", 0), row, act.Copy, V("GL", 0, 8))
+            at(25)
+            turn(run("TC", 0, 64), run("OG", 128, 64))
+            at(29)
+            ts(half("OG", 0), half("OG", 0), TINY, None, op_.max)
+            at(28)
+            ts(V("zb", 0, 2), V("TC", 0, 64, s=32), TINY, -1.0 / STEP, op_.is_le, op_.mult)
+            at(31)
+            tt(V("zb", 2, 4), V("TC", 0, 64, s=32), V("zb", 0, 2), op_.subtract)
+            for x in range(2):
+                at(37)
+                affine(half("TH", x), half("F", 1), col("zb", 2 + x), col("zb", x))
+                at((32, 37)[x])
+                ts(half("CS", 1 + x), z[1 - x], col("TC", 32 * x), None, (op_.is_lt, op_.is_le)[x])
+                at((44, 46)[x])
+                tt(half("CS", 3 * x), z[x], half("TH", x), op_.is_le)
+                at(*((50,), (5, 1))[x])
+                asum(col("S", x), run("J", P * x, P), run("CS", P * x, P))
         n2 = n if more else 128 - K
+        at(2)
         for x in "cs":
             a, b = V("p%d%s" % (t, x), 0, n2), V("p%d%s" % (t + 1, x), 0, n2)
             dma("s", u8(b) if x == "c" else ap(b), u8(a) if x == "c" else ap(a), [b], [a])
-        if t == 0:
-            for t2 in range(1, R):
-                v = V("o%ds" % t2, K, K + PAD)
-                dma("s", ap(v), ap(V("p0s", 0, PAD)), [v], [V("p0s", 0, PAD)])
+        at(17)
         turn(V("RC"), V("BC", BW - 96))
-        gap()
         for m in range(3):
+            at(20)
             ts(run("E", EW * m, 96), V("RC"), col("lo", m), col("hi", m), op_.max, op_.min)
-            if m < 2:
-                asum(col("Pm", m), run("JE", EW * m, EW), run("E", EW * m, EW))
-        gap()
-        vsum(col("Pm", 2), V("E", 2 * EW))
-        gap()
-        if t in (1, 2):
-            squares(t + 3)
-        for a in (0, 32, 64, 96):
-            b = a ^ 32
-            tt(V("T1", 0, 3, a, a + 32), V("Pm", 0, 3, a, a + 32), V("Pm", 0, 3, b, b + 32), op_.add)
-        gap()
+            at(23)
+            scan(V("JE", EW * m, EW * m + EW, 64), V("E", EW * m, EW * m + EW, 64), V("E", EW * m, EW * m + EW, p1=64), 0.0, op_.add)
         lst = V("L%d" % t, 0, 3)
-        for a in (0, 64):
+        if LIST:
+            at(27)
             for m in range(3):
-                ts(V("L%d" % t, m, m + 1, a, a + 64), V("T1", m, m + 1, a, a + 64), V("T1", m, m + 1, 64 - a, 128 - a), 1.0 / UNIT, op_.add, op_.mult)
-        gap()
+                c = EW * m + EW - 1
+                for p in (0, 32, 64, 96):
+                    ts(V("L%d" % t, m, m + 1, p, p + 32), V("JE", c, c + 1, 96), V("JE", c, c + 1, 64, 96), 1.0 / UNIT, op_.add, op_.mult)
+        else:
+            at(27)
+            for p in (64, 96):
+                tt(V("T1", 0, 3, p, p + 32), V("JE", EW - 1, p0=96, s=EW), V("JE", EW - 1, p0=64, p1=96, s=EW), op_.add)
+            at(30)
+            for p in (0, 64):
+                ts(V("L%d" % t, 0, 3, p, p + 64), V("T1", 0, 3, 64), 1.0 / UNIT, None, op_.mult)
+        at(34)
         pick(*pair("o%d" % t, 0, K), *pair("p%d" % t, 0, n), lst)
         dst = T.cores[rank ^ PART[t]]
         rid, pid, _e = topo.addr(dst)
         engs = topo.engines(core, dst)[:NE]
+        lanes.append(2 * len(engs))
         n1 = W[t + 1] if more else 128
-        order("p", "sent", 0, [], [V("o%dc" % t), V("o%ds" % t)])
-        g.remote_dma_fused([
-            RemoteDMATransfer(dst_ids=[DstId(rid=rid, pnc=pid)], dma_engine_mask=sum(1 << e for e in es), remote_sem=T.sem["arr%d" % t], src=src, dst=out)
-            for es, src, out in (
-                (engs[0::2], u8(V("o%dc" % t)), u8(V("p%dc" % (t + 1), n1 - K, n1))),
-                (engs[1::2], ap(V("o%ds" % t)), ap(V("p%ds" % (t + 1), n1 - K, n1 + PAD))))], local_sem=T.sem["sent"])
-        new, lp = run("PT", n, K), V("LP%d" % t, 0, 3)
+        parts = [RemoteDMATransfer(dst_ids=[DstId(rid=rid, pnc=pid)], dma_engine_mask=sum(1 << e for e in es), remote_sem=T.sem["arr%d" % t], src=src, dst=out)
+                 for es, src, out in ((engs, u8(V("o%dc" % t)), u8(V("p%dc" % (t + 1), n1 - K, n1))),
+                                      (engs, ap(V("o%ds" % t)), ap(V("p%ds" % (t + 1), n1 - K, n1 + PAD))))]
+        for x, part in zip("cs", parts):
+            call("p", [], [V("o%d%s" % (t, x))], lambda part=part: g.remote_dma_fused([part], local_sem=T.sem["sent"]), kind="send")
+        arrival = call("net", [V("p%dc" % (t + 1), n1 - K, n1), V("p%ds" % (t + 1), n1 - K, n1 + PAD)], [], ("arr%d" % t, lanes[t]), kind="net")
+        new, lp, lu = run("PT", n, K), V("LP%d" % t, 0, 3), V("LP%d" % t, 4, 7)
+        at(35)
         gather(new, V("PT", 0, n), lst)
+        at(38)
+        scan(run("D1", 0, K), V("DM"), new, 0.0, op_.max)
+        at(42)
+        ts(lp, V("D1", 15, K, s=16), col("pg", 0), None, op_.add)
         if t == 0:
-            squares(2)
-            qrep(3, 5)
-        gap()
-        scan(V("D1"), V("DM"), new, 0.0, op_.max)
-        if t:
-            scatter(run("Y", P, P), lq, run("YA", K, K))
-        gap()
+            at(45)
+            add_to(use(2), use(1))
+        if t + 2 < R:
+            at(35)
+            sact(run("PU", n, K), V("PU", 0, n), act.Copy, lst)
+            at(39)
+            scan(run("D1", K, K), V("DM"), run("PU", n, K), 0.0, op_.max)
+            at(43)
+            ts(lu, V("D1", K + 15, s=16), col("pg", 0), None, op_.add)
+            at(45)
+            scatter(V("SR"), lu, run("SV", n - P, K))
+            if t + 3 < R:
+                dma("s", ap(V("SF")), ap(V("SR", p1=8)), [V("SF")], [V("SR")])
         if more:
-            ts(V("zb", 0, 2), V("TC", 0, 64, s=32), TINY, -1.0 / STEP, op_.is_le, op_.mult)
-        for x in range(2 if more else 1):
-            ts(V("LP%d" % t, 3 * x, 3 * x + 3), V("D1", 15, s=16), col("pg", x), 1.0 / UNIT, op_.add, op_.mult)
-        if not more:
-            copy(V("YL"), V("Y"))
-            wait("s", "sent", NE * R)
-            dma("s", T.y[:, t * O * P - P:t * O * P], ap(run("Y", P, P)), [], [run("Y", P, P)])
-        else:
-            if t == 0:
-                dma("p", ap(use(2)), ap(use(1)), [use(2)], [use(1)], accum_op=op_.add)
-            sact(V("p2"), V("D1"), act.Identity, V("PL", 0, 1), bias=col("pg", 0))
-            p2 = col("p2", 0)
-            if t == 0:
-                results(own, 0, P, lambda o: run("Y", P * o, P))
+            at(36)
+            sact(run("ZL", 0, K), use(t + 1, n), act.Copy, lst)
+            at(40)
+            ts(run("ZL", K, K), run("ZL", 0, K), TINY, None, op_.max)
             for x in range(2):
-                ts(run("G", 128 + K + K * x, K), new, col("pl", x), PRED, op_.is_lt, op_.max)
-            tt(V("zb", 2, 4), V("TC", 0, 64, s=32), V("zb", 0, 2), op_.subtract)
-            if t == 1:
-                qrep(5, 6)
-            sact(half("G", 0), V("SH"), act.Sign, scale=-1.0, bias=p2)
-            scatter(V("Z"), V("LP%d" % t), V("big"))
-            scatter(V("SR"), lp, run("SV", n, K))
-            affine(half("G", 0), half("G", 0), -STEP, 1.0)
-            sact(half("OG", 0), run("Z", 0, P), act.Copy, V("GL", 0, 8))
-            sact(run("OG", 192, 64), V("SR"), act.Copy, V("GL", 8, 12))
+                sact(run("SG", K * x, K), new, act.Sign, bias=col("pm", x))
+            at(39)
+            sact(V("p2"), run("D1", 0, K), act.Identity, V("PL", 0, 1), bias=col("pg", 0))
+            at(38.5)
+            for x in range(2):
+                ts(run("G", 128 + K + K * x, K), new, col("pn", x), PRED, op_.is_lt, op_.max)
+            at(44.5)
+            ts(half("G", 0), V("SH"), p2, PRED, op_.is_ge, op_.max)
+            ts(run("G", 128, K), new, p2, PRED, op_.is_ge, op_.max)
+            at(40.5)
             for x in range(2):
                 affine(run("CM", K * x, K), run("G", 128 + K + K * x, K), col("zb", 2 + x), col("zb", x))
-            ts(run("CS", 0, P), run("Z", 128, P), col("TC", 0), None, op_.is_lt)
-            ts(half("CS", 2), half("Z", 0), col("TC", 32), None, op_.is_le)
-            ts(half("CS", 3), half("Z", 3), col("TC", 32), None, op_.is_lt)
-            counts(0)
-            ts(run("G", 128, K), new, p2, PRED, op_.is_ge, op_.max)
-            carry = [lambda a=a, t=t: scatter(use(t + 2), V("LP%d" % a, 0, 3), came(t + 2, a)) for a in range(t if t + 2 < R else 0)]
-            carry = [nothing] * (2 - len(carry)) + carry + [nothing]
-            carry[0]()
+            at(51)
+            for x in range(2):
+                asum(col("X", XW * (2 * x + 1) + K), run("J", 2 * P + K * x, K), run("SG", K * x, K), act.Square, scale=OUT)
+            at(49)
+            for x in range(2):
+                tt(run("X", XW * (2 * x + 1), K), run("ZL", 0, K), run("CM", K * x, K), op_.is_le)
+            at(46.5)
             tt(V("RZ"), half("OG", 0), half("G", 0), op_.mult)
-            turn(run("TC", 64, 64), run("OG", 192, 64))
-            if t:
-                wait("s", "arr%d" % t, NE)
-                store(t - 1)
+            tt(V("ZL", 2 * K, p1=64), V("ZL", K, 2 * K, p1=64), V("G", 128, 128 + K, p1=64), op_.mult)
 
-    log["p6c"].append((0, 128, 128 - K, 128, 1, True, "net", "arr%d" % (R - 1), NE))
-    log["p6s"].append((0, 128, 128 - K, 128 + PAD, 1, True, "net", "arr%d" % (R - 1), NE))
+    for o in range(O):
+        at(19)
+        store(R - 2, o, "s")
+        at(40)
+        sact(block(R - 1, o), block(R - 2, o), act.Copy)
+    at(60)
     results(pair("p6", 0, 128), 128 - K, 128, lambda o: run("YA", K * o, K))
     for o in range(O):
-        y = run("YL", P * o, P)
-        scatter(y, V("LP%d" % (R - 1), 0, 3), run("YA", K * o, K))
-        i = (R - 1) * O * P + P * o
-        dma("sa"[o], T.y[:, i:i + P], ap(y), [], [y])
+        scatter(block(R - 1, o), V("LP%d" % (R - 1), 0, 3), run("YA", K * o, K))
+        store(R - 1, o, "sa"[o])
 
+    count = {"v": 0, "a": 0, "t": 0, "p": 0, "d": 0}
+    seen, mark = {}, {}
+
+    def wait(q, sem, val):
+        if seen.get((q, sem), 0) < val:
+            seen[(q, sem)] = val
+            queues[q].wait_ge(T.sem[sem], val)
+
+    for i in sorted(range(len(calls)), key=lambda i: (calls[i][0], i)):
+        _step, q, fn, after, kind = calls[i]
+        if kind == "net":
+            mark[i] = fn
+            continue
+        need = {}
+        for j in after:
+            need[mark[j][0]] = max(need.get(mark[j][0], 0), mark[j][1])
+        for sem in sorted(need):
+            wait(q, sem, need[sem])
+        if kind == "send":
+            fn()
+            continue
+        key = "d" if kind == "dma" else q
+        count[key] += 1
+        mark[i] = ("d%d" % (count[key] - 1), 16) if key == "d" else ("s" + key, count[key])
+        fn().then_inc(T.sem[mark[i][0]], 16 if key == "d" else 1)
     for q in "vatp":
         wait("p", "s" + q, count[q])
     for i in range(count["d"]):
         wait("p", "d%d" % i, 16)
     for t in range(R):
-        wait("p", "arr%d" % t, NE)
-    wait("p", "sent", NE * R)
+        wait("p", "arr%d" % t, lanes[t])
+    wait("p", "sent", sum(lanes))

@@ -33,7 +33,7 @@ SCRATCH = {n: ("sbuf", [128, w], d) for n, w, d in (
     ("B", P, F32), ("B0", 2 * P, F32), ("OG", P, F32), ("TC", 128, F32),
     ("G", 128 + 3 * K, F32), ("RZ", 128, F32), ("A", K, F32), ("A2", K, F32), ("Z2", K, F32), ("CM", 2 * K, F32), ("v", 2, F32),
     ("p2", 16, F32), ("zb", 4, F32), ("CS", 2 * P, F32), ("C0", 4 * 160, F32), ("SG", 2 * K, F32), ("X", 4 * XW, F32), ("X2", AW, F32),
-    ("J", 5 * 128, F32), ("JE", 3 * EW, F32), ("S", 2, F32), ("BC", BW, F32), ("RC", 96, F32), ("E", 3 * EW, F32),
+    ("J", 5 * 128, F32), ("T0", P, F32), ("JE", 3 * EW, F32), ("S", 2, F32), ("BC", BW, F32), ("RC", 96, F32), ("E", 3 * EW, F32),
     ("T1", 4, F32), ("D1", 2 * K, F32),
     ("Y0", O * P, F32), ("Y1", O * P, F32), ("YA", O * K, F32), ("p6c", 128, CODE), ("p6s", 128 + PAD, U8))}
 for _t in range(R):
@@ -209,7 +209,7 @@ def rank_program(g, core, T, topo):
     for x in range(2):
         dma("sa"[x], ap(run("cb", 512 * x, 512)), T.c[:, 512 * x:512 * x + 512], [run("cb", 512 * x, 512)], [])
     dma("s", ap(V("wb")), T.w[:], [V("wb")], [V("cb")])
-    fill(V("F"), PRED)
+    fill(half("F", 1), PRED)
     fill(V("qb", 4 * R), 0.0)
     whole(V("qi"), [[1, R], [0, 8]], 0, 0)
     whole(col("pi", 0), [[0, 1]], 0, 1)
@@ -217,13 +217,12 @@ def rank_program(g, core, T, topo):
     whole(V("li"), [[16, 3]], 0, 0)
     whole(V("I17"), [[1, 17]], -1, 0)
     whole(V("gi", 8, 12), [[128, 2], [16, 2]], 0, 0)
-    slope(0, op_.is_gt, 1)
+    slope(1, op_.is_ge, -1)
     whole(V("gi", 0, 8), [[16, 8]], 0, 0)
     whole(V("gi", 12, 16), [[8, 2], [1, 2]], 0, 0)
     whole(V("bi"), [[K, R]], 128 - K * 512, 1)
     whole(V("IT"), [[1, P]], 0, 0)
     whole(V("PU", 0, P), [[1, 16], [16, 16]], 0, 0)
-    slope(1, op_.is_ge, -1)
     copy(V("qo"), V("qi"))
     for i, bits in enumerate((0x0F, 0x60, 0x30, 0x4F, 0x40)):
         ts(col("pi", 1 + i), col("pi", 0), bits, None, op_.bitwise_and)
@@ -283,14 +282,16 @@ def rank_program(g, core, T, topo):
                 mm("b%d" % (3 + x), *part, V("qc"), V("qs"))
                 at(-75 + 10 * x)
                 sact(half("B0", x), V("b%d" % x, 0, 128), act.Abs, bias=NIL)
-                at(-60 + 10 * x)
-                s0 = col("b%d" % (3 + x), 0)
-                ts(col("v", x), s0, -1.0, s0, op_.mult, op_.max)
-                tt(half("B0", 2 + x), half("B0", x), half("F", 0), op_.mult)
+                sact(col("v", x), col("b%d" % (3 + x), 0), act.Abs, bias=NIL)
+                at(-63)
+                sact(half("T0", x), half("F", 1), act.Copy, scale=col("v", x))
+                at(-50)
                 sact(half("Q", x), V("b%d" % x, 0, 128), act.Square)
-            for c, b, x, o, step in ((0, 2, 0, op_.is_lt, -45), (1, 1, 0, op_.is_lt, -45), (2, 0, 1, op_.is_le, -44), (3, 3, 1, op_.is_lt, -44)):
-                at(step)
-                ts(run("C0", 160 * c, 128), half("B0", b), NIL, col("v", x), op_.subtract, o)
+            for x in range(2):
+                at(-45)
+                tt(run("C0", 480 * x, 128), half("B0", x), half("T0", x), op_.is_le)
+                at(-46)
+                ts(run("C0", 160 + 160 * x, 128), half("B0", 1 - x), col("v", x), None, (op_.is_lt, op_.is_le)[x])
             at(14)
             for x in range(2):
                 scan(V("BC", BW - 480 + x, BW, s=3), run("C0", 320 * x, 160), run("C0", 320 * x + 160, 160), col("pl", x), op_.add)
@@ -304,13 +305,12 @@ def rank_program(g, core, T, topo):
                 tt(run("Q", QW + 128 * x, 128), run("Q", QW + 128 * x, 128), half("Q", x), op_.add)
             at(40)
             ts(V("GS"), V("gi", 12, 16), col("pg", 1), None, op_.add)
-            at(37.2)
-            qrep(2, 18)
-            at(44.5)
+            for t2 in (2, 3, 4):
+                at(-58)
+                qrep(t2, (-39, 31, ROUND + 23)[t2 - 2])
+            at(23)
             squares(2)
             at(53)
-            qrep(3)
-            at(46.5)
             quant(V("wc"), V("ws"), V("wb"))
         else:
             wnd = pair("p%d" % t, n - 128, n)
@@ -340,7 +340,7 @@ def rank_program(g, core, T, topo):
                 mm("b2", *rep(t + 1), *wnd)
                 at(4)
                 sact(V("AQ"), V("b2", 128 - K, 128), act.Square)
-                at(13)
+                at(11.5)
                 tt(came(t + 1, t - 1), V("A"), V("AQ"), op_.add)
             if t + 2 < R:
                 w = max(128, K * t)
@@ -354,7 +354,7 @@ def rank_program(g, core, T, topo):
                     squares(t + 2)
                 at(14)
                 add_to(use(t + 2, n), use(t + 1, n))
-            if t + 3 < R:
+            if t == 2:
                 at(16)
                 qrep(t + 3, 23)
             at(8)
@@ -369,7 +369,7 @@ def rank_program(g, core, T, topo):
                 if not more:
                     at(6)
                     sact(block(t - 1, o), block(t - 2, o), act.Copy)
-                at((53 if t == 1 else (32.5, 47)[o]) if more else 18)
+                at((53 if t == 1 else 47) if more else (18, 21)[o])
                 scatter(block(t - 1, o), V("LP%d" % (t - 1), 0, 3), run("YA", K * o, K))
         if more:
             if t == 0:
@@ -400,7 +400,7 @@ def rank_program(g, core, T, topo):
             ts(half("OG", 0), half("OG", 0), TINY, None, op_.max)
             at(28)
             ts(V("zb", 0, 2), V("TC", 0, 64, s=32), TINY, -1.0 / STEP, op_.is_le, op_.mult)
-            at(31)
+            at(36)
             tt(V("zb", 2, 4), V("TC", 0, 64, s=32), V("zb", 0, 2), op_.subtract)
             for x in range(2):
                 at(37)
@@ -458,7 +458,7 @@ def rank_program(g, core, T, topo):
         at(42)
         ts(lp, V("D1", 15, K, s=16), col("pg", 0), None, op_.add)
         if t == 0:
-            at(45)
+            at(36)
             add_to(use(2), use(1))
         if t + 2 < R:
             at(35)
@@ -500,7 +500,7 @@ def rank_program(g, core, T, topo):
             tt(V("ZL", 2 * K, p1=64), V("ZL", K, 2 * K, p1=64), V("G", 128, 128 + K, p1=64), op_.mult)
 
     for o in range(O):
-        at(19)
+        at(22)
         store(R - 2, o, "s")
         at(40)
         sact(block(R - 1, o), block(R - 2, o), act.Copy)
@@ -511,12 +511,14 @@ def rank_program(g, core, T, topo):
         store(R - 1, o, "sa"[o])
 
     count = {"v": 0, "a": 0, "t": 0, "p": 0, "d": 0}
-    seen, mark = {}, {}
+    seen, mark, behind = {q: {} for q in queues}, {}, {}
 
     def wait(q, sem, val):
-        if seen.get((q, sem), 0) < val:
-            seen[(q, sem)] = val
+        if seen[q].get(sem, 0) < val:
             queues[q].wait_ge(T.sem[sem], val)
+            seen[q][sem] = val
+            for s2, v2 in behind.get((sem, val), {}).items():
+                seen[q][s2] = max(seen[q].get(s2, 0), v2)
 
     for i in sorted(range(len(calls)), key=lambda i: (calls[i][0], i)):
         _step, q, fn, after, kind = calls[i]
@@ -526,7 +528,7 @@ def rank_program(g, core, T, topo):
         need = {}
         for j in after:
             need[mark[j][0]] = max(need.get(mark[j][0], 0), mark[j][1])
-        for sem in sorted(need):
+        for sem in sorted(need, key=lambda s: -len(behind.get((s, need[s]), ()))):
             wait(q, sem, need[sem])
         if kind == "send":
             fn()
@@ -534,11 +536,15 @@ def rank_program(g, core, T, topo):
         key = "d" if kind == "dma" else q
         count[key] += 1
         mark[i] = ("d%d" % (count[key] - 1), 16) if key == "d" else ("s" + key, count[key])
+        behind[mark[i]] = dict(seen[q])
         fn().then_inc(T.sem[mark[i][0]], 16 if key == "d" else 1)
-    for q in "vatp":
-        wait("p", "s" + q, count[q])
-    for i in range(count["d"]):
+    behind.clear()
+    for i in range(count["d"] - O):
         wait("p", "d%d" % i, 16)
     for t in range(R):
         wait("p", "arr%d" % t, lanes[t])
     wait("p", "sent", sum(lanes))
+    for q in "ptav":
+        wait("p", "s" + q, count[q])
+    for i in range(count["d"] - O, count["d"]):
+        wait("p", "d%d" % i, 16)

from concourse.bass import DstId, RemoteDMATransfer
from concourse.mybir import dt, AluOpType, AxisListType, ActivationFunctionType

N, P, K, R, O = 8, 256, 48, 6, 2
PART = [1, 2, 4, 1, 2, 4]
NE = 8
W = [P + K * t for t in range(R + 1)]
STEP = 2.0 ** -24
PRED = 1.0 - STEP
TINY = 2.0 ** -122
NIL = 2.0 ** -86
UNIT = 1.0 / 512
PAD = 0 * K
ITEMS = 3 * 128
XW = K + 32
OUT = 8.0
AW = 128 + K + 31
BW = 3 * 208
QW = W[R - 2]
EW = 97
LIST = 1
ROUND = 100

F32, CODE, U8, U16, BF, I32 = "float32", "float8_e4m3fn_x4", "uint8", "uint16", "bfloat16", "int32"
SCRATCH = {n: ("sbuf", [128, w], d) for n, w, d in (
    ("cb", 4 * P, BF), ("qb", 512, BF), ("wb", 512 * O, BF),
    ("qc", 128, CODE), ("qs", 128, U8), ("rc", 128 * R, CODE), ("rs", 128 * R, U8), ("wc", 128 * O, CODE), ("ws", 128 * O, U8),
    ("IT", P, F32), ("SV", 4 * K, F32), ("ok", 2, F32), ("PT", W[R], F32), ("F", P, F32), ("TH", P, F32), ("DM", K, F32), ("SH", 128, F32),
    ("pi", 6, I32), ("qi", 8 * R, I32), ("gi", 16, I32), ("pf", 5, F32), ("pg", 3, F32), ("pn", 2, F32), ("pl", 2, F32), ("pm", 2, F32),
    ("I17", 17, F32), ("M16", 32, F32), ("li", 3, F32), ("lo", 3, F32), ("hi", 3, F32), ("bi", R, F32), ("bs", R, F32), ("ZL", 3 * K, F32),
    ("GL", 12, U16), ("QL", 4, U16), ("PL", 2, U16), ("qo", 8 * R, U16),
    ("Q", R * QW, F32), ("AQ", K, F32), ("SR", P, F32), ("PU", W[R - 1], F32), ("SF", 16, F32), ("SO", 16, U16), ("GS", 4, U16),
    ("B", P, F32), ("B0", 2 * P, F32), ("OG", P, F32), ("TC", 128, F32),
    ("G", 128 + 3 * K, F32), ("RZ", 128, F32), ("A", K, F32), ("A2", K, F32), ("Z2", K, F32), ("CM", 2 * K, F32), ("v", 2, F32),
    ("p2", 16, F32), ("zb", 4, F32), ("CS", 2 * P, F32), ("C0", 4 * 160, F32), ("SG", 2 * K, F32), ("X", 4 * XW, F32), ("X2", AW, F32),
    ("J", 5 * 128, F32), ("T0", P, F32), ("JE", 3 * EW, F32), ("S", 2, F32), ("BC", BW, F32), ("RC", 96, F32), ("E", 3 * EW, F32),
    ("T1", 4, F32), ("D1", 2 * K, F32),
    ("Y0", O * P, F32), ("Y1", O * P, F32), ("YA", O * K, F32), ("p6c", 128, CODE), ("p6s", 128 + PAD, U8))}
for _t in range(R):
    for _n, _w, _d in (("p%dc", W[_t], CODE), ("p%ds", W[_t] + PAD, U8), ("o%dc", K, CODE), ("o%ds", K + PAD, U8),
                       ("L%d", 4, U16), ("LP%d", 8, U16)):
        SCRATCH[_n % _t] = ("sbuf", [128, _w], _d)
for _b in range(8):
    SCRATCH["b%d" % _b] = ("psum", [128, 512], F32)
NDMA = 52
SEMAPHORES = ["sv", "sa", "st", "sp", "sent"] + ["arr%d" % t for t in range(R)] + ["d%d" % i for i in range(NDMA)]


def rank_program(g, core, T, topo):
    rank = T.rank_of(core)
    if rank is None:
        return
    op_ = AluOpType
    act = ActivationFunctionType
    queues = {"v": g.vector, "a": g.scalar, "t": g.tensor, "p": g, "s": g.sync}
    calls = []
    log = {}
    psum = {"b%d" % b for b in range(8)}
    now, lanes = [0, 0], []

    def at(step, later=0):
        now[1] = ROUND * (now[0] + later) + step

    def V(n, c0=0, c1=None, p0=0, p1=128, s=1):
        return (n, p0, p1, c0, SCRATCH[n][1][1] if c1 is None else c1, s)

    def col(n, c):
        return V(n, c, c + 1)

    def run(n, c, w):
        return V(n, c, c + w)

    def ap(v):
        if not isinstance(v, tuple):
            return v
        n, p0, p1, c0, c1, s = v
        return T[n][p0:p1, c0:c1] if s == 1 else T[n][p0:p1, c0:c1:s]

    def u8(v):
        return ap(v).bitcast(dt.uint8)

    def views(*xs):
        return [x for x in xs if isinstance(x, tuple)]

    def call(q, writes, reads, fn, after=(), kind="op"):
        need = set(after)
        for vs, wr in ((reads, False), (writes, True)):
            for n, p0, p1, c0, c1, s in vs:
                whole = n in psum
                for a0, a1, b0, b1, s2, w2, q2, j in log.get(n, ()):
                    if not whole and (a1 <= p0 or p1 <= a0 or b1 <= c0 or c1 <= b0 or (s == s2 and (c0 - b0) % s)):
                        continue
                    if w2 or wr or whole and q2 != q:
                        need.add(j)
        for vs, wr in ((reads, False), (writes, True)):
            for n, p0, p1, c0, c1, s in vs:
                old = log.setdefault(n, [])
                if wr and s == 1:
                    old[:] = [e for e in old if not (p0 <= e[0] and e[1] <= p1 and c0 <= e[2] and e[3] <= c1)]
                old.append((p0, p1, c0, c1, s, wr, q, len(calls)))
        calls.append((now[1], q, fn, sorted(need), kind))
        return len(calls) - 1

    def dma(q, out, in_, writes, reads, after=(), **k):
        return call(q, writes, reads, lambda: queues[q].dma_start(out, in_, **k), after, "dma")

    def ts(out, in0, s1, s2, o0, o1=None):
        more = () if o1 is None else (o1,)
        call("v", [out], views(in0, s1, s2), lambda: g.vector.tensor_scalar(ap(out), ap(in0), ap(s1), ap(s2), o0, *more))

    def tt(out, a, b, o):
        call("v", [out], [a, b], lambda: g.vector.tensor_tensor(ap(out), ap(a), ap(b), o))

    def scan(out, a, b, first, o):
        call("v", [out], views(a, b, first), lambda: g.vector.tensor_tensor_scan(ap(out), ap(a), ap(b), ap(first), op_.add, o))

    def vsum(out, a):
        call("v", [out], [a], lambda: g.vector.tensor_reduce(ap(out), ap(a), AxisListType.X, op_.add))

    def copy(out, a):
        call("v", [out], [a], lambda: g.vector.tensor_copy(ap(out), ap(a)))

    def gather(out, win, off):
        call("v", [out], [win, off], lambda: g.vector.tensor_copy(ap(out), ap(win).indirect(ap(off))))

    def scatter(win, off, a):
        call("v", [win], [a, off], lambda: g.vector.tensor_copy(ap(win).indirect(ap(off)), ap(a)))

    def turn(out, a):
        call("v", [out], [a], lambda: g.vector.transpose(ap(out), ap(a)))

    def fill(v, x):
        call("v", [v], [], lambda: g.vector.memset(ap(v), x))

    def sact(out, a, f, off=None, **k):
        call("a", [out], views(a, off, *k.values()), lambda: g.scalar.activation(
            ap(out), ap(a).indirect(ap(off)) if off else ap(a), f, **{n: ap(x) for n, x in k.items()}))

    def affine(out, a, scale, bias):
        sact(out, a, act.Identity, scale=scale, bias=bias)

    def asum(out, junk, a, f=act.Copy, **k):
        call("a", [out, junk], [a], lambda: g.scalar.activation(ap(junk), ap(a), f, accum_out=ap(out), **k))

    def quant(c, s, a):
        call("v", [c, s], [a], lambda: g.vector.quantize_mx(ap(c), ap(s), ap(a)))

    def mm(bank, lc, ls, rc, rs):
        out = V(bank, 0, rc[4] - rc[3])
        call("t", [out], [lc, ls, rc, rs], lambda: g.tensor.matmul_mx(ap(out), ap(lc), ap(ls), ap(rc), ap(rs), True, True))

    def pick(oc, os, c, s, off, then=None):
        call("v", [oc], [c, off], lambda: g.vector.tensor_copy(ap(oc).bitcast(dt.uint32), ap(c).bitcast(dt.uint32).indirect(ap(off))))
        if then is not None:
            at(then)
        sact(os, s, act.Copy, off)

    def pair(n, a, b):
        return V(n + "c", a, b), V(n + "s", a, b)

    def rep(t):
        return pair("r", 128 * t, 128 * t + 128)

    def qrep(t, then=None):
        pick(*rep(t), V("qc"), V("qs"), V("qo", 8 * t, 8 * t + 8), then)

    def tile(o):
        return pair("w", 128 * o, 128 * o + 128)

    def whole(v, *pat):
        k = {} if SCRATCH[v[0]][2] == I32 else {"allow_small_or_imprecise_dtypes": True}
        call("p", [v], [], lambda: g.iota(ap(v), *pat, **k))

    def slope(x, o, s):
        call("p", [half("F", x)], [half("F", x)], lambda: g.affine_select(ap(half("F", x)), ap(half("F", x)), [[-s, 128]], o, 1.0, 0, s))

    def half(n, x):
        return V(n, 128 * x, 128 * x + 128)

    def results(wnd, a, b, out):
        for o in range(O):
            mm("b%d" % (6 + o), *tile(o), *wnd)
            sact(out(o), V("b%d" % (6 + o), a, b), act.Copy)

    def use(t, w=P):
        return run("Q", QW * t, w)

    def came(t, a, k=1):
        return run("Q", QW * t + P + K * a, K * k)

    def add_to(out, a, after=()):
        dma("p", ap(out), ap(a), [out], [a], after, accum_op=op_.add)

    def squares(t, w=P):
        mm("b5", *rep(t), *pair("p0", 0, w))
        sact(use(t, w), V("b5", 0, w), act.Square)

    def block(t, o):
        return run("Y%d" % (t == R - 2), P * o, P)

    def store(t, o, q, after=()):
        i = (t * O + o) * P
        dma(q, T.y[:, i:i + P], ap(block(t, o)), [], [block(t, o)], after)

    q16, b32, p2 = col("pf", 0), col("pf", 1), col("p2", 0)

    at(-90)
    dma("a", ap(V("qb", 0, 4 * R)), T.qt[:, 0:4 * R], [V("qb", 0, 4 * R)], [])
    for x in range(2):
        dma("sa"[x], ap(run("cb", 512 * x, 512)), T.c[:, 512 * x:512 * x + 512], [run("cb", 512 * x, 512)], [])
    dma("s", ap(V("wb")), T.w[:], [V("wb")], [V("cb")])
    fill(half("F", 1), PRED)
    fill(V("qb", 4 * R), 0.0)
    whole(V("qi"), [[1, R], [0, 8]], 0, 0)
    whole(col("pi", 0), [[0, 1]], 0, 1)
    whole(V("pn"), [[128, 2]], 0, 1)
    whole(V("li"), [[16, 3]], 0, 0)
    whole(V("I17"), [[1, 17]], -1, 0)
    whole(V("gi", 8, 12), [[128, 2], [16, 2]], 0, 0)
    slope(1, op_.is_ge, -1)
    whole(V("gi", 0, 8), [[16, 8]], 0, 0)
    whole(V("gi", 12, 16), [[8, 2], [1, 2]], 0, 0)
    whole(V("bi"), [[K, R]], 128 - K * 512, 1)
    whole(V("IT"), [[1, P]], 0, 0)
    whole(V("PU", 0, P), [[1, 16], [16, 16]], 0, 0)
    copy(V("qo"), V("qi"))
    for i, bits in enumerate((0x0F, 0x60, 0x30, 0x4F, 0x40)):
        ts(col("pi", 1 + i), col("pi", 0), bits, None, op_.bitwise_and)
    for c in range(4):
        fill(run("C0", 160 * c + 128, 32), 0.0)
    copy(V("pf"), V("pi", 1, 6))
    fill(V("X"), 0.0)
    quant(V("qc"), V("qs"), V("qb"))
    fill(V("BC", BW - 96), float(ITEMS))
    fill(V("X2", 128 + K), 0.0)
    ts(col("pg", 0), q16, 15.0, -float(P), op_.is_lt, op_.mult)
    qrep(0)
    affine(V("pl"), V("pn"), UNIT, 0.0)
    affine(V("lo"), V("li"), 1.0, q16)
    affine(V("pm"), V("pn"), -1.0, 0.0)
    affine(col("pg", 1), b32, 1.0 / 16, 0.0)
    sact(col("pg", 2), col("pn", 0), act.Relu, scale=-float(ITEMS), bias=float(ITEMS * (128 - K)))
    at(-76)
    affine(V("hi"), V("lo"), 1.0, 1.0 - UNIT)
    affine(V("E", EW - 1, 3 * EW, s=EW), V("lo"), -(ITEMS - 1.0 + UNIT) / 4, -(ITEMS - 1) * (1.0 - UNIT) / 4)
    affine(col("pg", 1), q16, 16.0, col("pg", 1))
    at(-79)
    qrep(1)
    at(-69)
    ts(V("M16", 0, 16), V("I17", 1, 17), q16, -4.0 * P, op_.is_equal, op_.mult)
    ts(V("M16", 16, 32), V("I17", 0, 16), q16, float(P), op_.is_equal, op_.mult)
    ts(V("QL"), run("C0", 128, 4), q16, None, op_.add)
    ts(V("GL", 8, 12), V("gi", 8, 12), q16, b32, op_.add, op_.add)
    at(25.5)
    tt(V("M16", 0, 16), V("M16", 0, 16), V("M16", 16, 32), op_.add)
    ts(col("PL", 0), col("pf", 2), 1.0, 15.0, op_.subtract, op_.max)
    at(30)
    sact(V("DM"), V("M16", 0, 16), act.Copy, V("QL", 0, 3))
    at(-59)
    ts(V("GL", 0, 8), V("gi", 0, 8), col("pf", 3), col("pf", 4), op_.add, op_.add)
    at(-40)
    affine(V("bs"), V("bi"), UNIT, col("pg", 2))
    affine(V("ok"), V("pn"), 0.0, OUT * OUT * K)
    affine(V("SV"), run("IT", 0, 4 * K), UNIT, P * UNIT)
    sact(V("SR"), V("PU", 0, P), act.Copy, scale=UNIT)
    for q, a, b in [("p", V("PT", 0, P), V("IT", 0, P))] + [
            ("s", V("SH", p0=64 * x, p1=64 * x + 64), V("IT", 128 * x, 128 * x + 128, 64 * x, 64 * x + 64)) for x in range(2)]:
        dma(q, ap(a), ap(b), [a], [b])
    own = pair("p0", 0, P)
    arrival = None

    for t in range(R):
        now[0] = t
        more = t + 1 < R
        n = W[t]
        if t == 0:
            for x in range(2):
                part = pair("p0", 128 * x, 128 * x + 128)
                at(-80 + 10 * x)
                quant(*part, run("cb", 512 * x, 512))
                mm("b%d" % x, *rep(0), *part)
                mm("b%d" % (3 + x), *part, V("qc"), V("qs"))
                at(-75 + 10 * x)
                sact(half("B0", x), V("b%d" % x, 0, 128), act.Abs, bias=NIL)
                sact(col("v", x), col("b%d" % (3 + x), 0), act.Abs, bias=NIL)
                at(-63)
                sact(half("T0", x), half("F", 1), act.Copy, scale=col("v", x))
                at(-50)
                sact(half("Q", x), V("b%d" % x, 0, 128), act.Square)
            for x in range(2):
                at(-45)
                tt(run("C0", 480 * x, 128), half("B0", x), half("T0", x), op_.is_le)
                at(-46)
                ts(run("C0", 160 + 160 * x, 128), half("B0", 1 - x), col("v", x), None, (op_.is_lt, op_.is_le)[x])
            at(14)
            for x in range(2):
                scan(V("BC", BW - 480 + x, BW, s=3), run("C0", 320 * x, 160), run("C0", 320 * x + 160, 160), col("pl", x), op_.add)
            at(-48)
            for t2 in range(R if PAD else 0):
                v = V("o%ds" % t2, K, K + PAD)
                dma("s", ap(v), ap(V("p0s", 0, PAD)), [v], [V("p0s", 0, PAD)])
            squares(1)
            for x in range(2):
                at(15 + 3 * x)
                tt(run("Q", QW + 128 * x, 128), run("Q", QW + 128 * x, 128), half("Q", x), op_.add)
            at(40)
            ts(V("GS"), V("gi", 12, 16), col("pg", 1), None, op_.add)
            for t2 in (2, 3, 4):
                at(-58)
                qrep(t2, (-39, 31, ROUND + 23)[t2 - 2])
            at(23)
            squares(2)
            at(53)
            quant(V("wc"), V("ws"), V("wb"))
        else:
            wnd = pair("p%d" % t, n - 128, n)
            at(0)
            mm("b0", *rep(t), *wnd)
            mm("b1", *wnd, V("qc"), V("qs"))
            at(3)
            sact(V("A2"), V("b0", 128 - K, 128), act.Abs, bias=NIL)
            sact(V("A"), V("b0", 128 - K, 128), act.Square)
            s0 = V("b1", t, t + 1, 64)
            for a in (0, 64):
                ts(V("v", 0, 1, a, a + 64), s0, s0, TINY, op_.mult, op_.max)
            ts(V("v", 1, 2, 64), s0, -1.0, s0, op_.mult, op_.max)
            at(6)
            tt(V("Z2", p0=64), V("A2", p0=64), V("G", 128, 128 + K, 64), op_.mult)
            for x in range(2):
                tt(run("X", XW * 2 * x, K), V("A"), run("CM", K * x, K), op_.is_le)
            ts(V("X2", 0, 128), V("RZ"), col("v", 0), None, op_.is_lt)
            ts(V("X2", 128, 128 + K, 0, 64), V("ZL", 2 * K, p1=64), V("v", 0, 1, 0, 64), None, op_.is_ge)
            ts(V("X2", 128, 128 + K, 64), V("Z2", p0=64), NIL, V("v", 1, 2, 64), op_.subtract, op_.is_lt)
            at(12)
            for x in range(2):
                scan(V("BC", BW - 3 * XW + x, BW, s=3), run("X", XW * 2 * x, XW), run("X", XW * (2 * x + 1), XW), col("S", x), op_.subtract)
            scan(V("BC", BW - 3 * AW + 2, BW, 64, s=3), V("X2", p0=64), V("X2", p1=64), V("bs", t, t + 1, 64), op_.add)
            if more:
                at(1)
                mm("b2", *rep(t + 1), *wnd)
                at(4)
                sact(V("AQ"), V("b2", 128 - K, 128), act.Square)
                at(11.5)
                tt(came(t + 1, t - 1), V("A"), V("AQ"), op_.add)
            if t + 2 < R:
                w = max(128, K * t)
                at(7)
                mm("b3", *rep(t + 2), *pair("p%d" % t, n - w, n))
                if t == 1:
                    sact(run("Q", QW * 3 + n - w, w), V("b3", 0, w), act.Square)
                    squares(3, n - w)
                else:
                    sact(came(t + 2, 0, t), V("b3", w - K * t, w), act.Square)
                    squares(t + 2)
                at(14)
                add_to(use(t + 2, n), use(t + 1, n))
            if t == 2:
                at(16)
                qrep(t + 3, 23)
            at(8)
            results(wnd, 128 - K, 128, lambda o: run("YA", K * o, K))
            if t == 1:
                at(24)
                results(own, 0, P, lambda o: block(0, o))
            for o in range(O):
                if t > 1:
                    at(1)
                    store(t - 2, o, "s", [arrival])
                if not more:
                    at(6)
                    sact(block(t - 1, o), block(t - 2, o), act.Copy)
                at((53 if t == 1 else 47) if more else (18, 21)[o])
                scatter(block(t - 1, o), V("LP%d" % (t - 1), 0, 3), run("YA", K * o, K))
        if more:
            if t == 0:
                at(24)
                tt(V("X", K, s=2 * XW), V("pl"), V("ok"), op_.add)
            else:
                at(6.5)
                sact(V("B"), use(t + 1, n - K), act.Copy, V("SO") if t > 1 else None)
                at(18)
                scatter(V("B"), V("LP%d" % (t - 1), 0, 3), came(t + 1, t - 1))
                if t + 2 < R:
                    at(43)
                    ts(V("SO"), V("SF"), 1.0 / UNIT, None, op_.mult)
                at(6)
                sact(run("OG", 192, 64), V("SR"), act.Copy, V("GS"))
                at(15)
                turn(run("TC", 64, 64), run("OG", 192, 64))
                at(24)
                tt(V("X", K, s=2 * XW), V("TC", 64, s=32), V("ok"), op_.add)
            at(22)
            row = V("B") if t else use(1)
            z = [run(row[0], row[3] + 128 * x, 128) for x in range(2)]
            sact(run("OG", 128, 64), row, act.Copy, V("GL", 8, 12))
            sact(half("OG", 0), row, act.Copy, V("GL", 0, 8))
            at(25)
            turn(run("TC", 0, 64), run("OG", 128, 64))
            at(29)
            ts(half("OG", 0), half("OG", 0), TINY, None, op_.max)
            at(28)
            ts(V("zb", 0, 2), V("TC", 0, 64, s=32), TINY, -1.0 / STEP, op_.is_le, op_.mult)
            at(36)
            tt(V("zb", 2, 4), V("TC", 0, 64, s=32), V("zb", 0, 2), op_.subtract)
            for x in range(2):
                at(37)
                affine(half("TH", x), half("F", 1), col("zb", 2 + x), col("zb", x))
                at((32, 37)[x])
                ts(half("CS", 1 + x), z[1 - x], col("TC", 32 * x), None, (op_.is_lt, op_.is_le)[x])
                at((44, 46)[x])
                tt(half("CS", 3 * x), z[x], half("TH", x), op_.is_le)
                at(*((50,), (5, 1))[x])
                asum(col("S", x), run("J", P * x, P), run("CS", P * x, P))
        n2 = n if more else 128 - K
        at(2)
        for x in "cs":
            a, b = V("p%d%s" % (t, x), 0, n2), V("p%d%s" % (t + 1, x), 0, n2)
            dma("s", u8(b) if x == "c" else ap(b), u8(a) if x == "c" else ap(a), [b], [a])
        at(17)
        turn(V("RC"), V("BC", BW - 96))
        for m in range(3):
            at(20)
            ts(run("E", EW * m, 96), V("RC"), col("lo", m), col("hi", m), op_.max, op_.min)
            at(23)
            scan(V("JE", EW * m, EW * m + EW, 64), V("E", EW * m, EW * m + EW, 64), V("E", EW * m, EW * m + EW, p1=64), 0.0, op_.add)
        lst = V("L%d" % t, 0, 3)
        if LIST:
            at(27)
            for m in range(3):
                c = EW * m + EW - 1
                for p in (0, 32, 64, 96):
                    ts(V("L%d" % t, m, m + 1, p, p + 32), V("JE", c, c + 1, 96), V("JE", c, c + 1, 64, 96), 1.0 / UNIT, op_.add, op_.mult)
        else:
            at(27)
            for p in (64, 96):
                tt(V("T1", 0, 3, p, p + 32), V("JE", EW - 1, p0=96, s=EW), V("JE", EW - 1, p0=64, p1=96, s=EW), op_.add)
            at(30)
            for p in (0, 64):
                ts(V("L%d" % t, 0, 3, p, p + 64), V("T1", 0, 3, 64), 1.0 / UNIT, None, op_.mult)
        at(34)
        pick(*pair("o%d" % t, 0, K), *pair("p%d" % t, 0, n), lst)
        dst = T.cores[rank ^ PART[t]]
        rid, pid, _e = topo.addr(dst)
        engs = topo.engines(core, dst)[:NE]
        lanes.append(2 * len(engs))
        n1 = W[t + 1] if more else 128
        parts = [RemoteDMATransfer(dst_ids=[DstId(rid=rid, pnc=pid)], dma_engine_mask=sum(1 << e for e in es), remote_sem=T.sem["arr%d" % t], src=src, dst=out)
                 for es, src, out in ((engs, u8(V("o%dc" % t)), u8(V("p%dc" % (t + 1), n1 - K, n1))),
                                      (engs, ap(V("o%ds" % t)), ap(V("p%ds" % (t + 1), n1 - K, n1 + PAD))))]
        for x, part in zip("cs", parts):
            call("p", [], [V("o%d%s" % (t, x))], lambda part=part: g.remote_dma_fused([part], local_sem=T.sem["sent"]), kind="send")
        arrival = call("net", [V("p%dc" % (t + 1), n1 - K, n1), V("p%ds" % (t + 1), n1 - K, n1 + PAD)], [], ("arr%d" % t, lanes[t]), kind="net")
        new, lp, lu = run("PT", n, K), V("LP%d" % t, 0, 3), V("LP%d" % t, 4, 7)
        at(35)
        gather(new, V("PT", 0, n), lst)
        at(38)
        scan(run("D1", 0, K), V("DM"), new, 0.0, op_.max)
        at(42)
        ts(lp, V("D1", 15, K, s=16), col("pg", 0), None, op_.add)
        if t == 0:
            at(36)
            add_to(use(2), use(1))
        if t + 2 < R:
            at(35)
            sact(run("PU", n, K), V("PU", 0, n), act.Copy, lst)
            at(39)
            scan(run("D1", K, K), V("DM"), run("PU", n, K), 0.0, op_.max)
            at(43)
            ts(lu, V("D1", K + 15, s=16), col("pg", 0), None, op_.add)
            at(45)
            scatter(V("SR"), lu, run("SV", n - P, K))
            if t + 3 < R:
                dma("s", ap(V("SF")), ap(V("SR", p1=8)), [V("SF")], [V("SR")])
        if more:
            at(36)
            sact(run("ZL", 0, K), use(t + 1, n), act.Copy, lst)
            at(40)
            ts(run("ZL", K, K), run("ZL", 0, K), TINY, None, op_.max)
            for x in range(2):
                sact(run("SG", K * x, K), new, act.Sign, bias=col("pm", x))
            at(39)
            sact(V("p2"), run("D1", 0, K), act.Identity, V("PL", 0, 1), bias=col("pg", 0))
            at(38.5)
            for x in range(2):
                ts(run("G", 128 + K + K * x, K), new, col("pn", x), PRED, op_.is_lt, op_.max)
            at(44.5)
            ts(half("G", 0), V("SH"), p2, PRED, op_.is_ge, op_.max)
            ts(run("G", 128, K), new, p2, PRED, op_.is_ge, op_.max)
            at(40.5)
            for x in range(2):
                affine(run("CM", K * x, K), run("G", 128 + K + K * x, K), col("zb", 2 + x), col("zb", x))
            at(51)
            for x in range(2):
                asum(col("X", XW * (2 * x + 1) + K), run("J", 2 * P + K * x, K), run("SG", K * x, K), act.Square, scale=OUT)
            at(49)
            for x in range(2):
                tt(run("X", XW * (2 * x + 1), K), run("ZL", 0, K), run("CM", K * x, K), op_.is_le)
            at(46.5)
            tt(V("RZ"), half("OG", 0), half("G", 0), op_.mult)
            tt(V("ZL", 2 * K, p1=64), V("ZL", K, 2 * K, p1=64), V("G", 128, 128 + K, p1=64), op_.mult)

    for o in range(O):
        at(22)
        store(R - 2, o, "s")
        at(40)
        sact(block(R - 1, o), block(R - 2, o), act.Copy)
    at(60)
    results(pair("p6", 0, 128), 128 - K, 128, lambda o: run("YA", K * o, K))
    for o in range(O):
        scatter(block(R - 1, o), V("LP%d" % (R - 1), 0, 3), run("YA", K * o, K))
        store(R - 1, o, "sa"[o])

    count = {"v": 0, "a": 0, "t": 0, "p": 0, "d": 0}
    seen, mark, behind = {q: {} for q in queues}, {}, {}

    def wait(q, sem, val):
        if seen[q].get(sem, 0) < val:
            queues[q].wait_ge(T.sem[sem], val)
            seen[q][sem] = val
            for s2, v2 in behind.get((sem, val), {}).items():
                seen[q][s2] = max(seen[q].get(s2, 0), v2)

    for i in sorted(range(len(calls)), key=lambda i: (calls[i][0], i)):
        _step, q, fn, after, kind = calls[i]
        if kind == "net":
            mark[i] = fn
            continue
        need = {}
        for j in after:
            need[mark[j][0]] = max(need.get(mark[j][0], 0), mark[j][1])
        for sem in sorted(need, key=lambda s: -len(behind.get((s, need[s]), ()))):
            wait(q, sem, need[sem])
        if kind == "send":
            fn()
            continue
        key = "d" if kind == "dma" else q
        count[key] += 1
        mark[i] = ("d%d" % (count[key] - 1), 16) if key == "d" else ("s" + key, count[key])
        behind[mark[i]] = dict(seen[q])
        fn().then_inc(T.sem[mark[i][0]], 16 if key == "d" else 1)
    behind.clear()
    for i in range(count["d"] - O):
        wait("p", "d%d" % i, 16)
    for t in range(R):
        wait("p", "arr%d" % t, lanes[t])
    wait("p", "sent", sum(lanes))
    for q in "ptav":
        wait("p", "s" + q, count[q])
    for i in range(count["d"] - O, count["d"]):
        wait("p", "d%d" % i, 16)
